import numpy as np, ml_dtypes
CORES = [48,51,52,55]
N = 4
BF = ml_dtypes.bfloat16
def gentries(a):
    return np.ascontiguousarray(a.reshape(8, 16, -1).transpose(0, 2, 1)).reshape(8, -1)
def gtable(e):
    e = np.asarray(e); return np.ascontiguousarray(e.reshape(8, -1, 16).transpose(0, 2, 1)).reshape(128, -1).astype(np.int32)
S, M, CAP, RO = 2048, 1024, 32, 3
W = N * S
def look(x, k, p, wt):
    n, m = p.shape[0], p.shape[3]; gi = np.arange(8)[None, :, None]
    q = np.stack([k[gi, 3 - t, p[:, :, t]] for t in range(4)], axis=2)
    xt = np.ascontiguousarray(x.transpose(0, 2, 1))
    c = [xt[gi, q[:, :, t]].reshape(n, 8, m, 4, 4) for t in range(4)]
    board = np.concatenate([np.concatenate([c[0], c[1]], axis=4), np.concatenate([c[2], c[3]], axis=4)], axis=3)
    hot = (board == 15).astype(np.int64); near = np.zeros((n, 8, m, 4, 4), np.int64)
    for i in range(3):
        for j in range(3):
            if (i, j) != (1, 1): near = near + hot[..., 1 + i:5 + i, 1 + j:5 + j]
    mid = board[..., 2:6, 2:6]
    y = np.where(mid == 0, np.where(near == 2, 15, 0), np.maximum(mid - 1, 0)).reshape(n, 8, m, 16)
    h = np.add.reduce(y * wt[None, :, None, :], axis=3) & (W - 1)
    r0 = xt[gi, h]; r1 = xt[gi, h ^ 1]
    return q, y, h, np.all(r0 == y, axis=3), np.all(r1 == y, axis=3), r0[..., 0] < 0, r1[..., 0] < 0
def content(rng, n):
    u = rng.random((n, 16)); lo = 0.6 * rng.random((n, 1)); hi = 1 - 0.4 * rng.random((n, 1))
    return np.where(u < lo, 0, np.where(u > hi, 15, rng.integers(0, 16, (n, 16))))
def world(rng, share, few, ends=0):
    x = np.full((8, 16, W), -1, np.int64); k = np.zeros((8, 4, W), np.int64); pools = []
    for g in range(8):
        o = rng.permutation(W)
        if ends == 1: o = np.concatenate([np.array([0, W - 1]), o[(o > 0) & (o < W - 1)]])
        if ends == 2: o = o[(o > 1) & (o < W - 16)]
        n = min(int(W * float(share[g])), len(o)); a = n // 2
        c = content(rng, n); pal = content(rng, int(few[g])); c[:a] = pal[rng.integers(0, len(pal), a)]
        x[g][:, o[:n]] = c.T
        k[g][:, o[:a]] = rng.choice(o[:a], (4, a)); k[g][:, o[a:n]] = rng.choice(o[a:n], (4, n - a))
        pools.append((o[:a], o[a:n]))
    return x, k, pools
def start(rng, pools, share, m=M, pw=1.0):
    p = np.zeros((N, 8, 4, m), np.int64)
    for g in range(8):
        a, b = pools[g]
        pa = a[(len(a) * rng.random((N, 4, m)) ** pw).astype(np.int64)]; pb = b[(len(b) * rng.random((N, 4, m)) ** pw).astype(np.int64)]
        p[:, g] = np.where(rng.random((N, 1, m)) < share[:, g, None, None], pa, pb)
    return p
def plant(rng, x, k, p, wt, pools, share, flip=0.3, wrong=0.1, odd=False):
    q, y, h = look(x, k, p, wt)[:3]
    for g in range(8):
        yy = y[:, g].reshape(-1, 16); hh = h[:, g].reshape(-1); hh = hh ^ (rng.random(len(hh)) < flip).astype(np.int64)
        i = rng.permutation(len(hh))[:int(share * len(hh))]; i = i[x[g, 0, hh[i]] < 0]
        u, j = np.unique(hh[i], return_index=True); v = yy[i[j]].copy(); off = v.copy()
        rows = np.arange(len(u)); col = rng.integers(0, 16, len(u)); err = rng.random(len(u)) < wrong
        off[rows, col] = (v[rows, col] + 1) & 15
        if odd:
            sort = rng.integers(0, 4, len(u)); e = np.flatnonzero(sort == 1); off[e, col[e]] = (v[e, col[e]] + 8) & 15
            off[sort == 2] = 0
            a, b = v[:, :15], v[:, 1:]; up = (a == 15) & (b < 15)
            can = (up | ((a == 0) & (b > 0))) & (np.arange(15) % 4 < 3)
            c = np.argmax(can * (1 - rng.random(can.shape)), axis=1)
            e = np.flatnonzero((sort == 3) & np.any(can, axis=1)); c = c[e]
            off[e] = v[e]; off[e, c] = 15 - v[e, c]; off[e, c + 1] = v[e, c + 1] + np.where(up[e, c], 1, -1)
        v = np.where(err[:, None], off, v)
        kk = rng.choice(np.concatenate(pools[g]), (4, len(u)))
        if odd: kk[:, rng.random(len(u)) < 0.25] = 0
        x[g][:, u] = v.T; k[g][:, u] = kk
def pack(x, k, p, wt):
    return {"cells": np.ascontiguousarray(x.reshape(8, 16, N, S).transpose(2, 0, 1, 3)).reshape(N, 128, S).astype(np.float32).astype(BF),
            "kids": np.ascontiguousarray(k.reshape(8, 4, N, S).transpose(2, 0, 1, 3)).reshape(N, 32, S).astype(np.int32),
            "nodes": np.stack([gtable(a.reshape(8, 4 * M)) for a in p]),
            "wt": np.ascontiguousarray(np.tile(wt.reshape(1, 128, 1), (N, 1, 1))).astype(np.int32)}
def setup_inputs(rng):
    wt = rng.integers(0, W, (8, 16)); few = rng.permutation(np.array([2, 2, 3, 3, 4, 5, 6, 6]))
    x, k, pools = world(rng, 0.35 + 0.2 * rng.random(8), few)
    p = start(rng, pools, rng.choice(np.array([0.3, 0.6, 0.9]), (N, 8)))
    plant(rng, x, k, p, wt, pools, 0.3)
    return pack(x, k, p, wt)
def setup_inputs_room(rng):
    wt = rng.integers(0, W, (8, 16)); x, k, pools = world(rng, 0.35 + 0.15 * rng.random(8), rng.integers(3, 7, 8))
    cand = start(rng, pools, np.full((N, 8), 0.1), 2 * M)
    plant(rng, x, k, cand, wt, pools, 0.15)
    q, y, h, hit0, hit1, free0, free1 = look(x, k, cand, wt)
    own = np.where(hit0 | hit1 | ~(free0 | free1), -1, h // S); p = np.zeros((N, 8, 4, M), np.int64)
    want = np.where(free0, h, h ^ 1); taken = np.zeros(W, bool)
    for r in range(N):
        for g in range(8):
            sel = []
            for o in range(N):
                n = int(rng.choice(np.array([0, 1, CAP - 1, CAP, CAP + 1, 2 * CAP])))
                if r == 0 and o == 1: n = (CAP, CAP + 1, 2 * CAP, CAP - 1, 1, 0, CAP, CAP + 1)[g]
                f = rng.permutation(np.flatnonzero(own[r, g] == o))
                if g == 6 and o == 1:
                    n = CAP; f = f[np.unique(want[r, g, f], return_index=True)[1]]
                    f = rng.permutation(f[~taken[want[r, g, f]]]); taken[want[r, g, f[:n]]] = True
                sel.append(f[:n])
            sel = np.concatenate(sel); rest = np.flatnonzero(own[r, g] < 0)
            sel = rng.permutation(np.concatenate([sel, rng.choice(rest, M - len(sel))]))
            if r == 1 and g == 2:
                last = rng.permutation(np.flatnonzero(own[r, g] == 2))[:CAP]
                sel = np.concatenate([rng.choice(np.flatnonzero((own[r, g] >= 0) & (own[r, g] != 2)), M - len(last)), last])
            p[r, g] = cand[r, g][:, sel]
    return pack(x, k, p, wt)
def setup_inputs_clash(rng):
    wt = (2 * rng.integers(0, W // 2, (8, 1)) + 1) * rng.integers(0, 3, (8, 16)) & (W - 1)
    z = rng.permutation(8); wt[z[0]] = 0; wt[z[1]] = 0; wt[z[1], rng.integers(0, 16)] = W - 1
    x, k, pools = world(rng, 0.25 + 0.2 * rng.random(8), rng.integers(2, 9, 8), 2)
    p = start(rng, pools, rng.choice(np.array([0.2, 0.5, 0.8]), (N, 8)))
    return pack(x, k, p, wt)
def setup_inputs_near(rng):
    wt = rng.integers(0, W, (8, 16)); wt[rng.integers(0, 8)] = rng.integers(W - W // 8, W, 16)
    x, k, pools = world(rng, 0.15 + 0.2 * rng.random(8), rng.integers(2, 9, 8), 1)
    p = start(rng, pools, rng.choice(np.array([0.2, 0.5, 0.8]), (N, 8)))
    plant(rng, x, k, p, wt, pools, 0.5, 0.0, 0.5, True); plant(rng, x, k, p, wt, pools, 0.7, 1.0, 0.3, True)
    return pack(x, k, p, wt)
def setup_inputs_alike(rng):
    wt = rng.integers(0, W, (8, 16)); x, k, pools = world(rng, np.array([0.4, 0.98, 0.3, 0.05, 0.5, 0.4, 1.0, 0.6]), np.array([1, 3, 2, 2, 1, 4, 2, 12]), 1)
    a = pools[2][0]; k[2][:, a] = rng.choice(np.array([0, W - 1]), (4, len(a)))
    share = rng.random((N, 8)); share[:, [0, 2]] = 1.0
    p = start(rng, pools, share); p[:, 2] = rng.choice(np.array([0, W - 1]), (N, 4, M))
    for g in (3, 5, 7): p[:, g] = p[:, g][:, :, rng.integers(0, 8, M)]
    return pack(x, k, p, wt)
def setup_inputs_spread(rng):
    wt = np.minimum(np.exp2(rng.random((8, 16)) * np.log2(W)).astype(np.int64), W - 1) * (rng.random((8, 16)) > 0.0625)
    x, k, pools = world(rng, rng.permutation(np.linspace(0.08, 0.92, 8)), rng.integers(1, 41, 8))
    p = start(rng, pools, rng.random((N, 8)), M, 4.0)
    plant(rng, x, k, p, wt, pools, 0.2)
    return pack(x, k, p, wt)
def check_inputs(d):
    bad = []
    c = np.asarray(d["cells"]).astype(np.float32).reshape(N, 8, 16, S); e = c == -1
    if not np.all(e | ((c >= 0) & (c <= 15) & (c == np.floor(c)))): bad.append("numbers of cells")
    if np.any(np.any(e, axis=2) != np.all(e, axis=2)): bad.append("places of cells empty in part")
    ok = True
    for name in ("kids", "nodes", "wt"):
        if np.min(d[name]) < 0 or np.max(d[name]) > W - 1: bad.append("range of " + name); ok = False
    if np.any(d["wt"] != d["wt"][:1]): bad.append("wt alike on all ranks")
    full = ~np.any(e, axis=2).transpose(1, 0, 2).reshape(8, W)
    kd = np.asarray(d["kids"]).astype(np.int64).reshape(N, 8, 4, S).transpose(1, 2, 0, 3).reshape(8, 4, W)
    if np.any((kd != 0) & ~full[:, None, :]): bad.append("children of empty places")
    if ok:
        to = np.take_along_axis(full, kd.reshape(8, -1), 1).reshape(8, 4, W)
        if np.any(full[:, None, :] & ~to): bad.append("children name full places")
        if not all(np.all(np.take_along_axis(full, gentries(a).astype(np.int64), 1)) for a in d["nodes"]): bad.append("nodes name full places")
    return bad
def reference(cells, kids, nodes, wt):
    x = np.concatenate([a.astype(np.float32).astype(np.int64).reshape(8, 16, S) for a in cells], axis=2)
    k = np.concatenate([a.astype(np.int64).reshape(8, 4, S) for a in kids], axis=2)
    p = np.stack([gentries(a).astype(np.int64).reshape(8, 4, M) for a in nodes])
    w = wt[0].astype(np.int64).reshape(8, 16); gi = np.arange(8)[None, :, None]
    for rnd in range(RO):
        q, y, h, hit0, hit1, free0, free1 = look(x, k, p, w)
        at = np.where(hit0, h, np.where(hit1, h ^ 1, -1))
        got = np.stack([k[gi, t, np.maximum(at, 0)] for t in range(4)], axis=2)
        p = np.where(at[:, :, None] >= 0, got, q)
        want = np.where(at >= 0, -1, np.where(free0, h, np.where(free1, h ^ 1, -1)))
        keep = np.zeros(want.shape, bool)
        for o in range(N):
            mine = (want >= 0) & (want // S == o)
            keep = keep | (mine & (np.add.accumulate(mine.astype(np.int64), axis=2) <= CAP))
        for g in range(8):
            i = np.flatnonzero(keep[:, g].reshape(-1))
            u, first = np.unique(want[:, g].reshape(-1)[i], return_index=True); win = i[first]
            x[g][:, u] = y[:, g].reshape(-1, 16)[win].T
            k[g][:, u] = q[:, g].transpose(1, 0, 2).reshape(4, -1)[:, win]
    return {"ycells": np.stack([x[:, :, r * S:(r + 1) * S].reshape(128, S) for r in range(N)]).astype(np.float32).astype(BF),
            "ykids": np.stack([k[:, :, r * S:(r + 1) * S].reshape(32, S) for r in range(N)]).astype(np.float32),
            "ynodes": np.stack([gtable(a.reshape(8, 4 * M)) for a in p]).astype(np.float32)}

@@ -1,0 +1,597 @@
+from concourse.bass import DstId, RemoteDMATransfer
+from concourse.mybir import AluOpType as A, ActivationFunctionType as F
+
+f32, b16, i32, u16 = "float32", "bfloat16", "int32", "uint16"
+SCRATCH = {}
+
+
+def _decl(dt, **kw):
+    for n, sh in kw.items():
+        SCRATCH[n] = ("sbuf", [128] + list(sh), dt)
+
+
+_decl(b16, XS=[4, 512], X=[2048], H=[4, 512], C0=[4, 128], SH=[8, 4, 4], SX=[8, 4, 4], WH=[4, 128], WX=[4, 128],
+      G=[8192], TT=[8192], TO0=[4096], TO1=[4096], L=[4224], LS=[2, 1024], CW=[2080], KH=[512], KLO=[512], ZR=[512],
+      WZ=[7, 2, 4, 4], WD=[7, 2, 4, 4], WK=[7, 2, 16], WT=[18], WC=[40], MK=[8], DM=[8, 16], WLW=[24], WLK=[32], TE=[256],
+      BW=[5, 64], BT=[5, 64], WP1=[8, 16], WP2=[8, 8, 16], WLT=[4, 2, 16], WLC=[4, 4, 2, 16], IW=[4, 224], KWM=[4, 7, 2, 16],
+      C=[1024], R=[2048], MO=[256], CK=[512], TC=[512], CC=[128], LR=[512], VC=[128], SO=[3, 4, 64], LB=[3, 4, 64])
+_decl(f32, RT=[8, 4, 4], CT=[8, 4, 4], FF=[16], J16=[20], GB=[16], KB=[4, 4, 2, 16], KT=[4, 4, 32], NF=[256],
+      KF=[512], KW=[2080], IDF=[128], NEG=[128], PM=[128], RW=[4, 128], BO=[128], WF=[4], JT=[128], NT=[64], DIAG=[256], RM=[256],
+      RB=[256], TRI=[256], T3=[36], NM=[9, 64], HP=[128], BX=[128], OW=[64], H1=[128], H2=[128], SEL=[128], MS=[64],
+      PR=[4, 128], QM=[2, 128], EM=[128], AN=[64], PZ=[192], UT=[320], CNT=[8], VN=[256], RL=[4, 3, 8],
+      MF=[128], DG=[256], DS=[256], AB=[256], M3=[72], VK=[128], YN=[256], YL=[256], OO=[3, 4, 8], LO=[3, 4, 4, 8])
+_decl(i32, PI=[1], FI=[16], KA=[4, 2, 64], NS=[4, 64], NI=[256], KN=[512], WI=[4], HI=[64], HJ=[4, 64], I8=[3, 8])
+_decl(u16, KL=[512], TL=[512], PL=[256], LL=[128], CL=[16], NL=[32], LOF=[32], OL=[8])
+SCRATCH["S"] = ("dram", [4, 128, 1024], b16)
+for _b in range(8):
+    SCRATCH["P%d" % _b] = ("psum", [128, 512], f32)
+SEMAPHORES = (["pe", "dve", "act", "pool", "ax0", "ax1", "ax2", "ax3", "ak", "an", "al", "ao0", "ao1", "ao2", "ay"]
+              + ["d%d" % i for i in range(40)])
+
+
+def rank_program(g, core, T, topo):
+    me = T.rank_of(core)
+    if me is None:
+        return
+    Q = {"pe": g.tensor, "dve": g.vector, "act": g.scalar, "pool": g, "sp": g.sync}
+    V, P = g.vector, [T["P%d" % b] for b in range(8)]
+    cnt = {"pe": 0, "dve": 0, "act": 0, "pool": 0}
+    seen = {q: {} for q in Q}
+    wrote, read, total, nsem = {}, {}, {}, [0]
+    peers = [me ^ 1, me ^ 2, me ^ 3]
+
+    def need(q, r, w):
+        m = {}
+        for k in list(r) + list(w):
+            for s, v in wrote.get(k, []) + (read.get(k, []) if k in w else []):
+                m[s] = max(m.get(s, 0), v)
+        for s, v in m.items():
+            if seen[q].get(s, 0) < v and not (q == "pe" and s == "pe"):
+                Q[q].wait_ge(T.sem[s], v)
+                seen[q][s] = v
+
+    def done(s, v, r, w):
+        total[s] = v
+        for k in r:
+            read.setdefault(k, []).append((s, v))
+        for k in w:
+            wrote[k] = [(s, v)]
+            read[k] = []
+
+    def op(q, fns, r, w):
+        r, w = r.split(), w.split()
+        need(q, r, w)
+        for f in (fns if isinstance(fns, list) else [fns]):
+            f().then_inc(T.sem[q], 1)
+            cnt[q] += 1
+        done(q, cnt[q], r, w)
+
+    def newsem():
+        nsem[0] += 1
+        return "d%d" % (nsem[0] - 1)
+
+    def dma(q, pairs, r, w):
+        r, w = r.split(), w.split()
+        need(q, r, w)
+        s = newsem()
+        for o, i in pairs:
+            Q[q].dma_start(o, i).then_inc(T.sem[s], 16)
+        done(s, 16 * len(pairs), r, w)
+
+    def emask(d, lo, n):
+        m = 0
+        for e in topo.engines(core, T.cores[d])[lo:lo + n]:
+            m |= 1 << e
+        return m
+
+    def send(items, n, r):
+        r = r.split()
+        need("pool", r, [])
+        s = newsem()
+        if len(items) == 1:
+            d, o, i, rs = items[0]
+            rid, pid = topo.addr(T.cores[d])[:2]
+            g.remote_dma(o, i, T.sem[rs], T.sem[s], pid, rid, emask(d, 0, n))
+        else:
+            tr = []
+            for j, (d, o, i, rs) in enumerate(items):
+                rid, pid = topo.addr(T.cores[d])[:2]
+                tr.append(RemoteDMATransfer(dst_ids=[DstId(rid=rid, pnc=pid)], dma_engine_mask=emask(d, j * n, n),
+                                            remote_sem=T.sem[rs], srcs=[i], dsts=[o]))
+            g.remote_dma_fused(tr, local_sem=T.sem[s])
+        done(s, n * len(items), r, [])
+
+    def arrives(s, v, w):
+        done(s, v, [], w.split())
+
+    def mm(ms, r, w):
+        op("pe", [(lambda m=m: g.tensor.matmul(*m)) for m in ms], r, w)
+
+    def ts(o, i, s1, o0, s2=None, o1=None):
+        if o1 is None:
+            return lambda: V.tensor_scalar(o, i, s1, None, o0)
+        return lambda: V.tensor_scalar(o, i, s1, s2, o0, o1)
+
+    def tt(o, a, b, p):
+        return lambda: V.tensor_tensor(o, a, b, p)
+
+    def cp(o, i):
+        return lambda: V.tensor_copy(o, i)
+
+    def ms(o, c):
+        return lambda: V.memset(o, c)
+
+    def scan(o, a, b, p0, p1):
+        return lambda: V.tensor_tensor_scan(o, a, b, 0.0, p0, p1)
+
+    def act(o, i, f=F.Identity, **k):
+        return lambda: g.scalar.activation(o, i, f, **k)
+
+    def io(o, pat, base, cm=0):
+        return lambda: g.iota(o, pat, base, cm, allow_small_or_imprecise_dtypes=True)
+
+    def put(key, o, pat, base, val, cm=1):
+        op("pool", lambda: g.affine_select(o, o, pat, A.not_equal, float(val), base, cm), "", key)
+
+    def keep(key, o, pat, base, cm):
+        op("pool", lambda: g.affine_select(o, o, pat, A.is_ge, 0.0, base, cm), "", key)
+
+    SHR, AND = A.arith_shift_right, A.bitwise_and
+    FF, IDB = T.FF, T.TE[:, 128:256]
+
+    def xload(dst, d):
+        return [(dst(h), T.cells[32 * d:32 * d + 32, 1024 * h:1024 * h + 1024]) for h in range(2)]
+    for d in peers:
+        dma("sp", xload(lambda h: T.XS[64 * h:64 * h + 64, d, :], d), "", "XS%d" % d)
+    dma("act", xload(lambda h: T.X[64 * h:64 * h + 64, 512 * me:512 * me + 512], me), "", "X%d" % me)
+    dma("sp", [(T.KA[:, e // 2, e % 2, :], T.kids[4 * e:4 * e + 4, :]) for e in range(8)], "", "KA")
+
+    op("pool", lambda: g.iota(T.PI[:], [[0, 1]], 0, 1), "", "PI")
+    op("dve", [ms(T.BO[:], 1.0), ms(T.SH[:], 0.0), ms(T.SX[:], 0.0)], "", "SH SX BO")
+    op("dve", scan(T.MF[:], T.BO[:], T.BO[:], A.mult, A.add), "BO", "MF")
+    fields = [(3, 3), (1, 16), (1, 3), (0, 65), (0, 15), (0, 12), (0, 9), (5, 1), (6, 1)]
+    op("dve", [ts(T.FI[:, j:j + 1], T.PI[:], s, SHR, m, AND) for j, (s, m) in enumerate(fields)], "PI", "FI")
+    op("dve", [ts(T.C0[:, a, :], T.MF[:], -1.0, A.add) for a in range(4)], "MF", "C0")
+    op("dve", cp(FF[:, 0:9], T.FI[:, 0:9]), "FI", "FF")
+    op("dve", [ms(T.C0[p:p + 32, a, :], float(a)) for p in (32, 96) for a in range(4)], "", "C0")
+
+    def hconst(slot):
+        op("act", [act(T.H[64:128, slot, :], T.C0[64:128]), act(T.H[0:64, 2 + slot, :], T.C0[0:64])], "C0", "HC%d" % slot)
+    op("pool", [io(T.RT[:, 2 * t:2 * t + 2], [[16, 2], [1, 4], [0, 4]], 3 * (t >> 1) - 1) for t in range(4)]
+       + [io(T.CT[:, 4 * h:4 * h + 4], [[3, 2], [0, 8], [1, 4]], -1) for h in range(2)]
+       + [io(T.J16[:, 16:20], [[64, 2], [1, 2]], 0), io(T.J16[:, 0:16], [[1, 16]], 0)], "", "RT CT J16")
+    op("pool", [io(T.RT[:, 2 * t:2 * t + 2, 3, :], [[16, 2], [1, 2], [0, 2]], 2 * (t >> 1)) for t in range(4)]
+       + [io(T.CT[:, 4 * h:4 * h + 4, 3, :], [[2, 2], [0, 4], [1, 2]], 0) for h in range(2)], "", "RT CT")
+    for d in peers:
+        send([(d, T.X[:, 512 * me:512 * me + 512], T.XS[:, d, :], "ax%d" % me)], 16, "XS%d" % d)
+        arrives("ax%d" % d, 16, "X%d" % d)
+    op("dve", [tt(FF[:, 10:11], FF[:, 0:1], FF[:, 1:2], A.add), ts(FF[:, 11:12], FF[:, 4:5], 3.0, A.is_equal, 4.0, A.mult),
+               ts(FF[:, 12:13], FF[:, 5:6], 12.0, A.is_equal, -1.0, A.mult), ts(FF[:, 13:14], FF[:, 6:7], 8.0, A.is_equal, -129.0, A.mult),
+               ts(FF[:, 14:15], FF[:, 7:8], 2048.0, A.mult, FF[:, 4:5], A.add)], "FF", "FG")
+    dma("sp", [(T.KN[:], T.kids[:])], "", "KN XS%d" % peers[1])
+    dma("sp", [(T.CW[:, 0:2048], T.cells[:])], "", "CW")
+    dma("sp", [(T.NS[:, d, :], T.nodes[32 * d:32 * d + 32, :]) for d in peers], "", "NS")
+    dma("sp", [(T.NI[:, 64 * me:64 * me + 64], T.nodes[32 * me:32 * me + 32, :]), (T.WI[0:32, 0:1], T.wt[32 * me:32 * me + 32, :])], "", "NIo WI")
+    hconst(0)
+    op("act", [act(T.RT[:], T.RT[:], F.Abs, bias=FF[:, 10:11], scale=-1.0), act(T.CT[:], T.CT[:], F.Abs, bias=FF[:, 2:3], scale=-1.0)],
+       "FF FG", "RT CT")
+    hconst(1)
+
+    def hot(src, slot):
+        c = slice(512 * src, 512 * src + 512)
+        op("dve", [ts(T.H[0:64, slot, :], T.X[0:64, c], 15.0, A.is_equal), ts(T.H[64:128, 2 + slot, :], T.X[64:128, c], 15.0, A.is_equal)],
+           "X%d" % src, "H%d" % slot)
+
+    def zero(names):
+        op("dve", [ms(T[n][:], 0.0) for n in names.split()], "", names)
+    hot(me, 0)
+    op("dve", [ts(T.GB[:], T.J16[:, 0:16], FF[:, 11:12], A.mult, FF[:, 12:13], A.add), ts(T.J16[:, 16:20], T.J16[:, 16:20], FF[:, 3:4], A.is_equal),
+               tt(T.RT[:], T.RT[:], T.CT[:], A.max)], "FF FG CT", "J16 GB RT")
+    op("dve", [ts(T.SH[:, :, 0:3, 0:3], T.RT[:, :, 0:3, 0:3], 1.0, A.is_equal),
+               ts(T.SX[:, :, 0:3, 0:3], T.RT[:, :, 0:3, 0:3], 0.0, A.is_equal, 16.0, A.mult),
+               ts(T.SX[:, :, 3, :], T.RT[:, :, 3, :], 0.0, A.is_equal)], "RT", "SH SX")
+    op("dve", [ts(T.WH[:, j, :], T.SH[:], T.J16[:, 16 + j:17 + j], A.mult) for j in range(4)], "SH J16", "WH")
+    op("dve", [ts(T.WX[:, j, :], T.SX[:], T.J16[:, 16 + j:17 + j], A.mult) for j in range(4)], "SX J16", "WX")
+    op("dve", [ms(T.WH[64 * (1 - h) + 32 * b:64 * (1 - h) + 32 * b + 1, 2 * h:2 * h + 2, 7 - 4 * b::16], 1.0) for h in range(2) for b in range(2)],
+       "", "WH")
+
+    def gbuild(i, src, j, q):
+        ch, c, b = 4 * src + j, slice(512 * src, 512 * src + 512), (4 * i + j) % 8
+        mm([(P[b][:], T.WX[:, j, :], T.X[:, c], True, False), (P[b][:], T.WH[:, j, :], T.H[:, (j & 2) + (i & 1), :], False, True)],
+           "WH WX HC%d X%d H%d" % (i & 1, src, i & 1), "P%d" % b)
+        o, bias = T.G[:, 512 * ch:512 * ch + 512], T.GB[:, ch:ch + 1]
+        op(q, act(o, P[b][:], F.Relu, bias=bias) if q == "act" else ts(o, P[b][:], bias, A.add, 0.0, A.max), "GB", "P%d G%d" % (b, ch))
+    for j in range(4):
+        gbuild(0, me, j, "act")
+    zero("WP1 WP2 PM RW WC DM WZ WT IDF NEG WLW WLK")
+    op("dve", [ms(T.MK[:], 1.0), ms(T.TE[:, 0:128], 1.0), ms(IDB, 0.0)], "", "MK TE")
+    op("dve", [cp(T.KB[:, :, :, s, :], T.KA[:, :, s, :]) for s in range(2)], "KA", "KB")
+    hot(peers[0], 1)
+    for j in range(4):
+        gbuild(1, peers[0], j, "act")
+    op("dve", lambda: V.transpose(T.KT[:], T.KB[:]), "KB", "KT")
+    op("dve", [cp(T.KL[:, b::4], T.KT[:, :, b, :]) for b in range(4)], "KT", "KL")
+    hot(peers[1], 0)
+    for j in range(4):
+        gbuild(2, peers[1], j, "act")
+    op("dve", cp(T.TL[:, 128 * me:128 * me + 128], T.KL[:, 128 * me:128 * me + 128]), "KL", "TLo")
+    zero("BW BT ZR PZ RB")
+    hot(peers[2], 1)
+    op("dve", cp(T.KF[:], T.KN[:]), "KN", "KF")
+    op("dve", ts(T.KN[:], T.KN[:], 127, AND), "", "KN")
+    op("dve", ts(T.KH[:], T.KF[:], 1.0 / 128, A.mult, 128.50390625, A.add), "KF", "KH")
+    op("dve", cp(T.KLO[:], T.KN[:]), "KN", "KLO")
+    for j in range(4):
+        gbuild(3, peers[2], j, "dve" if j == 3 else "act")
+    GALL = " ".join("G%d" % c for c in range(16))
+
+    put("WP1", T.WP1[:, :, 0:8], [[-16, 8], [-2, 8]], 0, 1)
+    put("WP1", T.WP1[:, :, 0:8], [[-16, 8], [-2, 8]], -1, 16)
+    op("pool", [(lambda q=q, e=e: g.affine_select(T.WP2[:, 2 * q + e, :, 8 + e::2], T.WP2[:, 2 * q + e, :, 8 + e::2], [[-16, 8], [-4, 4]],
+                                                  A.not_equal, 1.0, -q, 1)) for q in range(4) for e in range(2)], "", "WP2")
+    send([(d, T.TL[:, 128 * me:128 * me + 128], T.KL[:, 128 * d:128 * d + 128], "ak") for d in peers], 4, "KL")
+    arrives("ak", 12, "TL")
+    put("PM", T.PM[:], [[1, 4], [-64, 2], [-4, 16]], -3, 1)
+    for b in range(4):
+        put("RW", T.RW[:, b, :], [[0, 4], [-1, 32]], -32 * b, 1)
+    for e in range(6):
+        n = 3 if e < 4 else 2
+        put("WC", T.WC[:, 0:8 * n], [[-6, n], [-16, 2], [-32, 4]], -e, 16 ** e)
+    keep("MK", T.MK[:], [[-16, 2], [-32, 4]], 0, 1)
+    keep("MK", T.MK[:], [[16, 2], [32, 4]], 15, -1)
+    send([(d, T.NI[:, 64 * me:64 * me + 64], T.NS[:, d, :], "an") for d in peers], 4, "NS")
+    arrives("an", 12, "NI")
+    for t in range(4):
+        tr, tc = 1 - (t >> 1), 1 - (t & 1)
+        put("DM", T.DM[:, 2 * t:2 * t + 2, 12:16], [[-16, 2], [-4, 2], [-1, 2]], -8 * tr - 2 * tc, 1)
+        put("WZ", T.WZ[:, 3, :, tr:tr + 3, tc:tc + 3], [[-16, 2], [-4, 3], [-1, 3]], -32 * t, 1)
+    put("WT", T.WT[:, 0:8], [[-16, 8]], -3, 128)
+    put("WT", T.WT[:, 0:8], [[-16, 8]], -7, 1)
+    put("TE", IDB, [[-1, 128]], 0, 1)
+    put("IDF", T.IDF[:], [[-1, 128]], 0, 1)
+
+    def gather(q, o, win, off, r, w):
+        op(q, act(o, win.indirect(off)) if q == "act" else cp(o, win.indirect(off)), r, w)
+
+    def tbuild(q, a, b):
+        gather(q, T.TT[:, 16 * a:16 * b], T.G[:, :], T.TL[:, a:b], GALL + " TL TLo", "TT%d" % a)
+    tbuild("act", 0, 64)
+    tbuild("dve", 64, 224)
+    for q in range(4):
+        mm([m for pi in range(2) for m in
+            [(P[q][:, 256 * pi:256 * pi + 256], T.WP1[:], T.CW[:, 512 * q + pi:512 * q + 512:2], True, False),
+             (P[q][:, 256 * pi:256 * pi + 256], T.WP2[:, 2 * q], T.KH[:, pi::2], False, False),
+             (P[q][:, 256 * pi:256 * pi + 256], T.WP2[:, 2 * q + 1], T.KLO[:, pi::2], False, True)]], "WP1 WP2 CW KH KLO", "P%d" % q)
+    op("dve", [ts(T.WI[0:32, 1:2], T.WI[0:32, 0:1], 6, SHR), ts(T.WI[0:32, 2:3], T.WI[0:32, 0:1], 63, AND)], "WI", "WJ")
+    op("dve", cp(T.NF[:], T.NI[:]), "NI NIo", "NF")
+    mm([(P[5][:, 0:256], T.PM[:], T.NF[:], True, True)], "PM NF", "P5")
+    op("dve", [ts(T.WF[0:32, 0:1], T.WI[0:32, 1:2], 64.0, A.mult), cp(T.WF[0:32, 1:2], T.WI[0:32, 2:3]), ms(T.RM[:], 1.0)], "WJ", "WF RM")
+    mm([(P[4][:, 0:2], T.RW[0:32, 0, :], T.WF[0:32, 0:2], True, True)], "RW WF", "P4")
+    zero("WD WK WLT WLC")
+    for q in range(4):
+        op("act", act(T.LS[:, :, 256 * q:256 * q + 256], P[q][:], bias=FF[:, 13:14]), "FG", "P%d LS%d" % (q, q))
+    LSA = "LS0 LS1 LS2 LS3"
+    dma("sp", [(T.S[:, 32 * j:32 * j + 32, :], T.LS[:, j >> 1, :]) for j in range(4)], LSA, "S")
+    op("dve", cp(T.WF[:, 2:4], P[4][:, 0:2]), "", "P4 WG")
+    op("dve", cp(T.PL[:], P[5][:, 0:256]), "", "P5 PL")
+    op("dve", [ts(T.WC[:, 24:32], T.MK[:], T.WF[:, 2:3], A.mult), ts(T.WC[:, 32:40], T.MK[:], T.WF[:, 3:4], A.mult)], "WG MK", "WC")
+    mm([(P[4][:, 0:10], T.DM[0:32], T.WC[0:32, 0::4], True, True)], "DM WC", "P4")
+    tbuild("act", 224, 416)
+    tbuild("dve", 416, 512)
+    op("dve", cp(T.WT[:, 8:18], P[4][:, 0:10]), "", "P4 WT")
+    TALL = "TT0 TT64 TT224 TT416"
+    dma("sp", [(T.L[32 * j:32 * j + 32, 1024 * me:1024 * me + 1024], T.LS[32 * me:32 * me + 32, j >> 1, :]) for j in range(4)], LSA + " S", "Lo")
+
+    put("NEG", T.NEG[:], [[-1, 128]], 0, -1)
+    for e in range(3):
+        n = 3 if e < 2 else 2
+        put("WLW", T.WLW[:, 0:8 * n], [[-3, n], [-16, 8]], -e, 256 ** e)
+    put("WLK", T.WLK[:], [[-2, 4], [-16, 8]], -8, 128)
+    put("WLK", T.WLK[:], [[-2, 4], [-16, 8]], -9, 1)
+    keep("TE", T.TE[:, 0:128], [[1, 128]], -1, -1)
+    op("pool", [io(T.NT[:], [[16, 64]], 0), io(T.T3[:, 32:34], [[16, 2]], 0), io(T.DIAG[:], [[0, 16], [1, 16]], 0),
+                io(T.TRI[:], [[-16, 2], [0, 4], [1, 32]], 0), io(T.T3[:, 0:16], [[0, 2], [16, 8]], 4096), io(T.T3[:, 16:24], [[0, 4], [16, 2]], 2048),
+                io(T.T3[:, 24:32], [[992, 4], [-16, 2]], -4096), io(T.JT[:], [[0, 4], [1, 32]], -127),
+                io(T.BW[:, 1::2, :], [[0, 128]], 1), io(T.BT[:, 1::2, :], [[0, 128]], 1)], "", "K2 BW BT")
+    for d in peers:
+        send([(d, T.L[:, 1024 * me:1024 * me + 1024], T.S[d], "al")], 16, "S")
+    arrives("al", 48, "La")
+    dma("sp", [(T.KW[16 * e:16 * e + 4, 0:2048], T.KF[16 * e:16 * e + 16, :]) for e in range(8)], "KF La", "KW")
+    for n in ("BW", "BT"):
+        keep(n, T[n][:, 1::2, :], [[-64, 2], [-16, 4], [0, 16]], 0, 1)
+    keep("BW", T.BW[:, 1::2, :], [[64, 2], [16, 4], [0, 16]], 15, -1)
+    keep("BT", T.BT[:, 1::2, :], [[64, 2], [1, 64]], 0, -1)
+    put("BT", T.BT[:, 1::2, :], [[-64, 2], [-1, 64]], 0, -127)
+    keep("BO", T.BO[:], [[-16, 8], [0, 16]], 0, 1)
+    keep("BO", T.BO[:], [[16, 8], [0, 16]], 15, -1)
+    for t in range(4):
+        tr, tc = 1 - (t >> 1), 1 - (t & 1)
+        put("WD", T.WD[:, 3, :, 2 * tr:2 * tr + 2, 2 * tc:2 * tc + 2], [[-16, 2], [-2, 2], [-1, 2]], -32 * t - 12, 1)
+        for mc in range(2):
+            put("WLT", T.WLT[:, :, :, 4 * tr + tc:4 * tr + tc + 3:2], [[0, 4], [-16, 2], [-2, 2]], -32 * t - 12 - mc, 16 ** mc)
+    for e in range(2):
+        put("WLT", T.WLT[:, :, :, 8 + e::2], [[0, 4], [-16, 2], [32, 4]], -99 - 4 * e, 1)
+        put("WK", T.WK[:, 3, :, e:8:2], [[-16, 2], [32, 4]], -99 - 4 * e, 1)
+    for b in range(4):
+        for e in range(2):
+            put("WLC", T.WLC[:, b, :, :, 0:8], [[0, 4], [-16, 2], [-2, 8]], -32 * b - e, 16 ** e)
+
+    def consts2(part):
+        c4 = FF[:, 4:5]
+        if part == 0:
+            op("dve", [ms(T.TE[0:64, 64:128], 0.0), ms(T.RM[:, 0::16], 0.0), ms(T.RB[:, 0::32], 65536.0),
+                       ts(FF[:, 15:16], FF[:, 8:9], 1024.0, A.mult, FF[:, 14:15], A.add),
+                       ts(T.T3[:, 32:34], T.T3[:, 32:34], c4, A.add, 0.5, A.add), ts(T.T3[:, 0:24], T.T3[:, 0:24], c4, A.add),
+                       ts(T.T3[:, 24:32], T.T3[:, 24:32], c4, A.subtract)], "FF FG", "TE RM RB F7 K2")
+        else:
+            op("dve", [ts(T.DIAG[:], T.DIAG[:], c4, A.is_equal), ts(T.TRI[:], T.TRI[:], c4, A.is_ge, 4096.0, A.mult),
+                       ts(T.NT[:], T.NT[:], FF[:, 15:16], A.add)], "FF F7", "K2")
+
+    def tgather(rd, q, cc):
+        TO = T["TO%d" % (rd % 2)]
+        gather(q, TO[:, 1024 * cc:1024 * cc + 1024], T.TT[:, :], T.PL[:, 64 * cc:64 * cc + 64], TALL + " PL", "TO%d_%d" % (rd % 2, cc))
+
+    def zmm(rd, cc):
+        TO, be, hf = T["TO%d" % (rd % 2)], cc >> 1, cc & 1
+        mm([(P[be][:, 128 * ka + 64 * hf:128 * ka + 64 * hf + 64], T.WZ[:, 3 - u:7 - u], TO[:, 1024 * cc + 4 * u + ka:1024 * cc + 1024:16],
+             u == 0, u == 3) for ka in range(4) for u in range(4)], "WZ TO%d_%d" % (rd % 2, cc), "P%d" % be)
+
+    def tpart(rd, be):
+        TO = T["TO%d" % (rd % 2)]
+        mm([(P[2 + be][:, 0:288], IDB, T.ZR[:, 0:288], True, False)]
+           + [(P[2 + be][:, k:288:16], TO[:, 2048 * be + k:2048 * be + 2048:16], T.WT[:], False, False) for k in range(16)],
+           "TE ZR WT TO%d_%d TO%d_%d" % (rd % 2, 2 * be, rd % 2, 2 * be + 1), "P%d" % (2 + be))
+
+    def cond(be):
+        op("dve", ts(T.C[:, 512 * be:512 * be + 512], P[be][:], 2.0, A.is_equal, 15.0, A.mult), "", "P%d C%d" % (be, be))
+
+    def cmm(be):
+        mm([(P[2 + be][:, 128 + ka:288:4], T.C[:, 512 * be + 128 * ka:512 * be + 128 * ka + 128], T.WC[:], False, ka == 3)
+            for ka in range(4)], "WC C%d" % be, "P%d" % (2 + be))
+
+    def tevac(be):
+        op("act", act(T.NM[:, :, 32 * be:32 * be + 32], P[2 + be][:, 0:288]), "", "P%d NM%d" % (2 + be, be))
+
+    def hash1(fill):
+        op("dve", tt(T.HI[:], T.NM[:, 7, :], T.NM[:, 8, :], A.add), "NM0 NM1", "HI")
+        fill(0)
+        op("dve", ts(T.HJ[:, 0, :], T.HI[:], 1, SHR, 4095, AND), "HI", "HJ0")
+        op("dve", [ts(T.HJ[:, 1, :], T.HI[:], 1, AND), ts(T.HJ[:, 2, :], T.HI[:], 11, SHR, 3, AND)], "HI", "HJ")
+        op("dve", [cp(T.HP[:, 64 * pi:64 * pi + 64], T.HJ[:, 0, :]) for pi in range(2)], "HJ0", "HP")
+        mm([(P[5][:, 256:384], T.HP[:], T.IDF[:], True, True)], "HP IDF", "P5")
+        fill(1)
+        op("dve", cp(T.LL[:], P[5][:, 256:384]), "", "P5 LL")
+
+    def at(rd, t, c):
+        return t[:, :, c::4] if rd == 2 else t[:, :, 32 * (3 - c):32 * (3 - c) + 32]
+
+    def lookup(rd):
+        op("act", [act(at(rd, T.QM, c), T.NM[:, 3 - c, :]) for c in range(4)], "NM0 NM1", "QM")
+        gather("act", T.R[:, 1024:2048], T.L[:, 0:4096], T.LL[:, 64:128], "Lo La L LL", "R1")
+        gather("dve", T.R[:, 0:1024], T.L[:, 0:4096], T.LL[:, 0:64], "Lo La L LL", "R0")
+        mm([(P[1][:], IDB, T.ZR[:], True, False)]
+           + [(P[1][:, 64 * j:64 * j + 64], T.NEG[:], T.NM[:, 3 - (j >> 1), :], False, False) for j in range(8)], "TE ZR NEG NM0 NM1", "P1")
+        mm([(P[5 + be][:, 0:128], T.QM[:, be, :], T.IDF[:], True, False) for be in range(2)], "QM IDF", "P5 P6")
+        mm([(P[0][:, k:384:16], T.R[:, k::16], T.WLW[:], True, True) for k in range(16)], "R0 R1 WLW", "P0")
+        mm([(P[1][:, k::16], T.R[:, k::16], T.WLK[:], False, k == 15) for k in range(16)], "R0 R1 WLK", "P1")
+        op("dve", [ts(T.BX[:, 0:64], T.HJ[:, 1, :], -1.0, A.mult, 2.0, A.add), ts(T.BX[:, 64:128], T.HJ[:, 1, :], 1.0, A.add),
+                   ts(T.OW[:], T.HJ[:, 2, :], 1.0, A.add), ts(T.HJ[:, 3, :], T.HI[:], 2046, AND)], "HJ HI", "BX OW HJ3")
+
+    def choose(rd):
+        p0, e, o = P[0], P[0][:, 256:320], T.H1[:, 0:64]
+        eq = [p0[:, 0:64], p0[:, 64:128], T.H1[:, 0:64], T.H1[:, 64:128], p0[:, 384:448], p0[:, 448:512]]
+        op("dve", [ts(T.EM[:], p0[:, 256:384], 0.0, A.is_lt)]
+           + [tt(eq[j], p0[:, 64 * j:64 * j + 64], T.NM[:, 4 + (j >> 1), :], A.is_equal) for j in range(6)], "NM0 NM1", "P0 EM H1")
+        op("dve", [tt(T.H2[:], p0[:, 0:128], T.H1[:], A.mult), tt(p0[:, 128:256], p0[:, 384:512], T.BX[:], A.mult)], "BX H1", "P0 H2")
+        op("dve", tt(T.EM[:], T.EM[:], T.BX[:], A.mult), "BX", "EM")
+        op("dve", [tt(e, p0[:, 128:192], T.H2[:, 0:64], A.mult), tt(o, p0[:, 192:256], T.H2[:, 64:128], A.mult)], "H2", "P0 H1")
+        op("dve", tt(T.AN[:], T.EM[:, 64:128], T.EM[:, 0:64], A.not_equal), "EM", "AN")
+        op("dve", [tt(T.SEL[:, 0:64], e, o, A.is_gt), tt(T.SEL[:, 64:128], e, o, A.is_lt), tt(T.MS[:], e, o, A.is_equal)], "H1", "P0 SEL MS")
+        op("dve", tt(T.OW[:], T.OW[:], T.AN[:], A.mult), "AN", "OW")
+        op("dve", [tt(at(rd, T.PR, c), P[1][:, 128 * c:128 * c + 128], T.SEL[:], A.mult) for c in range(4)], "SEL", "P1 PR")
+        for be in range(2):
+            mm([(P[5 + be][:, 0:128], T.PR[:, 2 * pi + be, :], T.IDF[:], False, pi == 1) for pi in range(2)], "PR IDF", "P%d" % (5 + be))
+        op("dve", tt(T.OW[:], T.OW[:], T.MS[:], A.mult), "MS", "OW")
+        op("dve", tt(T.AN[:], T.EM[:, 64:128], T.EM[:, 0:64], A.is_gt), "EM", "AN")
+        op("dve", [ts(T.MO[:, 64 * j:64 * j + 64], T.OW[:], float(j + 1), A.is_equal) for j in range(4)], "OW", "MO")
+        mm([(P[7][:, 256 * h:256 * h + 256], T.MO[:, 128 * h:128 * h + 128], T.TE[:], True, True) for h in range(2)], "MO TE", "P7")
+        op("dve", tt(T.PZ[:, 64:128], T.AN[:], T.HJ[:, 3, :], A.add), "AN HJ3", "PZ")
+
+    def newlist(rd):
+        for be in range(2):
+            if rd == 2:
+                op("dve", cp(T.YN[:, 128 * be:128 * be + 128], P[5 + be][:, 0:128]), "", "P%d YN%d" % (5 + be, be))
+            else:
+                op("dve", cp(T.PL[:, 128 * be:128 * be + 128], P[5 + be][:, 0:128]), "", "P%d PL" % (5 + be))
+
+    def claim2():
+        op("act", act(T.CK[:], P[7][:]), "", "P7 CK")
+
+        def term(b, o, hf, W, x, start, stop):
+            k = 1 + 2 * (o & 1) - hf
+            c = 256 * (o >> 1) + 128 * x + 64 * hf
+            return (P[b][:, 64 * o:64 * o + 64], W[:, k:k + 2, :], T.CK[:, c:c + 64], start, stop)
+        mm([term(6, o, hf, T.BW, 0, hf == 0, hf == 1) for o in range(4) for hf in range(2)], "BW CK", "P6")
+        mm([term(4, o, j >> 1, (T.BW, T.BT)[j & 1], j & 1, j == 0, j == 3) for o in range(4) for j in range(4)]
+           + [(P[4][:, 256:320], T.PZ[:, 64 - 64 * h:192 - 64 * h], T.IDF[:, 64 * h:64 * h + 64], h == 0, h == 1)
+              for h in range(2)], "BW BT CK PZ IDF", "P4")
+        op("act", [act(T.LR[:, 64 * j:64 * j + 64], P[6][:, 64 * (j >> 1):64 * (j >> 1) + 64], F.Sign, bias=T.T3[:, 32 + (j & 1):33 + (j & 1)],
+                       scale=-1.0, accum_out=T.CNT[:, j:j + 1]) for j in range(8)], "K2", "P6 LR CNT")
+        op("act", [act(T.UT[:, 0:256], P[4][:, 0:256]), act(T.UT[:, 256:320], P[4][:, 256:320], F.Copy, bias=1.0)], "", "P4 UT")
+        mm([(P[7][:, 0:256], T.IDF[:], T.TRI[:], True, False)], "IDF K2", "P7")
+
+    def claim3():
+        op("dve", [ts(T.CL[:, 2 * o:2 * o + 2], T.CNT[:, 2 * o:2 * o + 2], 0.5, A.mult, 31.0 + 64 * o, A.add) for o in range(4)]
+           + [ts(T.CL[:, 8:16], T.CNT[:], 0.5, A.mult, 31.0, A.add)], "CNT", "CL")
+        op("dve", tt(T.MF[:], T.UT[:, 0:256].indirect(T.CL[:, 0:8]), T.JT[:], A.is_equal), "UT CL K2", "MF")
+        op("dve", [tt(T.VN[:, 0:128], T.UT[:, 256:320].indirect(T.CL[:, 8:16]), T.MF[:], A.mult),
+                   tt(T.VN[:, 128:256], T.NT[:, :].indirect(T.CL[:, 8:16]), T.MF[:], A.mult)], "UT MF CL K2", "VN")
+        mm([(P[6][:, 0:256], T.BO[:], T.VN[:], True, True)], "BO VN", "P6")
+        mm([(P[7][:, 128 * h:128 * h + 128], T.BO[:], T.VN[:, 0:128], False, h == 1) for h in range(2)], "BO VN", "P7")
+
+    def rep(n, rhs, r):
+        ks = [2 * (src & 1) + (src >> 1) for src in range(4)]
+        mm([(P[6][:, n * src:n * src + n], T.RW[:, k, :], rhs, True, True) for src, k in enumerate(ks)], "RW " + r, "P6")
+
+    def claim4():
+        op("dve", tt(T.DG[:], P[6][:, 0:256], T.DIAG[:], A.mult), "K2", "P6 DG")
+        op("dve", scan(T.DS[:], T.RM[:], T.DG[:], A.mult, A.add), "RM DG", "DS")
+        rep(8, T.DS[:, 143::16], "DS")
+        op("act", [act(T.AB[:, 32 * j:32 * j + 32], P[7][:, 128 * (j & 1) + 32 * (j >> 1):128 * (j & 1) + 32 * (j >> 1) + 32], F.Abs,
+                       bias=T.DS[:, 16 * j + 15:16 * j + 16], scale=-1.0) for j in range(8)], "DS", "P7 AB")
+        key, M3 = T.DS[:, 15:128:16], T.M3
+        op("dve", ts(T.I8[:, 0, :], key, -1.0, A.add), "DS", "I8")
+        op("dve", [ts(T.I8[:, 1, :], T.I8[:, 0, :], 1, SHR), ts(T.I8[:, 2, :], T.I8[:, 0, :], 1, AND),
+                   tt(M3[:, 40:48], T.I8[:, 0, :], T.T3[:, 16:24], A.subtract)], "I8 K2", "I9 D3")
+        op("dve", cp(T.NL[:], P[6][:, 0:32]), "", "P6 NL")
+        op("dve", [tt(M3[:, 24 + 8 * j:32 + 8 * j], T.I8[:, 1, :], T.T3[:, 24:32], A.add) for j in range(2)], "I9 K2", "D4")
+
+    def claim5(rd):
+        key, M3 = T.DS[:, 15:128:16], T.M3
+        op("dve", scan(T.DG[:], T.RB[:], T.AB[:], A.add, A.min), "RB AB", "DG")
+        op("dve", tt(M3[:, 16:24], T.DG[:, 31::32], key, A.min), "DG DS", "M3")
+        op("dve", ts(M3[:, 16:24], M3[:, 16:24], 0.5, A.is_gt), "", "M3")
+        if rd < 2:
+            op("dve", [tt(M3[:, 8:16], M3[:, 16:24], T.I8[:, 2, :], A.mult), tt(M3[:, 0:8], M3[:, 16:24], T.I8[:, 2, :], A.is_gt)], "I9", "M3")
+        a = 0 if rd < 2 else 16
+        op("dve", tt(M3[:, a:24], M3[:, a:24], M3[:, 24 + a:48], A.mult), "D3 D4", "M3")
+        op("dve", tt(M3[:, 48 + a:72], M3[:, a:24], T.T3[:, a:24], A.add), "M3 K2", "WR")
+        rep(24 - a, M3[:, 48 + a:72], "WR")
+
+    def claim5e(rd):
+        if rd == 2:
+            op("dve", cp(T.OO[:, rd], P[6][:, 0:32]), "", "P6 OO%d" % rd)
+            return
+        op("dve", cp(T.RL[:], P[6][:, 0:96]), "", "P6 RL")
+        op("dve", [cp(T.LOF[64 * h:64 * h + 64, :], T.RL[64 * h:64 * h + 64, :, h, :]) for h in range(2)] + [cp(T.OO[:, rd], T.RL[:, :, 2, :])],
+           "RL", "LOF OO%d" % rd)
+
+    def rec1(rd):
+        n = rd % 2
+        gather("act", T.TC[:], T["TO%d" % n][:, :], T.NL[:, :], "NL " + " ".join("TO%d_%d" % (n, c) for c in range(4)), "TC")
+
+    def rec1m():
+        mm([(P[7][:, 0:128], T.WZ[:, 3 - u:7 - u], T.TC[:, 128 * u:128 * u + 128], u == 0, u == 3) for u in range(4)], "WZ TC", "P7")
+
+    def rec2(rd):
+        op("dve", ts(T.CC[:], P[7][:, 0:128], 2.0, A.is_equal, 15.0, A.mult), "", "P7 CC")
+        if rd < 2:
+            mm([m for u in range(4) for m in
+                [(P[4][:, 128 * u:128 * u + 128], T.WLT[:], T.TC[:, 128 * u:128 * u + 128], True, False),
+                 (P[4][:, 128 * u:128 * u + 128], T.WLC[:, u], T.CC[:], False, True)]], "WLT WLC TC CC", "P4")
+            op("act", act(T.LR[:], P[4][:]), "", "P4 LR")
+
+    def rec3(rd):
+        mm([(P[7][:, 128:256], T.WK[:, 3 - u:7 - u], T.TC[:, 128 * u:128 * u + 128], u == 0, u == 3) for u in range(4)]
+           + [(P[7][:, 0:128], T.WD[:, 3 - u:7 - u], T.TC[:, 128 * u:128 * u + 128], u == 0, False) for u in range(4)]
+           + [(P[7][:, 0:128], IDB, T.CC[:], False, True)], "WD WK TE TC CC", "P7")
+        op("act", [act(T.SO[:, rd, :, 32 * j:32 * j + 32], P[7][:, 128 * j:128 * j + 128]) for j in range(2)], "", "P7 SO%d" % rd)
+
+    def lscatter(src):
+        op("dve", cp(T.L[:, :].indirect(T.LOF[:, 8 * src:8 * src + 8]), T.LR[:, 128 * src:128 * src + 128]), "LOF LR Lo La", "L")
+
+    def post(rd):
+        send([(d, T.LB[:, rd, me, :], T.SO[:, rd, d, :], "ao%d" % rd) for d in peers]
+             + [(d, T.LO[:, rd, me], T.OO[:, rd], "ao%d" % rd) for d in peers], 2, "SO%d OO%d" % (rd, rd))
+        arrives("ao%d" % rd, 12, "LB%d" % rd)
+
+    def own1(rd):
+        for b, j, W in ((2, 0, lambda k, d: T.IW[:, k, 96 - 32 * d:224 - 32 * d]), (3, 1, lambda k, d: T.KWM[:, k, 3 - d:7 - d])):
+            mm([(P[b][:, 32 * s:32 * s + 32], W(s, d), (T.SO if d == me else T.LB)[:, rd, d, 32 * j:32 * j + 32], d == 0, d == 3)
+                for s in range(4) for d in range(4)], "IW KWM SO%d LB%d" % (rd, rd), "P%d" % b)
+        op("act", act(T.VC[:], P[2][:, 0:128]), "", "P2 VC")
+        op("act", act(T.VK[:], P[3][:, 0:128]), "", "P3 VK")
+
+    def own2(rd):
+        op("dve", [cp(T.OL[32 * d:32 * d + 32, :], T.OO[32 * d:32 * d + 32, rd, :, 2 * me:2 * me + 2] if d == me
+                      else T.LO[32 * d:32 * d + 32, rd, d, :, 2 * me:2 * me + 2]) for d in range(4)], "OO%d LB%d" % (rd, rd), "OL")
+
+        def sc(W, Vv, s, k):
+            op("dve", cp(W[:, :].indirect(T.OL[:, 2 * s:2 * s + 2]), Vv[:, 32 * s:32 * s + 32]), "OL V" + k[0], k)
+        order = [(0, 3), (1, 3), (0, 2), (1, 2), (0, 1), (1, 1), (0, 0), (1, 0)] if rd < 2 else [(0, 3), (0, 2), (0, 1), (1, 3), (0, 0), (1, 2), (1, 1), (1, 0)]
+        for w, s in order:
+            sc((T.CW, T.KW)[w], (T.VC, T.VK)[w], s, ("CW", "KW")[w])
+            if rd == 2 and (w, s) == (0, 0):
+                dma("sp", [(T.ycells[:], T.CW[:, 0:2048])], "CW", "yc")
+        if rd == 2:
+            dma("act", [(T.ykids[4 * e:4 * e + 4, :], T.KW[16 * e:16 * e + 4, 0:2048]) for e in range(4)], "KW", "yk")
+            dma("sp", [(T.ykids[4 * e:4 * e + 4, :], T.KW[16 * e:16 * e + 4, 0:2048]) for e in range(4, 8)], "KW", "yl")
+
+    for cc in range(4):
+        tgather(0, "act" if cc & 1 else "dve", cc)
+    zmm(0, 0)
+    zmm(0, 1)
+    tpart(0, 0)
+    cond(0)
+    zmm(0, 2)
+    zmm(0, 3)
+    cmm(0)
+    zero("IW")
+    cond(1)
+    zero("KWM")
+    tevac(0)
+    tpart(0, 1)
+    cmm(1)
+    tevac(1)
+    hash1(consts2)
+    for b in range(4):
+        put("IW", T.IW[:, b, 96:128], [[-1, 32]], -32 * b, 1)
+        for e in range(2):
+            put("KWM", T.KWM[:, b, 3, :, 0:4], [[-16, 2], [-2, 4]], -32 * b - e, 128 if e == 0 else 1)
+    for rd in range(3):
+        lookup(rd)
+        choose(rd)
+        newlist(rd)
+        if rd == 2:
+            send([(d, T.YL[:, 64 * me:64 * me + 64], T.YN[:, 64 * d:64 * d + 64], "ay") for d in peers], 4, "YN0 YN1")
+            arrives("ay", 12, "YL")
+            dma("sp", [(T.ynodes[32 * d:32 * d + 32, :], (T.YN if d == me else T.YL)[:, 64 * d:64 * d + 64]) for d in range(4)], "YN0 YN1 YL", "yn")
+            claim2()
+            own1(0)
+            claim3()
+            own2(0)
+            claim4()
+            rec1(rd)
+            rec1m()
+            claim5(rd)
+            rec2(rd)
+            rec3(rd)
+            claim5e(rd)
+            post(rd)
+            own1(1)
+            own2(1)
+            own1(2)
+            own2(2)
+            break
+        tgather(rd + 1, "dve", 0)
+        claim2()
+        zmm(rd + 1, 0)
+        tgather(rd + 1, "act", 1)
+        tgather(rd + 1, "act", 3)
+        claim3()
+        tgather(rd + 1, "dve", 2)
+        zmm(rd + 1, 1)
+        claim4()
+        rec1(rd)
+        cond(0)
+        zmm(rd + 1, 2)
+        zmm(rd + 1, 3)
+        rec1m()
+        claim5(rd)
+        rec2(rd)
+        cond(1)
+        tpart(rd + 1, 0)
+        cmm(0)
+        tevac(0)
+        tpart(rd + 1, 1)
+        cmm(1)
+        tevac(1)
+        claim5e(rd)
+        lscatter(3)
+        lscatter(2)
+        rec3(rd)
+        post(rd)
+        hash1(lambda j: lscatter(1 - j))
+    for s, v in total.items():
+        if seen["pool"].get(s, 0) < v:
+            g.wait_ge(T.sem[s], v)

@@ -11,22 +11,25 @@ def _decl(dt, **kw):
 
 
 _decl(b16, XS=[4, 512], X=[2048], H=[4, 512], C0=[4, 128], SH=[8, 4, 4], SX=[8, 4, 4], WH=[4, 128], WX=[4, 128],
-      G=[8192], TT=[8192], TO0=[4096], TO1=[4096], L=[4224], LS=[2, 1024], CW=[2080], KH=[512], KLO=[512], ZR=[512],
-      WZ=[7, 2, 4, 4], WD=[7, 2, 4, 4], WK=[7, 2, 16], WT=[18], WC=[40], MK=[8], DM=[8, 16], WLW=[24], WLK=[32], TE=[256],
-      BW=[5, 64], BT=[5, 64], WP1=[8, 16], WP2=[8, 8, 16], WLT=[4, 2, 16], WLC=[4, 4, 2, 16], IW=[4, 224], KWM=[4, 7, 2, 16],
-      C=[1024], R=[2048], MO=[256], CK=[512], TC=[512], CC=[128], LR=[512], VC=[128], SO=[3, 4, 64], LB=[3, 4, 64])
-_decl(f32, RT=[8, 4, 4], CT=[8, 4, 4], FF=[16], J16=[20], GB=[16], KB=[4, 4, 2, 16], KT=[4, 4, 32], NF=[256],
-      KF=[512], KW=[2080], IDF=[128], NEG=[128], PM=[128], RW=[4, 128], BO=[128], WF=[4], JT=[128], NT=[64], DIAG=[256], RM=[256],
-      RB=[256], TRI=[256], T3=[36], NM=[9, 64], HP=[128], BX=[128], OW=[64], H1=[128], H2=[128], SEL=[128], MS=[64],
-      PR=[4, 128], QM=[2, 128], EM=[128], AN=[64], PZ=[192], UT=[320], CNT=[8], VN=[256], RL=[4, 3, 8],
-      MF=[128], DG=[256], DS=[256], AB=[256], M3=[72], VK=[128], YN=[256], YL=[256], OO=[3, 4, 8], LO=[3, 4, 4, 8])
-_decl(i32, PI=[1], FI=[16], KA=[4, 2, 64], NS=[4, 64], NI=[256], KN=[512], WI=[4], HI=[64], HJ=[4, 64], I8=[3, 8])
-_decl(u16, KL=[512], TL=[512], PL=[256], LL=[128], CL=[16], NL=[32], LOF=[32], OL=[8])
-SCRATCH["S"] = ("dram", [4, 128, 1024], b16)
+      G=[8192], TT=[8192], TO=[4096], L=[8320], LS=[4, 512], CW=[2080], KH=[512], KLO=[512],
+      WZ=[13, 4, 4], WY=[13, 16], WT=[4], WC=[16], MK=[8], SM=[2], DM=[8, 16], R0=[2, 2, 2, 16], WF=[2], WD=[32], WK=[32], WE=[64], WJ=[64],
+      WQ=[2, 136], RP=[256], B2=[144], TE=[192], IDB=[128], TRI=[256], BW=[2, 128], BT=[2, 2, 128], WP1=[8, 16], WLX=[128], WKD=[8, 128],
+      RB16=[4, 128], WA=[4, 14, 16], WB=[4, 14, 16], WO=[4, 14, 16],
+      C=[8, 2, 64], Y=[1024], R=[2048], EQ=[512], TQ=[128], SEL=[128], SC=[6, 64], MO=[256], CK=[384], MF=[128], SG=[512],
+      YG=[3, 128], LR=[512], VC=[3, 128], LB=[3, 4, 32], UH=[128])
+_decl(f32, RT=[8, 4, 4], CT=[8, 4, 4], FF=[40], J16=[20], GB=[16], KB=[4, 4, 2, 16], KT=[4, 4, 32], NF=[256], MI=[128],
+      KF=[512], KW=[2080], IDF=[128], PM=[2, 17, 8], PF=[33, 4], RW=[4, 128], BO=[128], WG=[4], JT=[128], DIAG=[128], RM=[128],
+      RB=[256], T3=[18], TP=[4, 16], NM=[128], HP=[128], PR=[2, 2, 4, 32], PZ=[130], UT=[320], CNT=[8], CF=[8], VN=[128],
+      DG=[256], DS=[128], AB=[256], M3=[48], VK=[3, 128], YN=[2, 128], YL=[4, 128], YF=[256])
+_decl(i32, PI=[1], FI=[16], KA=[4, 2, 64], NS=[4, 64], NI=[256], KN=[512], WI=[4], HI=[2, 2, 16], HJ=[3, 64])
+_decl(u16, KL=[512], TL=[512], PL=[256], LL=[128], CL=[16], NL=[8], OO=[3, 4, 16], LO=[3, 4, 4, 16], OL=[3, 8])
+SCRATCH["S"] = ("dram", [4, 128, 512], b16)
 for _b in range(8):
     SCRATCH["P%d" % _b] = ("psum", [128, 512], f32)
-SEMAPHORES = (["pe", "dve", "act", "pool", "ax0", "ax1", "ax2", "ax3", "ak", "an", "al", "ao0", "ao1", "ao2", "ay"]
-              + ["d%d" % i for i in range(40)])
+SEMAPHORES = (["pe", "dve", "act", "pool", "ax0", "ax1", "ax2", "ax3", "ak", "an", "al0", "al1", "al2", "al3",
+               "ao0", "ao1", "ao2", "ar0", "ar1", "ar2", "ay"] + ["d%d" % i for i in range(48)])
+
+ORDER = [7,8,1,6,4,3,14,24,9,2,10,85,5,23,11,15,12,22,-29,-27,-28,16,30,32,37,54,-34,-33,53,62,56,55,57,40,58,41,73,43,13,75,39,36,42,77,44,93,-76,18,71,-74,83,59,47,-72,170,122,35,20,78,51,38,25,65,45,17,49,139,91,-46,128,61,19,94,-26,-50,52,98,158,-48,84,89,63,101,-31,141,21,92,96,133,100,167,102,111,-97,68,103,66,108,135,112,104,70,64,119,60,-105,95,124,106,-99,121,110,120,115,-109,67,117,-116,168,113,-107,118,69,86,132,90,153,125,114,129,151,-146,154,142,79,160,147,-150,123,140,161,162,145,-152,80,87,126,127,81,-148,137,149,155,130,131,166,184,-185,82,88,156,-187,186,192,193,-189,157,194,188,198,196,-191,197,190,195,163,200,199,202,169,203,204,206,205,207,209,208,212,171,134,210,164,201,213,-211,-173,216,144,217,214,218,221,222,136,-215,220,223,143,230,219,138,-224,165,225,-229,228,234,159,231,226,-227,233,174,235,232,237,236,238,239,240,241,242,243,245,248,246,-247,244,249,172,253,254,251,255,288,257,250,256,258,-291,259,260,176,261,252,262,263,-289,290,264,177,265,-293,178,269,266,302,270,268,298,292,296,271,273,275,300,-294,179,299,272,175,277,267,180,297,278,301,-295,279,276,306,307,181,280,310,311,281,308,284,282,274,309,303,182,313,316,312,285,314,317,183,-315,318,320,304,286,-319,305,325,321,324,326,322,327,287,283,323,-328,329,332,-331,335,336,334,-333,330,339,340,341,338,342,343,337,344,345,346,347,349,352,350,348,351,353,357,358,355,359,392,354,360,362,-393,361,363,364,365,356,366,367,-394,395,368,369,-399,373,370,404,398,408,402,-397,403,374,396,400,412,375,405,413,376,495,401,-372,381,410,382,377,378,411,383,417,371,379,384,414,-380,415,385,416,388,386,418,406,-419,407,424,420,389,409,429,425,390,430,431,426,421,-432,391,422,427,-423,387,433,428,436,-437,441,439,434,-435,496,442,438,443,497,445,440,498,446,444,447,448,449,450,456,451,457,453,454,459,458,452,-455,522,460,461,465,490,462,463,499,464,466,500,467,501,468,469,504,502,470,471,-503,513,505,472,506,474,514,477,-476,473,507,478,481,480,475,515,479,516,491,492,483,484,485,486,493,509,494,517,508,487,518,510,512,488,519,511,482,531,536,520,532,-521,523,537,524,533,-539,525,534,526,527,535,529,538,528,530,489,540,541,543,545,547,542,549,544,546,548,551,550]
 
 
 def rank_program(g, core, T, topo):
@@ -58,8 +61,24 @@ def rank_program(g, core, T, topo):
             wrote[k] = [(s, v)]
             read[k] = []
 
+    prog = []
+
     def op(q, fns, r, w):
-        r, w = r.split(), w.split()
+        prog.append(("op", q, fns, r.split(), w.split()))
+
+    def dma(q, pairs, r, w):
+        prog.append(("dma", q, pairs, r.split(), w.split()))
+
+    def send(items, n, r):
+        prog.append(("send", "pool", (items, n), r.split(), []))
+
+    def arrives(s, v, w):
+        prog.append(("arr", "ext", (s, v), [], w.split()))
+
+    def either(o, i, r, w):
+        op("x", (cp(o, i), act(o, i)), r, w)
+
+    def do_op(q, fns, r, w):
         need(q, r, w)
         for f in (fns if isinstance(fns, list) else [fns]):
             f().then_inc(T.sem[q], 1)
@@ -70,8 +89,7 @@ def rank_program(g, core, T, topo):
         nsem[0] += 1
         return "d%d" % (nsem[0] - 1)
 
-    def dma(q, pairs, r, w):
-        r, w = r.split(), w.split()
+    def do_dma(q, pairs, r, w):
         need(q, r, w)
         s = newsem()
         for o, i in pairs:
@@ -84,8 +102,7 @@ def rank_program(g, core, T, topo):
             m |= 1 << e
         return m
 
-    def send(items, n, r):
-        r = r.split()
+    def do_send(items, n, r):
         need("pool", r, [])
         s = newsem()
         if len(items) == 1:
@@ -100,9 +117,6 @@ def rank_program(g, core, T, topo):
                                             remote_sem=T.sem[rs], srcs=[i], dsts=[o]))
             g.remote_dma_fused(tr, local_sem=T.sem[s])
         done(s, n * len(items), r, [])
-
-    def arrives(s, v, w):
-        done(s, v, [], w.split())
 
     def mm(ms, r, w):
         op("pe", [(lambda m=m: g.tensor.matmul(*m)) for m in ms], r, w)
@@ -130,6 +144,10 @@ def rank_program(g, core, T, topo):
     def io(o, pat, base, cm=0):
         return lambda: g.iota(o, pat, base, cm, allow_small_or_imprecise_dtypes=True)
 
+    def puts(key, items):
+        op("pool", [(lambda o=o, pat=pat, base=base, val=val: g.affine_select(o, o, pat, A.not_equal, float(val), base, 1))
+                    for o, pat, base, val in items], "", key)
+
     def put(key, o, pat, base, val, cm=1):
         op("pool", lambda: g.affine_select(o, o, pat, A.not_equal, float(val), base, cm), "", key)
 
@@ -137,7 +155,10 @@ def rank_program(g, core, T, topo):
         op("pool", lambda: g.affine_select(o, o, pat, A.is_ge, 0.0, base, cm), "", key)
 
     SHR, AND = A.arith_shift_right, A.bitwise_and
-    FF, IDB = T.FF, T.TE[:, 128:256]
+    FF, IDB = T.FF, T.IDB[:]
+
+    def col(j):
+        return FF[:, j:j + 1]
 
     def xload(dst, d):
         return [(dst(h), T.cells[32 * d:32 * d + 32, 1024 * h:1024 * h + 1024]) for h in range(2)]
@@ -145,14 +166,15 @@ def rank_program(g, core, T, topo):
         dma("sp", xload(lambda h: T.XS[64 * h:64 * h + 64, d, :], d), "", "XS%d" % d)
     dma("act", xload(lambda h: T.X[64 * h:64 * h + 64, 512 * me:512 * me + 512], me), "", "X%d" % me)
     dma("sp", [(T.KA[:, e // 2, e % 2, :], T.kids[4 * e:4 * e + 4, :]) for e in range(8)], "", "KA")
+    dma("act", [(T.KN[:], T.kids[:])], "", "KN")
 
     op("pool", lambda: g.iota(T.PI[:], [[0, 1]], 0, 1), "", "PI")
     op("dve", [ms(T.BO[:], 1.0), ms(T.SH[:], 0.0), ms(T.SX[:], 0.0)], "", "SH SX BO")
-    op("dve", scan(T.MF[:], T.BO[:], T.BO[:], A.mult, A.add), "BO", "MF")
-    fields = [(3, 3), (1, 16), (1, 3), (0, 65), (0, 15), (0, 12), (0, 9), (5, 1), (6, 1)]
+    op("dve", scan(T.MI[:], T.BO[:], T.BO[:], A.mult, A.add), "BO", "MI")
+    fields = [(3, 3), (1, 16), (1, 3), (0, 65), (0, 15), (0, 12), (2, 9), (4, 1), (6, 1), (0, 1), (0, 29), (0, 32), (1, 1), (0, 3), (5, 3), (0, 63)]
     op("dve", [ts(T.FI[:, j:j + 1], T.PI[:], s, SHR, m, AND) for j, (s, m) in enumerate(fields)], "PI", "FI")
-    op("dve", [ts(T.C0[:, a, :], T.MF[:], -1.0, A.add) for a in range(4)], "MF", "C0")
-    op("dve", cp(FF[:, 0:9], T.FI[:, 0:9]), "FI", "FF")
+    op("dve", [ts(T.C0[:, a, :], T.MI[:], -1.0, A.add) for a in range(4)], "MI", "C0")
+    op("dve", [cp(FF[:, 0:16], T.FI[:, 0:16]), ts(T.RP[:, 0:128], T.MI[:], -41.0, A.add), ts(T.RP[:, 128:256], T.MI[:], 87.0, A.add)], "FI MI", "FF RP")
     op("dve", [ms(T.C0[p:p + 32, a, :], float(a)) for p in (32, 96) for a in range(4)], "", "C0")
 
     def hconst(slot):
@@ -165,15 +187,17 @@ def rank_program(g, core, T, topo):
     for d in peers:
         send([(d, T.X[:, 512 * me:512 * me + 512], T.XS[:, d, :], "ax%d" % me)], 16, "XS%d" % d)
         arrives("ax%d" % d, 16, "X%d" % d)
-    op("dve", [tt(FF[:, 10:11], FF[:, 0:1], FF[:, 1:2], A.add), ts(FF[:, 11:12], FF[:, 4:5], 3.0, A.is_equal, 4.0, A.mult),
-               ts(FF[:, 12:13], FF[:, 5:6], 12.0, A.is_equal, -1.0, A.mult), ts(FF[:, 13:14], FF[:, 6:7], 8.0, A.is_equal, -129.0, A.mult),
-               ts(FF[:, 14:15], FF[:, 7:8], 2048.0, A.mult, FF[:, 4:5], A.add)], "FF", "FG")
-    dma("sp", [(T.KN[:], T.kids[:])], "", "KN XS%d" % peers[1])
-    dma("sp", [(T.CW[:, 0:2048], T.cells[:])], "", "CW")
+    op("dve", [tt(col(20), col(0), col(1), A.add), ts(col(21), col(4), 3.0, A.is_equal, 4.0, A.mult),
+               ts(col(22), col(5), 12.0, A.is_equal, -1.0, A.mult), ts(col(23), col(6), 8.0, A.is_equal, -129.0, A.mult),
+               ts(col(26), col(11), 2.0, A.mult, col(10), A.add), ts(col(27), col(12), 15.0, A.mult, 1.0, A.add),
+               ts(col(28), col(5), 2.0, A.mult, col(13), A.add), cp(col(29), T.PI[:])], "FF PI", "FG")
     dma("sp", [(T.NS[:, d, :], T.nodes[32 * d:32 * d + 32, :]) for d in peers], "", "NS")
     dma("sp", [(T.NI[:, 64 * me:64 * me + 64], T.nodes[32 * me:32 * me + 32, :]), (T.WI[0:32, 0:1], T.wt[32 * me:32 * me + 32, :])], "", "NIo WI")
+    for n, k in (("PM", 136), ("DM", 128), ("R0", 128), ("WZ", 208), ("WY", 208), ("WP1", 128), ("WD", 32), ("WE", 64), ("WK", 32), ("WJ", 64), ("WQ", 136)):
+        parts = [T[n][:, 0], T[n][:, 1]] if k == 136 else [T[n][:]]
+        op("x", (ms(T[n][:], 0.0), [act(o, T.RP[:, 0:k], F.Copy, scale=0.0) for o in parts]), "RP", n)
     hconst(0)
-    op("act", [act(T.RT[:], T.RT[:], F.Abs, bias=FF[:, 10:11], scale=-1.0), act(T.CT[:], T.CT[:], F.Abs, bias=FF[:, 2:3], scale=-1.0)],
+    op("act", [act(T.RT[:], T.RT[:], F.Abs, bias=col(20), scale=-1.0), act(T.CT[:], T.CT[:], F.Abs, bias=col(2), scale=-1.0)],
        "FF FG", "RT CT")
     hconst(1)
 
@@ -182,10 +206,8 @@ def rank_program(g, core, T, topo):
         op("dve", [ts(T.H[0:64, slot, :], T.X[0:64, c], 15.0, A.is_equal), ts(T.H[64:128, 2 + slot, :], T.X[64:128, c], 15.0, A.is_equal)],
            "X%d" % src, "H%d" % slot)
 
-    def zero(names):
-        op("dve", [ms(T[n][:], 0.0) for n in names.split()], "", names)
     hot(me, 0)
-    op("dve", [ts(T.GB[:], T.J16[:, 0:16], FF[:, 11:12], A.mult, FF[:, 12:13], A.add), ts(T.J16[:, 16:20], T.J16[:, 16:20], FF[:, 3:4], A.is_equal),
+    op("dve", [ts(T.GB[:], T.J16[:, 0:16], col(21), A.mult, col(22), A.add), ts(T.J16[:, 16:20], T.J16[:, 16:20], col(3), A.is_equal),
                tt(T.RT[:], T.RT[:], T.CT[:], A.max)], "FF FG CT", "J16 GB RT")
     op("dve", [ts(T.SH[:, :, 0:3, 0:3], T.RT[:, :, 0:3, 0:3], 1.0, A.is_equal),
                ts(T.SX[:, :, 0:3, 0:3], T.RT[:, :, 0:3, 0:3], 0.0, A.is_equal, 16.0, A.mult),
@@ -195,403 +217,386 @@ def rank_program(g, core, T, topo):
     op("dve", [ms(T.WH[64 * (1 - h) + 32 * b:64 * (1 - h) + 32 * b + 1, 2 * h:2 * h + 2, 7 - 4 * b::16], 1.0) for h in range(2) for b in range(2)],
        "", "WH")
 
-    def gbuild(i, src, j, q):
+    def gbuild(i, src, j):
         ch, c, b = 4 * src + j, slice(512 * src, 512 * src + 512), (4 * i + j) % 8
         mm([(P[b][:], T.WX[:, j, :], T.X[:, c], True, False), (P[b][:], T.WH[:, j, :], T.H[:, (j & 2) + (i & 1), :], False, True)],
            "WH WX HC%d X%d H%d" % (i & 1, src, i & 1), "P%d" % b)
         o, bias = T.G[:, 512 * ch:512 * ch + 512], T.GB[:, ch:ch + 1]
-        op(q, act(o, P[b][:], F.Relu, bias=bias) if q == "act" else ts(o, P[b][:], bias, A.add, 0.0, A.max), "GB", "P%d G%d" % (b, ch))
+        op("x", (ts(o, P[b][:], bias, A.add, 0.0, A.max), act(o, P[b][:], F.Relu, bias=bias)), "GB", "P%d G%d" % (b, ch))
     for j in range(4):
-        gbuild(0, me, j, "act")
-    zero("WP1 WP2 PM RW WC DM WZ WT IDF NEG WLW WLK")
-    op("dve", [ms(T.MK[:], 1.0), ms(T.TE[:, 0:128], 1.0), ms(IDB, 0.0)], "", "MK TE")
-    op("dve", [cp(T.KB[:, :, :, s, :], T.KA[:, :, s, :]) for s in range(2)], "KA", "KB")
-    hot(peers[0], 1)
-    for j in range(4):
-        gbuild(1, peers[0], j, "act")
-    op("dve", lambda: V.transpose(T.KT[:], T.KB[:]), "KB", "KT")
-    op("dve", [cp(T.KL[:, b::4], T.KT[:, :, b, :]) for b in range(4)], "KT", "KL")
-    hot(peers[1], 0)
-    for j in range(4):
-        gbuild(2, peers[1], j, "act")
-    op("dve", cp(T.TL[:, 128 * me:128 * me + 128], T.KL[:, 128 * me:128 * me + 128]), "KL", "TLo")
-    zero("BW BT ZR PZ RB")
-    hot(peers[2], 1)
+        gbuild(0, me, j)
     op("dve", cp(T.KF[:], T.KN[:]), "KN", "KF")
+    op("dve", [ts(col(30), col(8), 2.0, A.mult, col(26), A.add), ts(col(31), col(7), 64.0, A.mult, col(28), A.add)]
+       + [ts(col(32 + d), col(14), float(d), A.is_equal) for d in range(4)], "FF FG", "FH")
     op("dve", ts(T.KN[:], T.KN[:], 127, AND), "", "KN")
-    op("dve", ts(T.KH[:], T.KF[:], 1.0 / 128, A.mult, 128.50390625, A.add), "KF", "KH")
+    op("act", act(T.KH[:], T.KF[:], F.Copy, scale=1.0 / 128, bias=128.50390625), "KF", "KH")
+    op("dve", [ts(T.WLX[:], T.RP[:, 40:168], col(30), A.is_equal, col(27), A.mult)]
+       + [ts(T.WKD[:, 2 * d + e], T.RP[:, 8 - 4 * e:136 - 4 * e], col(31), A.is_equal, col(32 + d), A.mult) for d in range(4) for e in range(2)],
+       "RP FH", "WLX WKD")
     op("dve", cp(T.KLO[:], T.KN[:]), "KN", "KLO")
-    for j in range(4):
-        gbuild(3, peers[2], j, "dve" if j == 3 else "act")
-    GALL = " ".join("G%d" % c for c in range(16))
-
-    put("WP1", T.WP1[:, :, 0:8], [[-16, 8], [-2, 8]], 0, 1)
-    put("WP1", T.WP1[:, :, 0:8], [[-16, 8], [-2, 8]], -1, 16)
-    op("pool", [(lambda q=q, e=e: g.affine_select(T.WP2[:, 2 * q + e, :, 8 + e::2], T.WP2[:, 2 * q + e, :, 8 + e::2], [[-16, 8], [-4, 4]],
-                                                  A.not_equal, 1.0, -q, 1)) for q in range(4) for e in range(2)], "", "WP2")
-    send([(d, T.TL[:, 128 * me:128 * me + 128], T.KL[:, 128 * d:128 * d + 128], "ak") for d in peers], 4, "KL")
-    arrives("ak", 12, "TL")
-    put("PM", T.PM[:], [[1, 4], [-64, 2], [-4, 16]], -3, 1)
-    for b in range(4):
-        put("RW", T.RW[:, b, :], [[0, 4], [-1, 32]], -32 * b, 1)
-    for e in range(6):
-        n = 3 if e < 4 else 2
-        put("WC", T.WC[:, 0:8 * n], [[-6, n], [-16, 2], [-32, 4]], -e, 16 ** e)
-    keep("MK", T.MK[:], [[-16, 2], [-32, 4]], 0, 1)
-    keep("MK", T.MK[:], [[16, 2], [32, 4]], 15, -1)
+    op("dve", [cp(T.KB[:, :, :, s, :], T.KA[:, :, s, :]) for s in range(2)], "KA", "KB")
+    op("dve", [ts(T.IDF[:], T.RP[:, 40:168], col(29), A.is_equal), ts(IDB, T.RP[:, 40:168], col(29), A.is_equal)], "RP FG", "IDF IDB")
+    op("dve", lambda: V.transpose(T.KT[:], T.KB[:]), "KB", "KT")
+    op("dve", [ts(T.TE[:, 64:192], T.RP[:, 40:168], col(29), A.is_equal), ts(T.TE[:, 0:64], T.RP[:, 40:104], col(15), A.is_gt)], "RP FF FG", "TE")
+    op("dve", [cp(T.KL[:, b::4], T.KT[:, :, b, :]) for b in range(4)], "KT", "KL")
+    op("dve", cp(T.TL[:, 128 * me:128 * me + 128], T.KL[:, 128 * me:128 * me + 128]), "KL", "TLo")
     send([(d, T.NI[:, 64 * me:64 * me + 64], T.NS[:, d, :], "an") for d in peers], 4, "NS")
     arrives("an", 12, "NI")
-    for t in range(4):
-        tr, tc = 1 - (t >> 1), 1 - (t & 1)
-        put("DM", T.DM[:, 2 * t:2 * t + 2, 12:16], [[-16, 2], [-4, 2], [-1, 2]], -8 * tr - 2 * tc, 1)
-        put("WZ", T.WZ[:, 3, :, tr:tr + 3, tc:tc + 3], [[-16, 2], [-4, 3], [-1, 3]], -32 * t, 1)
-    put("WT", T.WT[:, 0:8], [[-16, 8]], -3, 128)
-    put("WT", T.WT[:, 0:8], [[-16, 8]], -7, 1)
-    put("TE", IDB, [[-1, 128]], 0, 1)
-    put("IDF", T.IDF[:], [[-1, 128]], 0, 1)
+    puts("PM", [(T.PM[:, kh, 1::2, :], [[1, 4], [-64, 2], [-8, 8]], -3 - 4 * kh, 1) for kh in range(2)])
+    send([(d, T.TL[:, 128 * me:128 * me + 128], T.KL[:, 128 * d:128 * d + 128], "ak") for d in peers], 4, "KL")
+    arrives("ak", 12, "TL")
+    quad = [(t, 1 - (t >> 1), 1 - (t & 1)) for t in range(4)]
+    puts("DM", [(T.DM[:, 2 * t:2 * t + 2, 12:16], [[-16, 2], [-4, 2], [-1, 2]], -8 * tr - 2 * tc, 1) for t, tr, tc in quad])
 
-    def gather(q, o, win, off, r, w):
-        op(q, act(o, win.indirect(off)) if q == "act" else cp(o, win.indirect(off)), r, w)
+    def lpack(d):
+        b = 4 + (d ^ me)
+        xs, k = (T.X[:, 512 * me:512 * me + 512], "X%d" % me) if d == me else (T.XS[:, d, :], "XS%d" % d)
+        mm([(P[b][:], T.WLX[:], xs, True, False), (P[b][:], T.WKD[:, 2 * d], T.KH[:], False, False),
+            (P[b][:], T.WKD[:, 2 * d + 1], T.KLO[:], False, True)], "WLX WKD KH KLO " + k, "P%d" % b)
+        op("x", (ts(T.LS[:, d, :], P[b][:], col(23), A.add), act(T.LS[:, d, :], P[b][:], bias=col(23))), "FG", "P%d LS%d" % (b, d))
+    for d in peers + [me]:
+        lpack(d)
+    for d in peers:
+        send([(d, T.S[me], T.LS[:, d, :], "al%d" % me)], 16, "LS%d" % d)
+        arrives("al%d" % d, 16, "S%d" % d)
+    dma("sp", [(T.CW[:, 0:2048], T.cells[:])], "", "CW")
+    for d in [me] + peers:
+        dma("sp", [(T.L[32 * r:32 * r + 32, 2048 * d:2048 * d + 2048], T.LS[:, d, :] if d == me else T.S[d]) for r in range(4)],
+            "LS%d" % d if d == me else "S%d" % d, "L%d" % d + (" KL" if d == me else ""))
+    dma("sp", [(T.KW[16 * e:16 * e + 4, 0:2048], T.KF[16 * e:16 * e + 16, :]) for e in range(8)], "KF", "KW")
+    hot(peers[0], 1)
+    hot(peers[1], 0)
+    op("dve", [ms(T.MK[:], 1.0), ms(T.BW[:], 1.0), ms(T.BT[:], 1.0),
+               ts(T.WI[0:32, 1:2], T.WI[0:32, 0:1], 6, SHR), ts(T.WI[0:32, 2:3], T.WI[0:32, 0:1], 63, AND),
+               cp(T.SM[:, 1:2], col(7)), ts(T.SM[:, 0:1], col(7), 0.0, A.is_equal)], "WI FF", "MK BW BT WI2 SM")
+    for i in range(1, 4):
+        for j in range(4):
+            if (i, j) == (1, 3):
+                op("dve", [ts(T.WF[0:32, 0:1], T.WI[0:32, 1:2], 64.0, A.mult), cp(T.WF[0:32, 1:2], T.WI[0:32, 2:3])], "WI2", "WF")
+            if (i, j) == (2, 0):
+                hot(peers[2], 1)
+            if (i, j) == (2, 3):
+                op("dve", cp(T.NF[:], T.NI[:]), "NI NIo", "NF")
+            gbuild(i, peers[i - 1], j)
+    GALL = " ".join("G%d" % c for c in range(16))
+    LALL = "L0 L1 L2 L3 L"
 
-    def tbuild(q, a, b):
-        gather(q, T.TT[:, 16 * a:16 * b], T.G[:, :], T.TL[:, a:b], GALL + " TL TLo", "TT%d" % a)
-    tbuild("act", 0, 64)
-    tbuild("dve", 64, 224)
-    for q in range(4):
-        mm([m for pi in range(2) for m in
-            [(P[q][:, 256 * pi:256 * pi + 256], T.WP1[:], T.CW[:, 512 * q + pi:512 * q + 512:2], True, False),
-             (P[q][:, 256 * pi:256 * pi + 256], T.WP2[:, 2 * q], T.KH[:, pi::2], False, False),
-             (P[q][:, 256 * pi:256 * pi + 256], T.WP2[:, 2 * q + 1], T.KLO[:, pi::2], False, True)]], "WP1 WP2 CW KH KLO", "P%d" % q)
-    op("dve", [ts(T.WI[0:32, 1:2], T.WI[0:32, 0:1], 6, SHR), ts(T.WI[0:32, 2:3], T.WI[0:32, 0:1], 63, AND)], "WI", "WJ")
-    op("dve", cp(T.NF[:], T.NI[:]), "NI NIo", "NF")
-    mm([(P[5][:, 0:256], T.PM[:], T.NF[:], True, True)], "PM NF", "P5")
-    op("dve", [ts(T.WF[0:32, 0:1], T.WI[0:32, 1:2], 64.0, A.mult), cp(T.WF[0:32, 1:2], T.WI[0:32, 2:3]), ms(T.RM[:], 1.0)], "WJ", "WF RM")
-    mm([(P[4][:, 0:2], T.RW[0:32, 0, :], T.WF[0:32, 0:2], True, True)], "RW WF", "P4")
-    zero("WD WK WLT WLC")
-    for q in range(4):
-        op("act", act(T.LS[:, :, 256 * q:256 * q + 256], P[q][:], bias=FF[:, 13:14]), "FG", "P%d LS%d" % (q, q))
-    LSA = "LS0 LS1 LS2 LS3"
-    dma("sp", [(T.S[:, 32 * j:32 * j + 32, :], T.LS[:, j >> 1, :]) for j in range(4)], LSA, "S")
-    op("dve", cp(T.WF[:, 2:4], P[4][:, 0:2]), "", "P4 WG")
-    op("dve", cp(T.PL[:], P[5][:, 0:256]), "", "P5 PL")
-    op("dve", [ts(T.WC[:, 24:32], T.MK[:], T.WF[:, 2:3], A.mult), ts(T.WC[:, 32:40], T.MK[:], T.WF[:, 3:4], A.mult)], "WG MK", "WC")
-    mm([(P[4][:, 0:10], T.DM[0:32], T.WC[0:32, 0::4], True, True)], "DM WC", "P4")
-    tbuild("act", 224, 416)
-    tbuild("dve", 416, 512)
-    op("dve", cp(T.WT[:, 8:18], P[4][:, 0:10]), "", "P4 WT")
-    TALL = "TT0 TT64 TT224 TT416"
-    dma("sp", [(T.L[32 * j:32 * j + 32, 1024 * me:1024 * me + 1024], T.LS[32 * me:32 * me + 32, j >> 1, :]) for j in range(4)], LSA + " S", "Lo")
-
-    put("NEG", T.NEG[:], [[-1, 128]], 0, -1)
+    puts("R0", [(T.R0[:, sh], [[-16, 2], [0, 2], [-1, 16]], 0, 1) for sh in range(2)])
+    keep("MK", T.MK[:], [[-32, 2], [-64, 2], [-16, 2]], 0, 1)
+    keep("MK", T.MK[:], [[32, 2], [64, 2], [16, 2]], 15, -1)
+    for t, tr, tc in quad:
+        put("WZ", T.WZ[:, 5:8:2, tr:tr + 3, tc:tc + 3], [[-16, 2], [-4, 3], [-1, 3]], -32 * t, 1)
+    for mc in range(2):
+        puts("WY", [(T.WY[:, 5:8:2, 4 * tr + tc:4 * tr + tc + 3:2], [[-16, 2], [-2, 2]], -32 * t - 12 - mc, 16 ** mc) for t, tr, tc in quad]
+             + [(T.WY[:, 5:8:2, 8 + mc::2], [[-16, 2], [32, 4]], -99 - 4 * mc, 1)])
+    put("WP1", T.WP1[:, :, 0:8], [[-16, 8], [-2, 8]], 0, 1)
+    put("WP1", T.WP1[:, :, 0:8], [[-16, 8], [-2, 8]], -1, 16)
     for e in range(3):
         n = 3 if e < 2 else 2
-        put("WLW", T.WLW[:, 0:8 * n], [[-3, n], [-16, 8]], -e, 256 ** e)
-    put("WLK", T.WLK[:], [[-2, 4], [-16, 8]], -8, 128)
-    put("WLK", T.WLK[:], [[-2, 4], [-16, 8]], -9, 1)
-    keep("TE", T.TE[:, 0:128], [[1, 128]], -1, -1)
-    op("pool", [io(T.NT[:], [[16, 64]], 0), io(T.T3[:, 32:34], [[16, 2]], 0), io(T.DIAG[:], [[0, 16], [1, 16]], 0),
-                io(T.TRI[:], [[-16, 2], [0, 4], [1, 32]], 0), io(T.T3[:, 0:16], [[0, 2], [16, 8]], 4096), io(T.T3[:, 16:24], [[0, 4], [16, 2]], 2048),
-                io(T.T3[:, 24:32], [[992, 4], [-16, 2]], -4096), io(T.JT[:], [[0, 4], [1, 32]], -127),
-                io(T.BW[:, 1::2, :], [[0, 128]], 1), io(T.BT[:, 1::2, :], [[0, 128]], 1)], "", "K2 BW BT")
-    for d in peers:
-        send([(d, T.L[:, 1024 * me:1024 * me + 1024], T.S[d], "al")], 16, "S")
-    arrives("al", 48, "La")
-    dma("sp", [(T.KW[16 * e:16 * e + 4, 0:2048], T.KF[16 * e:16 * e + 16, :]) for e in range(8)], "KF La", "KW")
-    for n in ("BW", "BT"):
-        keep(n, T[n][:, 1::2, :], [[-64, 2], [-16, 4], [0, 16]], 0, 1)
-    keep("BW", T.BW[:, 1::2, :], [[64, 2], [16, 4], [0, 16]], 15, -1)
-    keep("BT", T.BT[:, 1::2, :], [[64, 2], [1, 64]], 0, -1)
-    put("BT", T.BT[:, 1::2, :], [[-64, 2], [-1, 64]], 0, -127)
+        put("WD", T.WD[:, 0:8 * n], [[-3, n], [-16, 8]], -e, 256 ** e)
+        put("WE", T.WE[:, 0:16 * n], [[-3, n], [0, 2], [-16, 8]], -e, -256 ** e)
+    put("WD", T.WD[:, 24:32], [[-16, 8]], 0, 1)
+    for e in range(2):
+        v = 128 if e == 0 else 1
+        put("WK", T.WK[:], [[2, 4], [-16, 8]], -14 - e, v)
+        put("WJ", T.WJ[:], [[2, 4], [0, 2], [-16, 8]], -14 - e, -v)
+        puts("WQ", [(T.WQ[:, sh, 7:135:8], [[2, 4], [-32, 2], [-16, 2]], -64 * sh - 14 - e, v) for sh in range(2)])
+
+    def gather(o, win, off, r, w):
+        either(o, win.indirect(off), r, w)
+
+    for a in range(0, 512, 64):
+        gather(T.TT[:, 16 * a:16 * a + 1024], T.G[:, :], T.TL[:, a:a + 64], GALL + " TL TLo", "TT%d" % a)
+    mm([(P[5][:, 64 * (2 * sh + kh):64 * (2 * sh + kh) + 64], T.PM[:, kh, 1 - sl:17 - sl], T.NF[:, 64 * (2 * sh + sl):64 * (2 * sh + sl) + 64],
+         sl == 0, sl == 1) for sh in range(2) for kh in range(2) for sl in range(2)], "PM NF", "P5")
+    mm([(P[4][:, 0:2], T.R0[0:32], T.WF[0:32, :], True, True), (P[4][:, 2:4], T.DM[0:32], T.WF[0:32, :], True, True)], "R0 DM WF", "P4")
+    op("dve", cp(T.PL[:], P[5][:, 0:256]), "", "P5 PL0 PL1")
+    op("dve", cp(T.WG[:], P[4][:, 0:4]), "", "P4 WG")
+    op("dve", [ts(T.WC[:, 8 * f:8 * f + 8], T.MK[:], T.WG[:, f:f + 1], A.mult) for f in range(2)]
+       + [ts(T.WT[:, 2 * f:2 * f + 2], T.SM[:], T.WG[:, 2 + f:3 + f], A.mult) for f in range(2)], "WG MK SM", "WC WT")
+    TALL = " ".join("TT%d" % a for a in range(0, 512, 64))
+
+    keep("BW", T.BW[:], [[-64, 2], [-8, 8], [0, 16]], 0, 1)
+    keep("BW", T.BW[:], [[64, 2], [8, 8], [0, 16]], 7, -1)
+    for kh in range(2):
+        keep("BT", T.BT[:, :, kh, :], [[128, 2], [16, 8], [1, 16]], -kh, -2)
+        put("BT", T.BT[:, :, kh, :], [[128, 2], [16, 8], [1, 16]], -kh, -127, -2)
+        keep("BT", T.BT[:, :, kh, :], [[-64, 2], [-8, 8], [0, 16]], 0, 1)
+    op("pool", [io(T.T3[:, 16:18], [[16, 2]], 0), io(T.JT[:], [[0, 4], [1, 32]], -127), io(T.DIAG[:], [[0, 8], [1, 16]], 0),
+                io(T.DG[:], [[-16, 2], [0, 4], [1, 32]], 0), io(T.T3[:, 0:8], [[16, 8]], 8193), io(T.T3[:, 8:16], [[2048, 4], [16, 2]], 2049),
+                io(T.TP[:, :, 0:8], [[0, 4], [16, 8]], 8192), io(T.TP[:, :, 8:16], [[0, 16], [16, 2]], 2048),
+                io(T.RW[:], [[0, 512]], 0), io(T.B2[:], [[0, 144]], 0)], "", "K2 DG RW B2")
     keep("BO", T.BO[:], [[-16, 8], [0, 16]], 0, 1)
     keep("BO", T.BO[:], [[16, 8], [0, 16]], 15, -1)
-    for t in range(4):
-        tr, tc = 1 - (t >> 1), 1 - (t & 1)
-        put("WD", T.WD[:, 3, :, 2 * tr:2 * tr + 2, 2 * tc:2 * tc + 2], [[-16, 2], [-2, 2], [-1, 2]], -32 * t - 12, 1)
-        for mc in range(2):
-            put("WLT", T.WLT[:, :, :, 4 * tr + tc:4 * tr + tc + 3:2], [[0, 4], [-16, 2], [-2, 2]], -32 * t - 12 - mc, 16 ** mc)
-    for e in range(2):
-        put("WLT", T.WLT[:, :, :, 8 + e::2], [[0, 4], [-16, 2], [32, 4]], -99 - 4 * e, 1)
-        put("WK", T.WK[:, 3, :, e:8:2], [[-16, 2], [32, 4]], -99 - 4 * e, 1)
-    for b in range(4):
-        for e in range(2):
-            put("WLC", T.WLC[:, b, :, :, 0:8], [[0, 4], [-16, 2], [-2, 8]], -32 * b - e, 16 ** e)
+    puts("RW", [(T.RW[:, src, :], [[0, 4], [-32, 2], [-1, 16]], -64 * (src >> 1) - 16 * (src & 1), 1) for src in range(4)])
 
-    def consts2(part):
-        c4 = FF[:, 4:5]
-        if part == 0:
-            op("dve", [ms(T.TE[0:64, 64:128], 0.0), ms(T.RM[:, 0::16], 0.0), ms(T.RB[:, 0::32], 65536.0),
-                       ts(FF[:, 15:16], FF[:, 8:9], 1024.0, A.mult, FF[:, 14:15], A.add),
-                       ts(T.T3[:, 32:34], T.T3[:, 32:34], c4, A.add, 0.5, A.add), ts(T.T3[:, 0:24], T.T3[:, 0:24], c4, A.add),
-                       ts(T.T3[:, 24:32], T.T3[:, 24:32], c4, A.subtract)], "FF FG", "TE RM RB F7 K2")
+    def consts2():
+        c4 = col(4)
+        op("dve", [ts(col(24), col(9), -2193.0, A.mult, 2064.0, A.add), ts(col(25), c4, 64.0, A.mult)], "FF", "FK")
+        op("dve", [ms(T.RM[:], 1.0), ms(T.RB[:], 0.0), ms(T.PZ[:], 0.0),
+                   ts(T.T3[:, 16:18], T.T3[:, 16:18], c4, A.add, 0.5, A.add), ts(T.T3[:, 0:16], T.T3[:, 0:16], c4, A.add),
+                   ts(T.TP[:], T.TP[:], c4, A.add)], "FF", "RM RB PZ K2")
+        op("dve", [ms(T.RM[:, 0::16], 0.0), ms(T.RB[:, 0::32], 65536.0), ts(T.DIAG[:], T.DIAG[:], c4, A.is_equal),
+                   ts(T.TRI[:], T.DG[:], c4, A.is_ge, 16384.0, A.mult), ts(T.B2[:, 15:143:16], T.BO[:, 0::16], col(25), A.mult)],
+           "FF FK DG BO", "RM RB K2 B2")
+
+    def consts3():
+        op("pool", [io(T[n][:], [[0, 896]], 0) for n in ("WA", "WB", "WO")] + [io(T.PF[:], [[0, 132]], 0)], "", "WA WB WO PF")
+        put("PF", T.PF[:, 1::2, :], [[-16, 2], [-1, 8], [32, 4]], -96 - 8 * (me & 1), 1)
+        for src in range(4):
+            b = -64 * (src >> 1) - 16 * (src & 1)
+            puts("WA WB WO", [(T.WA[:, src, 6:8, 0::2], [[-32, 2], [-1, 8]], b, 1), (T.WB[:, src, 6:8, 0::2], [[-32, 2], [-1, 8]], b, -16),
+                              (T.WB[:, src, 6:8, 1::2], [[-32, 2], [-1, 8]], b, 1), (T.WO[:, src, 6:8, 0:4], [[-32, 2], [-2, 4]], b - 8, 128)])
+            put("WO", T.WO[:, src, 6:8, 0:4], [[-32, 2], [-2, 4]], b - 9, 1)
+
+    TO = T.TO
+
+    def tgather(sh, kh, a):
+        c = 128 * sh + 64 * kh + 32 * a
+        gather(TO[:, 16 * c:16 * c + 512], T.TT[:, :], T.PL[:, c:c + 32], TALL + " PL%d" % sh, "TO%d%d%d" % (sh, kh, a))
+
+    def tok(sh, kh):
+        return " TO%d%d0 TO%d%d1" % (sh, kh, sh, kh)
+
+    def win(W, sh, sl):
+        return W[:, 5 - 4 * sh - sl:13 - 4 * sh - sl]
+
+    def zmm(sh, kh):
+        c = 2048 * sh + 1024 * kh
+        for sl in range(2):
+            mm([(P[kh][:, 64 * kl:64 * kl + 64], win(T.WZ, sh, sl), TO[:, c + 8 * sl + kl:c + 1024:16], sh + sl + kl == 0, sh + sl + kl == 9)
+                for kl in range(8)], "WZ" + tok(sh, kh), "P%d" % kh)
+
+    def cond(kh):
+        op("dve", ts(T.C[:, :, kh, :], P[kh][:], 2.0, A.is_equal, 15.0, A.mult), "", "P%d C%d" % (kh, kh))
+
+    def tpart(sh):
+        for a in (0, 8):
+            mm([(P[4][:, 16 * sh + i:128:32], TO[:, 2048 * sh + i:2048 * sh + 2048:16], T.WT[:], sh + i == 0, False) for i in range(a, a + 8)],
+               "WT" + tok(sh, 0) + tok(sh, 1), "P4")
+
+    def cmm():
+        mm([(P[4][:, kl:128:8], T.C[:, kl], T.WC[:], False, kl == 7) for kl in range(8)], "WC C0 C1", "P4")
+        either(T.NM[:], P[4][:, 0:128], "", "P4 NM")
+
+    def ymm(sh, b):
+        for sl in range(2):
+            mm([(P[2 + b][:, 128 * u:128 * u + 128], win(T.WY, sh, sl), TO[:, 2048 * sh + 8 * sl + 4 * b + u:2048 * sh + 2048:16],
+                 sh + sl + u == 0, False) for u in range(4)], "WY" + tok(sh, 0) + tok(sh, 1), "P%d" % (2 + b))
+
+    def ycm(b):
+        mm([(P[2 + b][:], T.WP1[:], T.C[:, 4 * b:4 * b + 4], False, True)], "WP1 C0 C1", "P%d" % (2 + b))
+        either(T.Y[:, 512 * b:512 * b + 512], P[2 + b][:], "", "P%d Y%d" % (2 + b, b))
+
+    def hash1():
+        op("dve", [tt(T.HI[:, :, s, :], T.NM[:, 32 * s:32 * s + 32], T.NM[:, 64 + 32 * s:96 + 32 * s], A.add) for s in range(2)], "NM", "HI")
+        op("dve", [ts(T.HJ[:, 0, :], T.HI[:], 8190, AND), ts(T.HJ[:, 1, :], T.HI[:], 1, AND)], "HI", "HJ")
+        op("dve", [tt(T.HP[:, 0:64], T.HJ[:, 0, :], T.HJ[:, 1, :], A.add), tt(T.HP[:, 64:128], T.HJ[:, 0, :], T.HJ[:, 1, :], A.subtract)], "HJ", "HP")
+        mm([(P[4][:, 128:256], T.HP[:], T.IDF[:], True, True)], "HP IDF", "P4")
+        op("dve", ts(T.HJ[:, 2, :], T.HI[:], 11, SHR, 3, AND), "HI", "HK")
+
+    def hash2():
+        op("dve", ts(T.LL[:], P[4][:, 128:256], col(8), A.add), "FF", "P4 LL")
+
+    OW, AN, KBX, A1, HS = (T.SC[:, j, :] for j in range(5))
+
+    def lookup():
+        for j in range(4):
+            gather(T.R[:, 512 * j:512 * j + 512], T.L[:, 0:8192], T.LL[:, 32 * j:32 * j + 32], LALL + " LL", "R%d" % j)
+        op("dve", ts(OW, T.HJ[:, 2, :], 1.0, A.add, 0.125, A.mult), "HK", "OW")
+
+    def dmm():
+        mm([(P[0][:, kl::8], T.Y[:, 128 * kl:128 * kl + 128], T.WE[:], kl == 0, False) for kl in range(8)], "WE Y0 Y1", "P0")
+        mm([(P[1][:, kl::8], T.Y[:, 128 * kl:128 * kl + 128], T.WJ[:], kl == 0, False) for kl in range(8)], "WJ Y0 Y1", "P1")
+        for sh in range(2):
+            mm([(P[2 + sh][:, 0:128], T.WQ[:, sh, 7 - kl:135 - kl], T.Y[:, 128 * kl:128 * kl + 128], kl == 0, False) for kl in range(8)],
+               "WQ Y0 Y1", "P%d" % (2 + sh))
+        mm([(P[0][:, i::16], T.R[:, i::16], T.WD[:], False, i == 15) for i in range(16)], "R0 R1 R2 R3 WD", "P0")
+        mm([(P[1][:, i::16], T.R[:, i::16], T.WK[:], False, i == 15) for i in range(16)], "R0 R1 R2 R3 WK", "P1")
+
+    def choose():
+        EQ, S0, E0 = T.EQ, T.SEL[:, 0:64], T.EQ[:, 384:448]
+        op("dve", [ts(EQ[:, 0:384], P[0][:, 0:384], 0.0, A.is_equal), ts(EQ[:, 384:512], P[0][:, 384:512], 0.0, A.is_lt)], "", "P0 EQ")
+        op("dve", tt(T.TQ[:], EQ[:, 0:128], EQ[:, 128:256], A.mult), "EQ", "TQ")
+        op("dve", [tt(AN, E0, EQ[:, 448:512], A.max), tt(KBX, T.HJ[:, 1, :], E0, A.is_equal)], "EQ HJ", "AN KBX")
+        op("dve", [tt(S0, T.TQ[:, 0:64], EQ[:, 256:320], A.mult), tt(A1, T.TQ[:, 64:128], EQ[:, 320:384], A.mult)], "TQ EQ", "S0 A1")
+        op("dve", tt(AN, AN, OW, A.mult), "OW", "AN")
+        op("dve", [tt(T.SEL[:, 64:128], A1, S0, A.is_gt), tt(HS, A1, S0, A.max)], "S0 A1", "S1 HS")
+        op("dve", tt(AN, AN, HS, A.subtract), "HS", "AN")
+        op("dve", tt(T.PZ[:, 1:129:2], T.HJ[:, 0, :], KBX, A.add), "HJ KBX", "PZ")
+        op("dve", [ts(T.MO[:, 64 * o:64 * o + 64], AN, 0.125 * (o + 1), A.is_equal) for o in range(4)], "AN", "MO")
+        mm([(P[7][:, 192 * h:192 * h + 192], T.MO[:, 128 * h:128 * h + 128], T.TE[:], True, True) for h in range(2)], "MO TE", "P7")
+        either(T.CK[:], P[7][:, 0:384], "", "P7 CK")
+        op("dve", [tt(T.PR[:, :, :, t, :], P[1][:, 128 * t:128 * t + 128], T.SEL[:], A.mult) for t in range(4)], "S0 S1", "P1 PR")
+        for sh in range(2):
+            mm([(P[2 + sh][:, 0:128], T.PR[:, w, sh], T.IDF[:], False, w == 1) for w in range(2)], "PR IDF", "P%d" % (2 + sh))
+
+    def newlist(rd, sh):
+        if rd == 2:
+            either(T.YN[:, sh, :], P[2 + sh][:, 0:128], "", "P%d YN%d" % (2 + sh, sh))
         else:
-            op("dve", [ts(T.DIAG[:], T.DIAG[:], c4, A.is_equal), ts(T.TRI[:], T.TRI[:], c4, A.is_ge, 4096.0, A.mult),
-                       ts(T.NT[:], T.NT[:], FF[:, 15:16], A.add)], "FF F7", "K2")
-
-    def tgather(rd, q, cc):
-        TO = T["TO%d" % (rd % 2)]
-        gather(q, TO[:, 1024 * cc:1024 * cc + 1024], T.TT[:, :], T.PL[:, 64 * cc:64 * cc + 64], TALL + " PL", "TO%d_%d" % (rd % 2, cc))
-
-    def zmm(rd, cc):
-        TO, be, hf = T["TO%d" % (rd % 2)], cc >> 1, cc & 1
-        mm([(P[be][:, 128 * ka + 64 * hf:128 * ka + 64 * hf + 64], T.WZ[:, 3 - u:7 - u], TO[:, 1024 * cc + 4 * u + ka:1024 * cc + 1024:16],
-             u == 0, u == 3) for ka in range(4) for u in range(4)], "WZ TO%d_%d" % (rd % 2, cc), "P%d" % be)
-
-    def tpart(rd, be):
-        TO = T["TO%d" % (rd % 2)]
-        mm([(P[2 + be][:, 0:288], IDB, T.ZR[:, 0:288], True, False)]
-           + [(P[2 + be][:, k:288:16], TO[:, 2048 * be + k:2048 * be + 2048:16], T.WT[:], False, False) for k in range(16)],
-           "TE ZR WT TO%d_%d TO%d_%d" % (rd % 2, 2 * be, rd % 2, 2 * be + 1), "P%d" % (2 + be))
-
-    def cond(be):
-        op("dve", ts(T.C[:, 512 * be:512 * be + 512], P[be][:], 2.0, A.is_equal, 15.0, A.mult), "", "P%d C%d" % (be, be))
-
-    def cmm(be):
-        mm([(P[2 + be][:, 128 + ka:288:4], T.C[:, 512 * be + 128 * ka:512 * be + 128 * ka + 128], T.WC[:], False, ka == 3)
-            for ka in range(4)], "WC C%d" % be, "P%d" % (2 + be))
-
-    def tevac(be):
-        op("act", act(T.NM[:, :, 32 * be:32 * be + 32], P[2 + be][:, 0:288]), "", "P%d NM%d" % (2 + be, be))
-
-    def hash1(fill):
-        op("dve", tt(T.HI[:], T.NM[:, 7, :], T.NM[:, 8, :], A.add), "NM0 NM1", "HI")
-        fill(0)
-        op("dve", ts(T.HJ[:, 0, :], T.HI[:], 1, SHR, 4095, AND), "HI", "HJ0")
-        op("dve", [ts(T.HJ[:, 1, :], T.HI[:], 1, AND), ts(T.HJ[:, 2, :], T.HI[:], 11, SHR, 3, AND)], "HI", "HJ")
-        op("dve", [cp(T.HP[:, 64 * pi:64 * pi + 64], T.HJ[:, 0, :]) for pi in range(2)], "HJ0", "HP")
-        mm([(P[5][:, 256:384], T.HP[:], T.IDF[:], True, True)], "HP IDF", "P5")
-        fill(1)
-        op("dve", cp(T.LL[:], P[5][:, 256:384]), "", "P5 LL")
-
-    def at(rd, t, c):
-        return t[:, :, c::4] if rd == 2 else t[:, :, 32 * (3 - c):32 * (3 - c) + 32]
-
-    def lookup(rd):
-        op("act", [act(at(rd, T.QM, c), T.NM[:, 3 - c, :]) for c in range(4)], "NM0 NM1", "QM")
-        gather("act", T.R[:, 1024:2048], T.L[:, 0:4096], T.LL[:, 64:128], "Lo La L LL", "R1")
-        gather("dve", T.R[:, 0:1024], T.L[:, 0:4096], T.LL[:, 0:64], "Lo La L LL", "R0")
-        mm([(P[1][:], IDB, T.ZR[:], True, False)]
-           + [(P[1][:, 64 * j:64 * j + 64], T.NEG[:], T.NM[:, 3 - (j >> 1), :], False, False) for j in range(8)], "TE ZR NEG NM0 NM1", "P1")
-        mm([(P[5 + be][:, 0:128], T.QM[:, be, :], T.IDF[:], True, False) for be in range(2)], "QM IDF", "P5 P6")
-        mm([(P[0][:, k:384:16], T.R[:, k::16], T.WLW[:], True, True) for k in range(16)], "R0 R1 WLW", "P0")
-        mm([(P[1][:, k::16], T.R[:, k::16], T.WLK[:], False, k == 15) for k in range(16)], "R0 R1 WLK", "P1")
-        op("dve", [ts(T.BX[:, 0:64], T.HJ[:, 1, :], -1.0, A.mult, 2.0, A.add), ts(T.BX[:, 64:128], T.HJ[:, 1, :], 1.0, A.add),
-                   ts(T.OW[:], T.HJ[:, 2, :], 1.0, A.add), ts(T.HJ[:, 3, :], T.HI[:], 2046, AND)], "HJ HI", "BX OW HJ3")
-
-    def choose(rd):
-        p0, e, o = P[0], P[0][:, 256:320], T.H1[:, 0:64]
-        eq = [p0[:, 0:64], p0[:, 64:128], T.H1[:, 0:64], T.H1[:, 64:128], p0[:, 384:448], p0[:, 448:512]]
-        op("dve", [ts(T.EM[:], p0[:, 256:384], 0.0, A.is_lt)]
-           + [tt(eq[j], p0[:, 64 * j:64 * j + 64], T.NM[:, 4 + (j >> 1), :], A.is_equal) for j in range(6)], "NM0 NM1", "P0 EM H1")
-        op("dve", [tt(T.H2[:], p0[:, 0:128], T.H1[:], A.mult), tt(p0[:, 128:256], p0[:, 384:512], T.BX[:], A.mult)], "BX H1", "P0 H2")
-        op("dve", tt(T.EM[:], T.EM[:], T.BX[:], A.mult), "BX", "EM")
-        op("dve", [tt(e, p0[:, 128:192], T.H2[:, 0:64], A.mult), tt(o, p0[:, 192:256], T.H2[:, 64:128], A.mult)], "H2", "P0 H1")
-        op("dve", tt(T.AN[:], T.EM[:, 64:128], T.EM[:, 0:64], A.not_equal), "EM", "AN")
-        op("dve", [tt(T.SEL[:, 0:64], e, o, A.is_gt), tt(T.SEL[:, 64:128], e, o, A.is_lt), tt(T.MS[:], e, o, A.is_equal)], "H1", "P0 SEL MS")
-        op("dve", tt(T.OW[:], T.OW[:], T.AN[:], A.mult), "AN", "OW")
-        op("dve", [tt(at(rd, T.PR, c), P[1][:, 128 * c:128 * c + 128], T.SEL[:], A.mult) for c in range(4)], "SEL", "P1 PR")
-        for be in range(2):
-            mm([(P[5 + be][:, 0:128], T.PR[:, 2 * pi + be, :], T.IDF[:], False, pi == 1) for pi in range(2)], "PR IDF", "P%d" % (5 + be))
-        op("dve", tt(T.OW[:], T.OW[:], T.MS[:], A.mult), "MS", "OW")
-        op("dve", tt(T.AN[:], T.EM[:, 64:128], T.EM[:, 0:64], A.is_gt), "EM", "AN")
-        op("dve", [ts(T.MO[:, 64 * j:64 * j + 64], T.OW[:], float(j + 1), A.is_equal) for j in range(4)], "OW", "MO")
-        mm([(P[7][:, 256 * h:256 * h + 256], T.MO[:, 128 * h:128 * h + 128], T.TE[:], True, True) for h in range(2)], "MO TE", "P7")
-        op("dve", tt(T.PZ[:, 64:128], T.AN[:], T.HJ[:, 3, :], A.add), "AN HJ3", "PZ")
-
-    def newlist(rd):
-        for be in range(2):
-            if rd == 2:
-                op("dve", cp(T.YN[:, 128 * be:128 * be + 128], P[5 + be][:, 0:128]), "", "P%d YN%d" % (5 + be, be))
-            else:
-                op("dve", cp(T.PL[:, 128 * be:128 * be + 128], P[5 + be][:, 0:128]), "", "P%d PL" % (5 + be))
+            op("dve", cp(T.PL[:, 128 * sh:128 * sh + 128], P[2 + sh][:, 0:128]), "", "P%d PL%d" % (2 + sh, sh))
 
     def claim2():
-        op("act", act(T.CK[:], P[7][:]), "", "P7 CK")
-
-        def term(b, o, hf, W, x, start, stop):
-            k = 1 + 2 * (o & 1) - hf
-            c = 256 * (o >> 1) + 128 * x + 64 * hf
-            return (P[b][:, 64 * o:64 * o + 64], W[:, k:k + 2, :], T.CK[:, c:c + 64], start, stop)
-        mm([term(6, o, hf, T.BW, 0, hf == 0, hf == 1) for o in range(4) for hf in range(2)], "BW CK", "P6")
-        mm([term(4, o, j >> 1, (T.BW, T.BT)[j & 1], j & 1, j == 0, j == 3) for o in range(4) for j in range(4)]
-           + [(P[4][:, 256:320], T.PZ[:, 64 - 64 * h:192 - 64 * h], T.IDF[:, 64 * h:64 * h + 64], h == 0, h == 1)
-              for h in range(2)], "BW BT CK PZ IDF", "P4")
-        op("act", [act(T.LR[:, 64 * j:64 * j + 64], P[6][:, 64 * (j >> 1):64 * (j >> 1) + 64], F.Sign, bias=T.T3[:, 32 + (j & 1):33 + (j & 1)],
-                       scale=-1.0, accum_out=T.CNT[:, j:j + 1]) for j in range(8)], "K2", "P6 LR CNT")
-        op("act", [act(T.UT[:, 0:256], P[4][:, 0:256]), act(T.UT[:, 256:320], P[4][:, 256:320], F.Copy, bias=1.0)], "", "P4 UT")
-        mm([(P[7][:, 0:256], T.IDF[:], T.TRI[:], True, False)], "IDF K2", "P7")
+        mm([(P[6][:, 64 * o:64 * o + 64], T.BW[:, o & 1], T.CK[:, 192 * (o >> 1):192 * (o >> 1) + 64], True, True) for o in range(4)], "BW CK", "P6")
+        mm([(P[5][:, 64 * o:64 * o + 64], T.BW[:, o & 1] if j == 0 else T.BT[:, o & 1, j - 1],
+             T.CK[:, 192 * (o >> 1) + 64 * j:192 * (o >> 1) + 64 * j + 64], j == 0, j == 2) for o in range(4) for j in range(3)]
+           + [(P[5][:, 256:320], T.PZ[:, 1 - kh:129 - kh], T.IDF[:, 64 * kh:64 * kh + 64], kh == 0, kh == 1) for kh in range(2)],
+           "BW BT CK PZ IDF", "P5")
+        op("act", [act(T.SG[:, 64 * j:64 * j + 64], P[6][:, 64 * (j >> 1):64 * (j >> 1) + 64], F.Sign, bias=T.T3[:, 16 + (j & 1):17 + (j & 1)],
+                       scale=-1.0, accum_out=T.CNT[:, j:j + 1]) for j in range(8)], "K2", "P6 SG CNT")
+        op("act", [act(T.UT[:, 0:256], P[5][:, 0:256]), act(T.UT[:, 256:320], P[5][:, 256:320], F.Copy, bias=1.0)], "", "P5 UT")
+        mm([(P[7][:, 0:256], IDB, T.TRI[:], True, False)], "IDB K2", "P7")
 
     def claim3():
-        op("dve", [ts(T.CL[:, 2 * o:2 * o + 2], T.CNT[:, 2 * o:2 * o + 2], 0.5, A.mult, 31.0 + 64 * o, A.add) for o in range(4)]
-           + [ts(T.CL[:, 8:16], T.CNT[:], 0.5, A.mult, 31.0, A.add)], "CNT", "CL")
+        op("dve", [ts(T.CL[:, 2 * o:2 * o + 2], T.CNT[:, 2 * o:2 * o + 2], 0.5, A.mult, 31.0 + 64 * o, A.add) for o in range(4)], "CNT", "CL")
+        op("dve", [ts(T.CL[:, 8:16], T.CNT[:], 0.5, A.mult, 31.0, A.add), ts(T.CF[:], T.CNT[:], 0.5, A.mult, 31.0, A.add)], "CNT", "CM CF")
         op("dve", tt(T.MF[:], T.UT[:, 0:256].indirect(T.CL[:, 0:8]), T.JT[:], A.is_equal), "UT CL K2", "MF")
-        op("dve", [tt(T.VN[:, 0:128], T.UT[:, 256:320].indirect(T.CL[:, 8:16]), T.MF[:], A.mult),
-                   tt(T.VN[:, 128:256], T.NT[:, :].indirect(T.CL[:, 8:16]), T.MF[:], A.mult)], "UT MF CL K2", "VN")
-        mm([(P[6][:, 0:256], T.BO[:], T.VN[:], True, True)], "BO VN", "P6")
-        mm([(P[7][:, 128 * h:128 * h + 128], T.BO[:], T.VN[:, 0:128], False, h == 1) for h in range(2)], "BO VN", "P7")
+        mm([(P[6][:, 0:8], T.IDF[:], T.CF[:], True, False)], "IDF CF", "P6")
+        mm([(P[6][:, 0:8], T.B2[:, 15 - i:143 - i], T.MF[:, i::16], False, i == 15) for i in range(16)], "B2 MF", "P6")
+        op("dve", tt(T.VN[:], T.UT[:, 256:320].indirect(T.CL[:, 8:16]), T.MF[:], A.mult), "UT MF CM", "VN")
+        mm([(P[5][:, 0:128], T.BO[:], T.VN[:], True, True)], "BO VN", "P5")
+        mm([(P[7][:, 128 * h:128 * h + 128], T.BO[:], T.VN[:], False, h == 1) for h in range(2)], "BO VN", "P7")
 
-    def rep(n, rhs, r):
-        ks = [2 * (src & 1) + (src >> 1) for src in range(4)]
-        mm([(P[6][:, n * src:n * src + n], T.RW[:, k, :], rhs, True, True) for src, k in enumerate(ks)], "RW " + r, "P6")
-
-    def claim4():
-        op("dve", tt(T.DG[:], P[6][:, 0:256], T.DIAG[:], A.mult), "K2", "P6 DG")
-        op("dve", scan(T.DS[:], T.RM[:], T.DG[:], A.mult, A.add), "RM DG", "DS")
-        rep(8, T.DS[:, 143::16], "DS")
+    def claim4(rd):
+        op("dve", cp(T.NL[:], P[6][:, 0:8]), "", "P6 NL")
+        mm([(P[6][:, 0:64], T.IDF[:], T.TP[:], True, False)], "IDF K2", "P6")
+        gather(T.YG[:, rd, :], T.Y[:, :], T.NL[:, :], "NL Y0 Y1", "YG%d" % rd)
+        op("dve", tt(T.DG[:, 0:128], P[5][:, 0:128], T.DIAG[:], A.mult), "K2", "P5 DG")
+        op("dve", scan(T.DS[:], T.RM[:], T.DG[:, 0:128], A.mult, A.add), "RM DG", "DS")
         op("act", [act(T.AB[:, 32 * j:32 * j + 32], P[7][:, 128 * (j & 1) + 32 * (j >> 1):128 * (j & 1) + 32 * (j >> 1) + 32], F.Abs,
                        bias=T.DS[:, 16 * j + 15:16 * j + 16], scale=-1.0) for j in range(8)], "DS", "P7 AB")
         key, M3 = T.DS[:, 15:128:16], T.M3
-        op("dve", ts(T.I8[:, 0, :], key, -1.0, A.add), "DS", "I8")
-        op("dve", [ts(T.I8[:, 1, :], T.I8[:, 0, :], 1, SHR), ts(T.I8[:, 2, :], T.I8[:, 0, :], 1, AND),
-                   tt(M3[:, 40:48], T.I8[:, 0, :], T.T3[:, 16:24], A.subtract)], "I8 K2", "I9 D3")
-        op("dve", cp(T.NL[:], P[6][:, 0:32]), "", "P6 NL")
-        op("dve", [tt(M3[:, 24 + 8 * j:32 + 8 * j], T.I8[:, 1, :], T.T3[:, 24:32], A.add) for j in range(2)], "I9 K2", "D4")
+        op("dve", [tt(M3[:, 0:8], key, T.T3[:, 0:8], A.subtract), tt(M3[:, 8:16], key, T.T3[:, 8:16], A.subtract),
+                   ts(M3[:, 16:24], key, 1.0, A.min)], "DS K2", "D3")
+
+    def lrec(rd):
+        mm([(P[5][:, 128 * s:128 * s + 128], T.RB16[:, s, :], T.YG[:, rd, :], True, True) for s in range(4)], "RB16 YG%d" % rd, "P5")
+        either(T.LR[:], P[5][:], "", "P5 LR")
 
     def claim5(rd):
-        key, M3 = T.DS[:, 15:128:16], T.M3
+        M3 = T.M3
         op("dve", scan(T.DG[:], T.RB[:], T.AB[:], A.add, A.min), "RB AB", "DG")
-        op("dve", tt(M3[:, 16:24], T.DG[:, 31::32], key, A.min), "DG DS", "M3")
-        op("dve", ts(M3[:, 16:24], M3[:, 16:24], 0.5, A.is_gt), "", "M3")
-        if rd < 2:
-            op("dve", [tt(M3[:, 8:16], M3[:, 16:24], T.I8[:, 2, :], A.mult), tt(M3[:, 0:8], M3[:, 16:24], T.I8[:, 2, :], A.is_gt)], "I9", "M3")
-        a = 0 if rd < 2 else 16
-        op("dve", tt(M3[:, a:24], M3[:, a:24], M3[:, 24 + a:48], A.mult), "D3 D4", "M3")
-        op("dve", tt(M3[:, 48 + a:72], M3[:, a:24], T.T3[:, a:24], A.add), "M3 K2", "WR")
-        rep(24 - a, M3[:, 48 + a:72], "WR")
+        op("dve", tt(M3[:, 24:32], T.DG[:, 31::32], M3[:, 16:24], A.min), "DG D3", "M3")
+        op("dve", [tt(M3[:, 32 + 8 * j:40 + 8 * j], M3[:, 24:32], M3[:, 8 * j:8 * j + 8], A.mult) for j in range(2)], "M3 D3", "WR")
+        mm([(P[6][:, 16 * s:16 * s + 16], T.RW[:, s, :], M3[:, 32:48], False, s == 3) for s in range(4)], "RW WR", "P6")
+        op("dve", cp(T.OO[:, rd], P[6][:, 0:64]), "", "P6 OO%d" % rd)
 
-    def claim5e(rd):
-        if rd == 2:
-            op("dve", cp(T.OO[:, rd], P[6][:, 0:32]), "", "P6 OO%d" % rd)
-            return
-        op("dve", cp(T.RL[:], P[6][:, 0:96]), "", "P6 RL")
-        op("dve", [cp(T.LOF[64 * h:64 * h + 64, :], T.RL[64 * h:64 * h + 64, :, h, :]) for h in range(2)] + [cp(T.OO[:, rd], T.RL[:, :, 2, :])],
-           "RL", "LOF OO%d" % rd)
+    def lscatter(rd, src):
+        op("dve", cp(T.L[:, :].indirect(T.OO[:, rd, src, 0:8]), T.LR[:, 128 * src:128 * src + 128]), "OO%d LR L0 L1 L2 L3" % rd, "L")
 
-    def rec1(rd):
-        n = rd % 2
-        gather("act", T.TC[:], T["TO%d" % n][:, :], T.NL[:, :], "NL " + " ".join("TO%d_%d" % (n, c) for c in range(4)), "TC")
+    def post_rec(rd):
+        send([(d, T.LB[:, rd, me ^ d, :], T.YG[:, rd, 32 * d:32 * d + 32], "ar%d" % rd) for d in peers], 4, "YG%d" % rd)
+        arrives("ar%d" % rd, 12, "LB%d" % rd)
 
-    def rec1m():
-        mm([(P[7][:, 0:128], T.WZ[:, 3 - u:7 - u], T.TC[:, 128 * u:128 * u + 128], u == 0, u == 3) for u in range(4)], "WZ TC", "P7")
-
-    def rec2(rd):
-        op("dve", ts(T.CC[:], P[7][:, 0:128], 2.0, A.is_equal, 15.0, A.mult), "", "P7 CC")
-        if rd < 2:
-            mm([m for u in range(4) for m in
-                [(P[4][:, 128 * u:128 * u + 128], T.WLT[:], T.TC[:, 128 * u:128 * u + 128], True, False),
-                 (P[4][:, 128 * u:128 * u + 128], T.WLC[:, u], T.CC[:], False, True)]], "WLT WLC TC CC", "P4")
-            op("act", act(T.LR[:], P[4][:]), "", "P4 LR")
-
-    def rec3(rd):
-        mm([(P[7][:, 128:256], T.WK[:, 3 - u:7 - u], T.TC[:, 128 * u:128 * u + 128], u == 0, u == 3) for u in range(4)]
-           + [(P[7][:, 0:128], T.WD[:, 3 - u:7 - u], T.TC[:, 128 * u:128 * u + 128], u == 0, False) for u in range(4)]
-           + [(P[7][:, 0:128], IDB, T.CC[:], False, True)], "WD WK TE TC CC", "P7")
-        op("act", [act(T.SO[:, rd, :, 32 * j:32 * j + 32], P[7][:, 128 * j:128 * j + 128]) for j in range(2)], "", "P7 SO%d" % rd)
-
-    def lscatter(src):
-        op("dve", cp(T.L[:, :].indirect(T.LOF[:, 8 * src:8 * src + 8]), T.LR[:, 128 * src:128 * src + 128]), "LOF LR Lo La", "L")
-
-    def post(rd):
-        send([(d, T.LB[:, rd, me, :], T.SO[:, rd, d, :], "ao%d" % rd) for d in peers]
-             + [(d, T.LO[:, rd, me], T.OO[:, rd], "ao%d" % rd) for d in peers], 2, "SO%d OO%d" % (rd, rd))
-        arrives("ao%d" % rd, 12, "LB%d" % rd)
+    def post_off(rd):
+        send([(d, T.LO[:, rd, me], T.OO[:, rd], "ao%d" % rd) for d in peers], 4, "OO%d" % rd)
+        arrives("ao%d" % rd, 12, "LO%d" % rd)
 
     def own1(rd):
-        for b, j, W in ((2, 0, lambda k, d: T.IW[:, k, 96 - 32 * d:224 - 32 * d]), (3, 1, lambda k, d: T.KWM[:, k, 3 - d:7 - d])):
-            mm([(P[b][:, 32 * s:32 * s + 32], W(s, d), (T.SO if d == me else T.LB)[:, rd, d, 32 * j:32 * j + 32], d == 0, d == 3)
-                for s in range(4) for d in range(4)], "IW KWM SO%d LB%d" % (rd, rd), "P%d" % b)
-        op("act", act(T.VC[:], P[2][:, 0:128]), "", "P2 VC")
-        op("act", act(T.VK[:], P[3][:, 0:128]), "", "P3 VK")
+        own = T.YG[:, rd, 32 * me:32 * me + 32]
+        op("act", [act(T.UH[:, 0:32], own, F.Copy, scale=0.0625, bias=128.53125),
+                   act(T.UH[:, 32:128], T.LB[:, rd, 1:4, :], F.Copy, scale=0.0625, bias=128.53125)], "YG%d LB%d" % (rd, rd), "UH")
+
+        def rec(d):
+            return own if d == me else T.LB[:, rd, me ^ d, :]
+        a, b = (4, 4) if rd < 2 else (2, 3)
+        for s in range(4):
+            mm([(P[a][:, 32 * s:32 * s + 32], W[:, s, 6 - 2 * d:14 - 2 * d], rec(d) if j == 0 else T.UH[:, 32 * (me ^ d):32 * (me ^ d) + 32],
+                 d + j == 0, d + j == 4) for j, W in enumerate((T.WA, T.WB)) for d in range(4)], "WA WB UH YG%d LB%d" % (rd, rd), "P%d" % a)
+        for h in range(2):
+            mm([(P[b][:, 128 + 32 * s:160 + 32 * s], T.WO[:, s, 6 - 2 * d:14 - 2 * d], rec(d), d == 0, d == 3) for s in (2 * h, 2 * h + 1) for d in range(4)],
+               "WO YG%d LB%d" % (rd, rd), "P%d" % b)
+        op("act", act(T.VC[:, rd, :], P[a][:, 0:128], bias=col(24)), "FK", "P%d VC%d" % (a, rd))
+        either(T.VK[:, rd, :], P[b][:, 128:256], "", "P%d VK%d" % (b, rd))
 
     def own2(rd):
-        op("dve", [cp(T.OL[32 * d:32 * d + 32, :], T.OO[32 * d:32 * d + 32, rd, :, 2 * me:2 * me + 2] if d == me
-                      else T.LO[32 * d:32 * d + 32, rd, d, :, 2 * me:2 * me + 2]) for d in range(4)], "OO%d LB%d" % (rd, rd), "OL")
+        a = 8 + 2 * me
+        op("dve", [cp(T.OL[32 * d:32 * d + 32, rd, :], T.OO[32 * d:32 * d + 32, rd, :, a:a + 2] if d == me
+                      else T.LO[32 * d:32 * d + 32, rd, d, :, a:a + 2]) for d in range(4)], "OO%d LO%d" % (rd, rd), "OL%d" % rd)
 
         def sc(W, Vv, s, k):
-            op("dve", cp(W[:, :].indirect(T.OL[:, 2 * s:2 * s + 2]), Vv[:, 32 * s:32 * s + 32]), "OL V" + k[0], k)
-        order = [(0, 3), (1, 3), (0, 2), (1, 2), (0, 1), (1, 1), (0, 0), (1, 0)] if rd < 2 else [(0, 3), (0, 2), (0, 1), (1, 3), (0, 0), (1, 2), (1, 1), (1, 0)]
-        for w, s in order:
-            sc((T.CW, T.KW)[w], (T.VC, T.VK)[w], s, ("CW", "KW")[w])
-            if rd == 2 and (w, s) == (0, 0):
-                dma("sp", [(T.ycells[:], T.CW[:, 0:2048])], "CW", "yc")
+            op("dve", cp(W[:, :].indirect(T.OL[:, rd, 2 * s:2 * s + 2]), Vv[:, rd, 32 * s:32 * s + 32]), "OL%d V%s%d" % (rd, k[0], rd), k)
+        for s in (3, 2, 1, 0):
+            for w in range(2):
+                sc((T.CW, T.KW)[w], (T.VC, T.VK)[w], s, ("CW", "KW")[w])
         if rd == 2:
+            dma("sp", [(T.ycells[:], T.CW[:, 0:2048])], "CW", "yc")
             dma("act", [(T.ykids[4 * e:4 * e + 4, :], T.KW[16 * e:16 * e + 4, 0:2048]) for e in range(4)], "KW", "yk")
             dma("sp", [(T.ykids[4 * e:4 * e + 4, :], T.KW[16 * e:16 * e + 4, 0:2048]) for e in range(4, 8)], "KW", "yl")
 
-    for cc in range(4):
-        tgather(0, "act" if cc & 1 else "dve", cc)
-    zmm(0, 0)
-    zmm(0, 1)
-    tpart(0, 0)
-    cond(0)
-    zmm(0, 2)
-    zmm(0, 3)
-    cmm(0)
-    zero("IW")
-    cond(1)
-    zero("KWM")
-    tevac(0)
-    tpart(0, 1)
-    cmm(1)
-    tevac(1)
-    hash1(consts2)
-    for b in range(4):
-        put("IW", T.IW[:, b, 96:128], [[-1, 32]], -32 * b, 1)
-        for e in range(2):
-            put("KWM", T.KWM[:, b, 3, :, 0:4], [[-16, 2], [-2, 4]], -32 * b - e, 128 if e == 0 else 1)
-    for rd in range(3):
-        lookup(rd)
-        choose(rd)
-        newlist(rd)
-        if rd == 2:
-            send([(d, T.YL[:, 64 * me:64 * me + 64], T.YN[:, 64 * d:64 * d + 64], "ay") for d in peers], 4, "YN0 YN1")
-            arrives("ay", 12, "YL")
-            dma("sp", [(T.ynodes[32 * d:32 * d + 32, :], (T.YN if d == me else T.YL)[:, 64 * d:64 * d + 64]) for d in range(4)], "YN0 YN1 YL", "yn")
-            claim2()
-            own1(0)
-            claim3()
-            own2(0)
-            claim4()
-            rec1(rd)
-            rec1m()
-            claim5(rd)
-            rec2(rd)
-            rec3(rd)
-            claim5e(rd)
-            post(rd)
-            own1(1)
-            own2(1)
-            own1(2)
-            own2(2)
-            break
-        tgather(rd + 1, "dve", 0)
-        claim2()
-        zmm(rd + 1, 0)
-        tgather(rd + 1, "act", 1)
-        tgather(rd + 1, "act", 3)
-        claim3()
-        tgather(rd + 1, "dve", 2)
-        zmm(rd + 1, 1)
-        claim4()
-        rec1(rd)
+    def ynodes():
+        mm([(P[0][:, 64 * d:64 * d + 64], T.PF[:, 1 - kh:33 - kh],
+             T.YN[:, me >> 1, 64 * kh:64 * kh + 64] if d == me else T.YL[:, d, 64 * kh:64 * kh + 64], kh == 0, kh == 1)
+            for d in range(4) for kh in range(2)], "PF YN0 YN1 YL", "P0")
+        either(T.YF[:], P[0][:, 0:256], "", "P0 YF")
+        dma("sp", [(T.ynodes[32 * d:32 * d + 32, :], T.YF[:, 64 * d:64 * d + 64]) for d in range(4)], "YF", "yn")
+
+    def part_a():
+        for sh in range(2):
+            for kh in range(2):
+                tgather(sh, kh, 0)
+                tgather(sh, kh, 1)
+        zmm(0, 0)
+        zmm(0, 1)
+        tpart(0)
+        ymm(0, 0)
+        ymm(0, 1)
+        zmm(1, 0)
+        zmm(1, 1)
         cond(0)
-        zmm(rd + 1, 2)
-        zmm(rd + 1, 3)
-        rec1m()
-        claim5(rd)
-        rec2(rd)
+        tpart(1)
         cond(1)
-        tpart(rd + 1, 0)
-        cmm(0)
-        tevac(0)
-        tpart(rd + 1, 1)
-        cmm(1)
-        tevac(1)
-        claim5e(rd)
-        lscatter(3)
-        lscatter(2)
-        rec3(rd)
-        post(rd)
-        hash1(lambda j: lscatter(1 - j))
+        cmm()
+        ymm(1, 0)
+        ycm(0)
+        hash1()
+        ymm(1, 1)
+        ycm(1)
+        hash2()
+
+    consts2()
+    either(T.RB16[:], T.RW[:], "RW", "RB16")
+    consts3()
+    part_a()
+    for rd in range(3):
+        lookup()
+        dmm()
+        choose()
+        newlist(rd, 0)
+        newlist(rd, 1)
+        claim2()
+        claim3()
+        claim4(rd)
+        post_rec(rd)
+        if rd < 2:
+            lrec(rd)
+        claim5(rd)
+        post_off(rd)
+        if rd < 2:
+            for src in (3, 2, 1, 0):
+                lscatter(rd, src)
+            part_a()
+    send([(d, T.YL[:, me, :], T.YN[:, d >> 1, :], "ay") for d in peers], 4, "YN0 YN1")
+    arrives("ay", 12, "YL")
+    ynodes()
+    for rd in range(3):
+        own1(rd)
+        own2(rd)
+
+    for n in ORDER or range(1, len(prog) + 1):
+        rec = prog[abs(n) - 1]
+        kind, q, pay, r, w = rec
+        if kind == "op":
+            if q == "x":
+                q, pay = ("act", pay[1]) if n < 0 else ("dve", pay[0])
+            do_op(q, pay, r, w)
+        elif kind == "dma":
+            do_dma(q, pay, r, w)
+        elif kind == "send":
+            do_send(pay[0], pay[1], r)
+        else:
+            done(pay[0], pay[1], [], w)
     for s, v in total.items():
         if seen["pool"].get(s, 0) < v:
             g.wait_ge(T.sem[s], v)

@@ -13,23 +13,23 @@ def _decl(dt, **kw):
 _decl(b16, XS=[4, 512], X=[2048], H=[4, 512], C0=[4, 128], SH=[8, 4, 4], SX=[8, 4, 4], WH=[4, 128], WX=[4, 128],
       G=[8192], TT=[8192], TO=[4096], L=[8320], LS=[4, 512], CW=[2080], KH=[512], KLO=[512],
       WZ=[13, 4, 4], WY=[13, 16], WT=[4], WC=[16], MK=[8], SM=[2], DM=[8, 16], R0=[2, 2, 2, 16], WF=[2], WD=[32], WK=[32], WE=[64], WJ=[64],
-      WQ=[2, 136], RP=[256], B2=[144], TE=[192], IDB=[128], TRI=[256], BW=[2, 128], BT=[2, 2, 128], WP1=[8, 16], WLX=[128], WKD=[8, 128],
-      RB16=[4, 128], WA=[4, 14, 16], WB=[4, 14, 16], WO=[4, 14, 16],
-      C=[8, 2, 64], Y=[1024], R=[2048], EQ=[512], TQ=[128], SEL=[128], SC=[6, 64], MO=[256], CK=[384], MF=[128], SG=[512],
+      WQ=[2, 136], RP=[256], B2=[144], TE=[192], IDB=[128], ONE=[128], TRI=[384], BW=[2, 128], BT=[2, 2, 128], WP1=[8, 16], WLX=[128],
+      WKD=[8, 128], RB16=[4, 128], WA=[4, 14, 16], WB=[4, 14, 16], WO=[4, 14, 16],
+      C=[8, 2, 64], Y=[1024], R=[2048], EQ=[512], TQ=[128], SEL=[128], SC=[6, 64], MO=[256], FO=[4, 64], CK=[384], MF=[128], SG=[512],
       YG=[3, 128], LR=[512], VC=[3, 128], LB=[3, 4, 32], UH=[128])
 _decl(f32, RT=[8, 4, 4], CT=[8, 4, 4], FF=[40], J16=[20], GB=[16], KB=[4, 4, 2, 16], KT=[4, 4, 32], NF=[256], MI=[128],
-      KF=[512], KW=[2080], IDF=[128], PM=[2, 17, 8], PF=[33, 4], RW=[4, 128], BO=[128], WG=[4], JT=[128], DIAG=[128], RM=[128],
-      RB=[256], T3=[18], TP=[4, 16], NM=[128], HP=[128], PR=[2, 2, 4, 32], PZ=[130], UT=[320], CNT=[8], CF=[8], VN=[128],
-      DG=[256], DS=[128], AB=[256], M3=[48], VK=[3, 128], YN=[2, 128], YL=[4, 128], YF=[256])
-_decl(i32, PI=[1], FI=[16], KA=[4, 2, 64], NS=[4, 64], NI=[256], KN=[512], WI=[4], HI=[2, 2, 16], HJ=[3, 64])
-_decl(u16, KL=[512], TL=[512], PL=[256], LL=[128], CL=[16], NL=[8], OO=[3, 4, 16], LO=[3, 4, 4, 16], OL=[3, 8])
+      KF=[512], KW=[2080], IDF=[128], PM=[2, 17, 8], PF=[33, 4], RW=[4, 128], BO=[128], WG=[4], JT=[32], RM=[128],
+      RB=[256], T3=[18], TP=[3, 32], NM=[128], HP=[128], PR=[2, 2, 4, 32], PZ=[130], UT=[320], CNT=[8], CF=[8], VN=[128],
+      DG=[384], DS=[128], AB=[256], M3=[48], VK=[3, 128], YN=[2, 128], YL=[4, 128], YF=[256])
+_decl(i32, PI=[1], FI=[20], KA=[4, 2, 64], NS=[4, 64], NI=[256], KN=[512], WI=[4], HI=[2, 2, 16], HJ=[2, 64])
+_decl(u16, KL=[512], TL=[512], PL=[256], LL=[128], CL=[8], NL=[8], LF=[32], OO=[3, 4, 8], LO=[3, 4, 4, 8], OL=[3, 8])
 SCRATCH["S"] = ("dram", [4, 128, 512], b16)
 for _b in range(8):
     SCRATCH["P%d" % _b] = ("psum", [128, 512], f32)
 SEMAPHORES = (["pe", "dve", "act", "pool", "ax0", "ax1", "ax2", "ax3", "ak", "an", "al0", "al1", "al2", "al3",
-               "ao0", "ao1", "ao2", "ar0", "ar1", "ar2", "ay"] + ["d%d" % i for i in range(48)])
+               "ao0", "ao1", "ao2", "ar0", "ar1", "ar2", "ay"] + ["d%d" % i for i in range(52)])
 
-ORDER = [7,8,1,6,4,3,14,24,9,2,10,85,5,23,11,15,12,22,-29,-27,-28,16,30,32,37,54,-34,-33,53,62,56,55,57,40,58,41,73,43,13,75,39,36,42,77,44,93,-76,18,71,-74,83,59,47,-72,170,122,35,20,78,51,38,25,65,45,17,49,139,91,-46,128,61,19,94,-26,-50,52,98,158,-48,84,89,63,101,-31,141,21,92,96,133,100,167,102,111,-97,68,103,66,108,135,112,104,70,64,119,60,-105,95,124,106,-99,121,110,120,115,-109,67,117,-116,168,113,-107,118,69,86,132,90,153,125,114,129,151,-146,154,142,79,160,147,-150,123,140,161,162,145,-152,80,87,126,127,81,-148,137,149,155,130,131,166,184,-185,82,88,156,-187,186,192,193,-189,157,194,188,198,196,-191,197,190,195,163,200,199,202,169,203,204,206,205,207,209,208,212,171,134,210,164,201,213,-211,-173,216,144,217,214,218,221,222,136,-215,220,223,143,230,219,138,-224,165,225,-229,228,234,159,231,226,-227,233,174,235,232,237,236,238,239,240,241,242,243,245,248,246,-247,244,249,172,253,254,251,255,288,257,250,256,258,-291,259,260,176,261,252,262,263,-289,290,264,177,265,-293,178,269,266,302,270,268,298,292,296,271,273,275,300,-294,179,299,272,175,277,267,180,297,278,301,-295,279,276,306,307,181,280,310,311,281,308,284,282,274,309,303,182,313,316,312,285,314,317,183,-315,318,320,304,286,-319,305,325,321,324,326,322,327,287,283,323,-328,329,332,-331,335,336,334,-333,330,339,340,341,338,342,343,337,344,345,346,347,349,352,350,348,351,353,357,358,355,359,392,354,360,362,-393,361,363,364,365,356,366,367,-394,395,368,369,-399,373,370,404,398,408,402,-397,403,374,396,400,412,375,405,413,376,495,401,-372,381,410,382,377,378,411,383,417,371,379,384,414,-380,415,385,416,388,386,418,406,-419,407,424,420,389,409,429,425,390,430,431,426,421,-432,391,422,427,-423,387,433,428,436,-437,441,439,434,-435,496,442,438,443,497,445,440,498,446,444,447,448,449,450,456,451,457,453,454,459,458,452,-455,522,460,461,465,490,462,463,499,464,466,500,467,501,468,469,504,502,470,471,-503,513,505,472,506,474,514,477,-476,473,507,478,481,480,475,515,479,516,491,492,483,484,485,486,493,509,494,517,508,487,518,510,512,488,519,511,482,531,536,520,532,-521,523,537,524,533,-539,525,534,526,527,535,529,538,528,530,489,540,541,543,545,547,542,549,544,546,548,551,550]
+ORDER = [1,2,10,11,21,12,3,7,18,16,8,14,9,4,13,22,15,-19,17,38,28,32,47,29,-50,65,140,30,51,6,24,31,20,-36,141,52,-86,42,46,43,53,149,5,54,151,55,33,23,64,155,48,142,62,49,143,25,83,60,187,82,-44,56,63,153,-61,34,26,58,70,-57,188,93,41,84,138,-59,85,89,139,66,-94,76,91,35,67,81,90,102,27,-39,72,107,-103,78,98,100,-92,74,148,96,156,-108,37,77,40,75,79,101,104,144,-97,99,111,69,-105,109,68,137,-186,113,-110,87,145,115,114,-112,80,121,88,-116,106,146,95,117,174,165,-122,147,158,-161,119,129,178,123,166,179,169,-164,150,159,130,134,170,152,163,154,-118,-167,125,162,184,-168,124,126,171,131,120,-216,215,127,213,-214,223,224,132,218,-217,227,229,221,128,220,-219,222,228,231,172,232,175,185,233,133,176,234,173,-193,230,238,225,177,226,-45,235,236,-194,157,237,-191,71,-192,241,180,239,195,200,250,181,-240,251,-196,245,252,190,246,242,73,-253,182,247,243,201,248,-244,160,135,249,254,259,189,-255,256,260,263,266,267,268,257,-258,269,183,-202,261,197,262,264,270,-198,205,265,203,291,-271,272,-199,274,273,276,206,136,275,282,207,277,283,278,279,208,285,280,209,284,-326,281,286,288,327,-330,210,287,211,290,334,289,331,335,298,212,204,-333,292,293,294,295,344,-329,296,297,328,300,-332,299,301,345,304,336,-303,305,302,-307,337,310,308,-306,346,309,312,314,347,-313,348,338,315,351,339,316,349,322,350,311,-383,340,317,352,323,341,-353,342,358,343,318,359,363,324,364,365,360,354,-366,325,355,356,319,-362,361,-357,372,320,384,367,385,371,-369,373,376,386,387,368,-370,379,380,388,413,321,575,374,375,377,392,378,389,394,393,381,396,-390,395,382,-391,398,397,404,399,405,400,401,407,402,406,448,-450,403,-451,449,409,410,411,408,458,412,456,452,-453,457,460,420,459,414,-455,461,415,416,466,467,419,417,-454,418,470,421,423,422,426,425,-429,424,427,468,432,430,469,-428,431,434,576,577,471,-435,436,472,473,437,578,474,438,462,444,-475,433,463,-505,476,480,439,477,481,478,445,464,-479,465,482,485,446,-484,486,-494,487,440,447,483,-488,535,495,506,489,441,507,-492,493,442,508,509,510,490,-491,501,511,503,579,-512,496,513,580,581,443,497,498,514,499,504,-515,516,500,517,502,518,519,520,521,522,523,526,524,-525,582,583,584,531,532,533,585,586,587,527,534,528,536,-537,-529,538,542,539,530,540,541,561,588,589,543,545,590,544,-547,548,551,554,546,-549,552,553,591,592,-550,556,562,557,563,558,555,-566,559,571,564,572,567,565,574,568,569,570,560,-573,593,595,594,597,596,598,600,599,602,601,603,604]
 
 
 def rank_program(g, core, T, topo):
@@ -163,34 +163,44 @@ def rank_program(g, core, T, topo):
     def xload(dst, d):
         return [(dst(h), T.cells[32 * d:32 * d + 32, 1024 * h:1024 * h + 1024]) for h in range(2)]
     for d in peers:
-        dma("sp", xload(lambda h: T.XS[64 * h:64 * h + 64, d, :], d), "", "XS%d" % d)
+        for h, q in enumerate(("sp", "act")):
+            dma(q, xload(lambda h: T.XS[64 * h:64 * h + 64, d, :], d)[h:h + 1], "", "XS%d%s" % (d, "ab"[h]))
     dma("act", xload(lambda h: T.X[64 * h:64 * h + 64, 512 * me:512 * me + 512], me), "", "X%d" % me)
     dma("sp", [(T.KA[:, e // 2, e % 2, :], T.kids[4 * e:4 * e + 4, :]) for e in range(8)], "", "KA")
     dma("act", [(T.KN[:], T.kids[:])], "", "KN")
 
     op("pool", lambda: g.iota(T.PI[:], [[0, 1]], 0, 1), "", "PI")
-    op("dve", [ms(T.BO[:], 1.0), ms(T.SH[:], 0.0), ms(T.SX[:], 0.0)], "", "SH SX BO")
+    op("dve", [ms(T.BO[:], 1.0), ms(T.SH[:], 0.0)], "", "SH BO")
     op("dve", scan(T.MI[:], T.BO[:], T.BO[:], A.mult, A.add), "BO", "MI")
-    fields = [(3, 3), (1, 16), (1, 3), (0, 65), (0, 15), (0, 12), (2, 9), (4, 1), (6, 1), (0, 1), (0, 29), (0, 32), (1, 1), (0, 3), (5, 3), (0, 63)]
-    op("dve", [ts(T.FI[:, j:j + 1], T.PI[:], s, SHR, m, AND) for j, (s, m) in enumerate(fields)], "PI", "FI")
-    op("dve", [ts(T.C0[:, a, :], T.MI[:], -1.0, A.add) for a in range(4)], "MI", "C0")
-    op("dve", [cp(FF[:, 0:16], T.FI[:, 0:16]), ts(T.RP[:, 0:128], T.MI[:], -41.0, A.add), ts(T.RP[:, 128:256], T.MI[:], 87.0, A.add)], "FI MI", "FF RP")
-    op("dve", [ms(T.C0[p:p + 32, a, :], float(a)) for p in (32, 96) for a in range(4)], "", "C0")
+    fields = [(3, 3), (1, 16), (1, 3), (0, 65), (0, 15), (0, 12), (2, 9), (4, 1), (6, 1), (0, 1), (0, 29), (0, 32), (1, 1), (0, 3), (5, 3),
+              (0, 63), (2, 1), (3, 15)]
+    op("dve", [ts(T.FI[:, j:j + 1], T.PI[:], s, SHR, m, AND) for j, (s, m) in enumerate(fields[:6])], "PI", "FI")
+    op("dve", [ts(T.FI[:, j + 6:j + 7], T.PI[:], s, SHR, m, AND) for j, (s, m) in enumerate(fields[6:])], "PI", "FJ")
+    op("dve", [cp(FF[:, 6:17], T.FI[:, 6:17]), cp(col(36), T.FI[:, 17:18])], "FJ", "FE")
+    op("x", ([ts(T.C0[:, a, :], T.MI[:], -1.0, A.add) for a in range(4)], [act(T.C0[:, a, :], T.MI[:], F.Copy, bias=-1.0) for a in range(4)]), "MI", "C0")
+    op("dve", cp(FF[:, 0:6], T.FI[:, 0:6]), "FI", "FF")
+    op("x", ([ts(T.RP[:, 0:128], T.MI[:], -41.0, A.add), ts(T.RP[:, 128:256], T.MI[:], 87.0, A.add)],
+             [act(T.RP[:, 0:128], T.MI[:], F.Copy, bias=-41.0), act(T.RP[:, 128:256], T.MI[:], F.Copy, bias=87.0)]), "MI", "RP")
+    for p in (32, 96):
+        op("x", ([ms(T.C0[p:p + 32, a, :], float(a)) for a in range(4)],
+                 [act(T.C0[p:p + 32, a, :], T.MI[p:p + 32, :], F.Copy, scale=0.0, bias=float(a)) for a in range(4)]), "MI", "C0")
 
     def hconst(slot):
         op("act", [act(T.H[64:128, slot, :], T.C0[64:128]), act(T.H[0:64, 2 + slot, :], T.C0[0:64])], "C0", "HC%d" % slot)
     op("pool", [io(T.RT[:, 2 * t:2 * t + 2], [[16, 2], [1, 4], [0, 4]], 3 * (t >> 1) - 1) for t in range(4)]
        + [io(T.CT[:, 4 * h:4 * h + 4], [[3, 2], [0, 8], [1, 4]], -1) for h in range(2)]
        + [io(T.J16[:, 16:20], [[64, 2], [1, 2]], 0), io(T.J16[:, 0:16], [[1, 16]], 0)], "", "RT CT J16")
-    op("pool", [io(T.RT[:, 2 * t:2 * t + 2, 3, :], [[16, 2], [1, 2], [0, 2]], 2 * (t >> 1)) for t in range(4)]
-       + [io(T.CT[:, 4 * h:4 * h + 4, 3, :], [[2, 2], [0, 4], [1, 2]], 0) for h in range(2)], "", "RT CT")
     for d in peers:
-        send([(d, T.X[:, 512 * me:512 * me + 512], T.XS[:, d, :], "ax%d" % me)], 16, "XS%d" % d)
+        send([(d, T.X[:, 512 * me:512 * me + 512], T.XS[:, d, :], "ax%d" % me)], 16, "XS%da XS%db" % (d, d))
         arrives("ax%d" % d, 16, "X%d" % d)
     op("dve", [tt(col(20), col(0), col(1), A.add), ts(col(21), col(4), 3.0, A.is_equal, 4.0, A.mult),
-               ts(col(22), col(5), 12.0, A.is_equal, -1.0, A.mult), ts(col(23), col(6), 8.0, A.is_equal, -129.0, A.mult),
+               ts(col(22), col(5), 12.0, A.is_equal, -1.0, A.mult)], "FF", "FG")
+    op("dve", [ts(col(17), col(7), 60.0, A.mult, col(2), A.add), ts(col(18), col(16), 30.0, A.mult, col(0), A.add)], "FF FE", "FA")
+    op("dve", ts(col(19), col(17), col(18), A.add, col(20), A.add), "FA FG", "FB")
+    op("dve", ts(T.SX[:], T.RP[:, 28:156], col(19), A.is_equal), "RP FB", "SX")
+    op("dve", [ts(col(23), col(6), 8.0, A.is_equal, -129.0, A.mult),
                ts(col(26), col(11), 2.0, A.mult, col(10), A.add), ts(col(27), col(12), 15.0, A.mult, 1.0, A.add),
-               ts(col(28), col(5), 2.0, A.mult, col(13), A.add), cp(col(29), T.PI[:])], "FF PI", "FG")
+               ts(col(28), col(5), 2.0, A.mult, col(13), A.add), cp(col(29), T.PI[:])], "FF FE PI", "FD")
     dma("sp", [(T.NS[:, d, :], T.nodes[32 * d:32 * d + 32, :]) for d in peers], "", "NS")
     dma("sp", [(T.NI[:, 64 * me:64 * me + 64], T.nodes[32 * me:32 * me + 32, :]), (T.WI[0:32, 0:1], T.wt[32 * me:32 * me + 32, :])], "", "NIo WI")
     for n, k in (("PM", 136), ("DM", 128), ("R0", 128), ("WZ", 208), ("WY", 208), ("WP1", 128), ("WD", 32), ("WE", 64), ("WK", 32), ("WJ", 64), ("WQ", 136)):
@@ -203,15 +213,15 @@ def rank_program(g, core, T, topo):
 
     def hot(src, slot):
         c = slice(512 * src, 512 * src + 512)
-        op("dve", [ts(T.H[0:64, slot, :], T.X[0:64, c], 15.0, A.is_equal), ts(T.H[64:128, 2 + slot, :], T.X[64:128, c], 15.0, A.is_equal)],
-           "X%d" % src, "H%d" % slot)
+        for h in range(2):
+            o, i = T.H[64 * h:64 * h + 64, 2 * h + slot, :], T.X[64 * h:64 * h + 64, c]
+            op("x", (ts(o, i, 15.0, A.is_equal), act(o, i, F.Relu, bias=-14.0)), "X%d" % src, "H%d%d" % (slot, h))
 
     hot(me, 0)
     op("dve", [ts(T.GB[:], T.J16[:, 0:16], col(21), A.mult, col(22), A.add), ts(T.J16[:, 16:20], T.J16[:, 16:20], col(3), A.is_equal),
                tt(T.RT[:], T.RT[:], T.CT[:], A.max)], "FF FG CT", "J16 GB RT")
     op("dve", [ts(T.SH[:, :, 0:3, 0:3], T.RT[:, :, 0:3, 0:3], 1.0, A.is_equal),
-               ts(T.SX[:, :, 0:3, 0:3], T.RT[:, :, 0:3, 0:3], 0.0, A.is_equal, 16.0, A.mult),
-               ts(T.SX[:, :, 3, :], T.RT[:, :, 3, :], 0.0, A.is_equal)], "RT", "SH SX")
+               ts(T.SX[:, :, 0:3, 0:3], T.RT[:, :, 0:3, 0:3], 0.0, A.is_equal, 16.0, A.mult)], "RT", "SH SX")
     op("dve", [ts(T.WH[:, j, :], T.SH[:], T.J16[:, 16 + j:17 + j], A.mult) for j in range(4)], "SH J16", "WH")
     op("dve", [ts(T.WX[:, j, :], T.SX[:], T.J16[:, 16 + j:17 + j], A.mult) for j in range(4)], "SX J16", "WX")
     op("dve", [ms(T.WH[64 * (1 - h) + 32 * b:64 * (1 - h) + 32 * b + 1, 2 * h:2 * h + 2, 7 - 4 * b::16], 1.0) for h in range(2) for b in range(2)],
@@ -220,24 +230,24 @@ def rank_program(g, core, T, topo):
     def gbuild(i, src, j):
         ch, c, b = 4 * src + j, slice(512 * src, 512 * src + 512), (4 * i + j) % 8
         mm([(P[b][:], T.WX[:, j, :], T.X[:, c], True, False), (P[b][:], T.WH[:, j, :], T.H[:, (j & 2) + (i & 1), :], False, True)],
-           "WH WX HC%d X%d H%d" % (i & 1, src, i & 1), "P%d" % b)
+           "WH WX HC%d X%d H%d%d" % (i & 1, src, i & 1, j >> 1), "P%d" % b)
         o, bias = T.G[:, 512 * ch:512 * ch + 512], T.GB[:, ch:ch + 1]
         op("x", (ts(o, P[b][:], bias, A.add, 0.0, A.max), act(o, P[b][:], F.Relu, bias=bias)), "GB", "P%d G%d" % (b, ch))
     for j in range(4):
         gbuild(0, me, j)
     op("dve", cp(T.KF[:], T.KN[:]), "KN", "KF")
     op("dve", [ts(col(30), col(8), 2.0, A.mult, col(26), A.add), ts(col(31), col(7), 64.0, A.mult, col(28), A.add)]
-       + [ts(col(32 + d), col(14), float(d), A.is_equal) for d in range(4)], "FF FG", "FH")
+       + [ts(col(32 + d), col(14), float(d), A.is_equal) for d in range(4)], "FE FD", "FH")
     op("dve", ts(T.KN[:], T.KN[:], 127, AND), "", "KN")
     op("act", act(T.KH[:], T.KF[:], F.Copy, scale=1.0 / 128, bias=128.50390625), "KF", "KH")
     op("dve", [ts(T.WLX[:], T.RP[:, 40:168], col(30), A.is_equal, col(27), A.mult)]
        + [ts(T.WKD[:, 2 * d + e], T.RP[:, 8 - 4 * e:136 - 4 * e], col(31), A.is_equal, col(32 + d), A.mult) for d in range(4) for e in range(2)],
-       "RP FH", "WLX WKD")
+       "RP FD FH", "WLX WKD")
     op("dve", cp(T.KLO[:], T.KN[:]), "KN", "KLO")
     op("dve", [cp(T.KB[:, :, :, s, :], T.KA[:, :, s, :]) for s in range(2)], "KA", "KB")
-    op("dve", [ts(T.IDF[:], T.RP[:, 40:168], col(29), A.is_equal), ts(IDB, T.RP[:, 40:168], col(29), A.is_equal)], "RP FG", "IDF IDB")
+    op("dve", [ts(T.IDF[:], T.RP[:, 40:168], col(29), A.is_equal), ts(IDB, T.RP[:, 40:168], col(29), A.is_equal)], "RP FD", "IDF IDB")
     op("dve", lambda: V.transpose(T.KT[:], T.KB[:]), "KB", "KT")
-    op("dve", [ts(T.TE[:, 64:192], T.RP[:, 40:168], col(29), A.is_equal), ts(T.TE[:, 0:64], T.RP[:, 40:104], col(15), A.is_gt)], "RP FF FG", "TE")
+    op("dve", [ts(T.TE[:, 64:192], T.RP[:, 40:168], col(29), A.is_equal), ts(T.TE[:, 0:64], T.RP[:, 40:104], col(15), A.is_gt)], "RP FE FD", "TE")
     op("dve", [cp(T.KL[:, b::4], T.KT[:, :, b, :]) for b in range(4)], "KT", "KL")
     op("dve", cp(T.TL[:, 128 * me:128 * me + 128], T.KL[:, 128 * me:128 * me + 128]), "KL", "TLo")
     send([(d, T.NI[:, 64 * me:64 * me + 64], T.NS[:, d, :], "an") for d in peers], 4, "NS")
@@ -249,26 +259,17 @@ def rank_program(g, core, T, topo):
     puts("DM", [(T.DM[:, 2 * t:2 * t + 2, 12:16], [[-16, 2], [-4, 2], [-1, 2]], -8 * tr - 2 * tc, 1) for t, tr, tc in quad])
 
     def lpack(d):
-        b = 4 + (d ^ me)
-        xs, k = (T.X[:, 512 * me:512 * me + 512], "X%d" % me) if d == me else (T.XS[:, d, :], "XS%d" % d)
+        b = d ^ me
+        xs, k = (T.X[:, 512 * me:512 * me + 512], "X%d" % me) if d == me else (T.XS[:, d, :], "XS%da XS%db" % (d, d))
         mm([(P[b][:], T.WLX[:], xs, True, False), (P[b][:], T.WKD[:, 2 * d], T.KH[:], False, False),
             (P[b][:], T.WKD[:, 2 * d + 1], T.KLO[:], False, True)], "WLX WKD KH KLO " + k, "P%d" % b)
-        op("x", (ts(T.LS[:, d, :], P[b][:], col(23), A.add), act(T.LS[:, d, :], P[b][:], bias=col(23))), "FG", "P%d LS%d" % (b, d))
-    for d in peers + [me]:
-        lpack(d)
-    for d in peers:
-        send([(d, T.S[me], T.LS[:, d, :], "al%d" % me)], 16, "LS%d" % d)
-        arrives("al%d" % d, 16, "S%d" % d)
-    dma("sp", [(T.CW[:, 0:2048], T.cells[:])], "", "CW")
-    for d in [me] + peers:
-        dma("sp", [(T.L[32 * r:32 * r + 32, 2048 * d:2048 * d + 2048], T.LS[:, d, :] if d == me else T.S[d]) for r in range(4)],
-            "LS%d" % d if d == me else "S%d" % d, "L%d" % d + (" KL" if d == me else ""))
-    dma("sp", [(T.KW[16 * e:16 * e + 4, 0:2048], T.KF[16 * e:16 * e + 16, :]) for e in range(8)], "KF", "KW")
+        op("x", (ts(T.LS[:, d, :], P[b][:], col(23), A.add), act(T.LS[:, d, :], P[b][:], bias=col(23))), "FD", "P%d LS%d" % (b, d))
     hot(peers[0], 1)
     hot(peers[1], 0)
-    op("dve", [ms(T.MK[:], 1.0), ms(T.BW[:], 1.0), ms(T.BT[:], 1.0),
-               ts(T.WI[0:32, 1:2], T.WI[0:32, 0:1], 6, SHR), ts(T.WI[0:32, 2:3], T.WI[0:32, 0:1], 63, AND),
-               cp(T.SM[:, 1:2], col(7)), ts(T.SM[:, 0:1], col(7), 0.0, A.is_equal)], "WI FF", "MK BW BT WI2 SM")
+    for n, parts in (("MK", [T.MK[:]]), ("BT", [T.BT[:, 0], T.BT[:, 1]])):
+        op("x", (ms(T[n][:], 1.0), [act(o, T.RP[:, 0:8 if n == "MK" else 256], F.Copy, scale=0.0, bias=1.0) for o in parts]), "RP", n)
+    op("dve", [ts(T.WI[0:32, 1:2], T.WI[0:32, 0:1], 6, SHR), ts(T.WI[0:32, 2:3], T.WI[0:32, 0:1], 63, AND),
+               cp(T.SM[:, 1:2], col(7)), ts(T.SM[:, 0:1], col(7), 0.0, A.is_equal)], "WI FE", "WI2 SM")
     for i in range(1, 4):
         for j in range(4):
             if (i, j) == (1, 3):
@@ -278,6 +279,16 @@ def rank_program(g, core, T, topo):
             if (i, j) == (2, 3):
                 op("dve", cp(T.NF[:], T.NI[:]), "NI NIo", "NF")
             gbuild(i, peers[i - 1], j)
+    for d in peers + [me]:
+        lpack(d)
+    for d in peers:
+        send([(d, T.S[me], T.LS[:, d, :], "al%d" % me)], 16, "LS%d" % d)
+        arrives("al%d" % d, 16, "S%d" % d)
+    for d in [me] + peers:
+        dma("sp", [(T.L[32 * r:32 * r + 32, 2048 * d:2048 * d + 2048], T.LS[:, d, :] if d == me else T.S[d]) for r in range(4)],
+            "LS%d" % d if d == me else "S%d" % d, "L%d" % d + (" KL" if d == me else ""))
+    dma("sp", [(T.KW[16 * e:16 * e + 4, 0:2048], T.KF[16 * e:16 * e + 16, :]) for e in range(8)], "KF L0 L1 L2 L3", "KW")
+    dma("sp", [(T.CW[:, 0:2048], T.cells[:])], "L0 L1 L2 L3", "CW")
     GALL = " ".join("G%d" % c for c in range(16))
     LALL = "L0 L1 L2 L3 L"
 
@@ -316,32 +327,41 @@ def rank_program(g, core, T, topo):
        + [ts(T.WT[:, 2 * f:2 * f + 2], T.SM[:], T.WG[:, 2 + f:3 + f], A.mult) for f in range(2)], "WG MK SM", "WC WT")
     TALL = " ".join("TT%d" % a for a in range(0, 512, 64))
 
-    keep("BW", T.BW[:], [[-64, 2], [-8, 8], [0, 16]], 0, 1)
-    keep("BW", T.BW[:], [[64, 2], [8, 8], [0, 16]], 7, -1)
+    op("dve", ts(col(37), col(36), -1.0, A.mult, -129.0, A.add), "FE", "FL")
+    op("act", act(T.BW[:], T.RP[:], F.Copy, scale=0.0625, bias=131.03125), "RP", "BW")
+    op("act", act(T.BW[:], T.BW[:], F.Abs, bias=col(37)), "FL", "BW")
+    op("act", act(T.BW[:], T.BW[:], F.Relu, scale=-1.0, bias=1.0), "", "BW")
     for kh in range(2):
         keep("BT", T.BT[:, :, kh, :], [[128, 2], [16, 8], [1, 16]], -kh, -2)
         put("BT", T.BT[:, :, kh, :], [[128, 2], [16, 8], [1, 16]], -kh, -127, -2)
-        keep("BT", T.BT[:, :, kh, :], [[-64, 2], [-8, 8], [0, 16]], 0, 1)
-    op("pool", [io(T.T3[:, 16:18], [[16, 2]], 0), io(T.JT[:], [[0, 4], [1, 32]], -127), io(T.DIAG[:], [[0, 8], [1, 16]], 0),
-                io(T.DG[:], [[-16, 2], [0, 4], [1, 32]], 0), io(T.T3[:, 0:8], [[16, 8]], 8193), io(T.T3[:, 8:16], [[2048, 4], [16, 2]], 2049),
-                io(T.TP[:, :, 0:8], [[0, 4], [16, 8]], 8192), io(T.TP[:, :, 8:16], [[0, 16], [16, 2]], 2048),
-                io(T.RW[:], [[0, 512]], 0), io(T.B2[:], [[0, 144]], 0)], "", "K2 DG RW B2")
+        op("dve", tt(T.BT[:, :, kh, :], T.BT[:, :, kh, :], T.BW[:], A.mult), "BW", "BT")
+    op("pool", [io(T.T3[:, 16:18], [[16, 2]], 0), io(T.JT[:], [[1, 32]], -127), io(T.DG[:, 256:384], [[0, 8], [1, 16]], 0),
+                io(T.DG[:, 0:256], [[-16, 2], [0, 4], [1, 32]], 0), io(T.T3[:, 0:8], [[16, 8]], 8193), io(T.T3[:, 8:16], [[2048, 4], [16, 2]], 2049),
+                io(T.TP[:, 0], [[0, 4], [16, 8]], 8192), io(T.TP[:, 1], [[0, 16], [16, 2]], 2048), io(T.TP[:, 2], [[0, 4], [2048, 4], [0, 2]], 0)],
+       "", "K2 DG")
+    op("x", (ms(T.RW[:], 0.0), act(T.RW[:], T.C0[:], F.Copy, scale=0.0)), "C0", "RW")
+    op("x", (ms(T.B2[:], 0.0), act(T.B2[:], T.RP[:, 0:144], F.Copy, scale=0.0)), "RP", "B2")
     keep("BO", T.BO[:], [[-16, 8], [0, 16]], 0, 1)
     keep("BO", T.BO[:], [[16, 8], [0, 16]], 15, -1)
-    puts("RW", [(T.RW[:, src, :], [[0, 4], [-32, 2], [-1, 16]], -64 * (src >> 1) - 16 * (src & 1), 1) for src in range(4)])
+    puts("RW", [(T.RW[:, src, :], [[0, 4], [-32, 2], [-1, 16]], -64 * (src >> 1) - 16 * (src & 1), -1) for src in range(4)])
 
     def consts2():
         c4 = col(4)
-        op("dve", [ts(col(24), col(9), -2193.0, A.mult, 2064.0, A.add), ts(col(25), c4, 64.0, A.mult)], "FF", "FK")
-        op("dve", [ms(T.RM[:], 1.0), ms(T.RB[:], 0.0), ms(T.PZ[:], 0.0),
-                   ts(T.T3[:, 16:18], T.T3[:, 16:18], c4, A.add, 0.5, A.add), ts(T.T3[:, 0:16], T.T3[:, 0:16], c4, A.add),
-                   ts(T.TP[:], T.TP[:], c4, A.add)], "FF", "RM RB PZ K2")
-        op("dve", [ms(T.RM[:, 0::16], 0.0), ms(T.RB[:, 0::32], 65536.0), ts(T.DIAG[:], T.DIAG[:], c4, A.is_equal),
-                   ts(T.TRI[:], T.DG[:], c4, A.is_ge, 16384.0, A.mult), ts(T.B2[:, 15:143:16], T.BO[:, 0::16], col(25), A.mult)],
+        op("dve", [ts(col(24), col(9), -2193.0, A.mult, 2064.0, A.add), ts(col(25), c4, 64.0, A.mult)], "FF FE", "FK")
+        for n, k, v in (("RM", 128, 1.0), ("ONE", 128, 1.0), ("RB", 256, 0.0), ("PZ", 130, 0.0)):
+            op("x", (ms(T[n][:], v), act(T[n][:], T.RP[:, 0:k], F.Copy, scale=0.0, bias=v)), "RP", n)
+        op("dve", ts(T.T3[:, 16:18], T.T3[:, 16:18], c4, A.add, 0.5, A.add), "FF", "K2")
+        op("x", ([ts(T.T3[:, 0:16], T.T3[:, 0:16], c4, A.add), ts(T.TP[:, 0:2], T.TP[:, 0:2], c4, A.add)],
+                 [act(T.T3[:, 0:16], T.T3[:, 0:16], bias=c4), act(T.TP[:, 0:2], T.TP[:, 0:2], bias=c4)]), "FF", "K2")
+        op("dve", [ms(T.RM[:, 0::16], 0.0), ms(T.RB[:, 0::32], 2.0 ** 29), ts(T.TRI[:, 256:384], T.DG[:, 256:384], c4, A.not_equal, -2.0 ** 28, A.mult),
+                   ts(T.TRI[:, 0:256], T.DG[:, 0:256], c4, A.is_ge, 2.0 ** 28, A.mult), ts(T.B2[:, 15:143:16], T.BO[:, 0::16], col(25), A.mult)],
            "FF FK DG BO", "RM RB K2 B2")
+        op("x", (ts(T.BO[:], T.BO[:], 16384.0, A.mult), act(T.BO[:], T.BO[:], F.Copy, scale=16384.0)), "", "BO")
 
     def consts3():
-        op("pool", [io(T[n][:], [[0, 896]], 0) for n in ("WA", "WB", "WO")] + [io(T.PF[:], [[0, 132]], 0)], "", "WA WB WO PF")
+        for n in ("WA", "WB", "WO"):
+            op("x", (ms(T[n][:], 0.0), act(T[n][:], T.G[:, 0:896], F.Copy, scale=0.0)), GALL, n)
+        op("x", (ms(T.PF[:], 0.0), act(T.PF[:], T.RP[:, 0:132], F.Copy, scale=0.0)), "RP", "PF")
         put("PF", T.PF[:, 1::2, :], [[-16, 2], [-1, 8], [32, 4]], -96 - 8 * (me & 1), 1)
         for src in range(4):
             b = -64 * (src >> 1) - 16 * (src & 1)
@@ -350,6 +370,7 @@ def rank_program(g, core, T, topo):
             put("WO", T.WO[:, src, 6:8, 0:4], [[-32, 2], [-2, 4]], b - 9, 1)
 
     TO = T.TO
+    OW, AN, KBX, A1, HS = (T.SC[:, j, :] for j in range(5))
 
     def tgather(sh, kh, a):
         c = 128 * sh + 64 * kh + 32 * a
@@ -393,40 +414,41 @@ def rank_program(g, core, T, topo):
         op("dve", [ts(T.HJ[:, 0, :], T.HI[:], 8190, AND), ts(T.HJ[:, 1, :], T.HI[:], 1, AND)], "HI", "HJ")
         op("dve", [tt(T.HP[:, 0:64], T.HJ[:, 0, :], T.HJ[:, 1, :], A.add), tt(T.HP[:, 64:128], T.HJ[:, 0, :], T.HJ[:, 1, :], A.subtract)], "HJ", "HP")
         mm([(P[4][:, 128:256], T.HP[:], T.IDF[:], True, True)], "HP IDF", "P4")
-        op("dve", ts(T.HJ[:, 2, :], T.HI[:], 11, SHR, 3, AND), "HI", "HK")
+        op("x", (ts(OW, T.HP[:, 0:64], 2.0 ** -11, A.mult, 128.500244140625, A.add),
+                 act(OW, T.HP[:, 0:64], F.Copy, scale=2.0 ** -11, bias=128.500244140625)), "HP", "OW")
 
     def hash2():
-        op("dve", ts(T.LL[:], P[4][:, 128:256], col(8), A.add), "FF", "P4 LL")
-
-    OW, AN, KBX, A1, HS = (T.SC[:, j, :] for j in range(5))
+        op("dve", ts(T.LL[:], P[4][:, 128:256], col(8), A.add), "FE", "P4 LL")
 
     def lookup():
         for j in range(4):
             gather(T.R[:, 512 * j:512 * j + 512], T.L[:, 0:8192], T.LL[:, 32 * j:32 * j + 32], LALL + " LL", "R%d" % j)
-        op("dve", ts(OW, T.HJ[:, 2, :], 1.0, A.add, 0.125, A.mult), "HK", "OW")
+        op("x", (ts(OW, OW, 0.125, A.mult, -16.0, A.add), act(OW, OW, F.Copy, scale=0.125, bias=-16.0)), "", "OW")
 
     def dmm():
-        mm([(P[0][:, kl::8], T.Y[:, 128 * kl:128 * kl + 128], T.WE[:], kl == 0, False) for kl in range(8)], "WE Y0 Y1", "P0")
-        mm([(P[1][:, kl::8], T.Y[:, 128 * kl:128 * kl + 128], T.WJ[:], kl == 0, False) for kl in range(8)], "WJ Y0 Y1", "P1")
+        for b, Wy, Wr, k in ((0, T.WE, T.WD, "WE WD"), (1, T.WJ, T.WK, "WJ WK")):
+            mm([(P[b][:, kl::8], T.Y[:, 128 * kl:128 * kl + 128], Wy[:], kl == 0, False) for kl in range(4)], k + " Y0", "P%d" % b)
+            mm([(P[b][:, i::16], T.R[:, i::16], Wr[:], False, False) for i in range(16)], k + " R0 R1 R2 R3", "P%d" % b)
+            mm([(P[b][:, kl::8], T.Y[:, 128 * kl:128 * kl + 128], Wy[:], False, kl == 7) for kl in range(4, 8)], k + " Y1", "P%d" % b)
         for sh in range(2):
-            mm([(P[2 + sh][:, 0:128], T.WQ[:, sh, 7 - kl:135 - kl], T.Y[:, 128 * kl:128 * kl + 128], kl == 0, False) for kl in range(8)],
-               "WQ Y0 Y1", "P%d" % (2 + sh))
-        mm([(P[0][:, i::16], T.R[:, i::16], T.WD[:], False, i == 15) for i in range(16)], "R0 R1 R2 R3 WD", "P0")
-        mm([(P[1][:, i::16], T.R[:, i::16], T.WK[:], False, i == 15) for i in range(16)], "R0 R1 R2 R3 WK", "P1")
+            for b in range(2):
+                mm([(P[2 + sh][:, 0:128], T.WQ[:, sh, 7 - kl:135 - kl], T.Y[:, 128 * kl:128 * kl + 128], kl == 0, False) for kl in range(4 * b, 4 * b + 4)],
+                   "WQ Y%d" % b, "P%d" % (2 + sh))
 
     def choose():
         EQ, S0, E0 = T.EQ, T.SEL[:, 0:64], T.EQ[:, 384:448]
-        op("dve", [ts(EQ[:, 0:384], P[0][:, 0:384], 0.0, A.is_equal), ts(EQ[:, 384:512], P[0][:, 384:512], 0.0, A.is_lt)], "", "P0 EQ")
+        op("dve", ts(EQ[:, 0:384], P[0][:, 0:384], 0.0, A.is_equal), "", "P0 EQ")
+        op("x", (ts(EQ[:, 384:512], P[0][:, 384:512], 0.0, A.is_lt), act(EQ[:, 384:512], P[0][:, 384:512], F.Relu, scale=-1.0 / 17)), "", "P0 EM")
         op("dve", tt(T.TQ[:], EQ[:, 0:128], EQ[:, 128:256], A.mult), "EQ", "TQ")
-        op("dve", [tt(AN, E0, EQ[:, 448:512], A.max), tt(KBX, T.HJ[:, 1, :], E0, A.is_equal)], "EQ HJ", "AN KBX")
+        op("dve", [tt(AN, E0, EQ[:, 448:512], A.max), tt(KBX, T.HJ[:, 1, :], E0, A.is_equal)], "EM HJ", "AN KBX")
         op("dve", [tt(S0, T.TQ[:, 0:64], EQ[:, 256:320], A.mult), tt(A1, T.TQ[:, 64:128], EQ[:, 320:384], A.mult)], "TQ EQ", "S0 A1")
         op("dve", tt(AN, AN, OW, A.mult), "OW", "AN")
         op("dve", [tt(T.SEL[:, 64:128], A1, S0, A.is_gt), tt(HS, A1, S0, A.max)], "S0 A1", "S1 HS")
-        op("dve", tt(AN, AN, HS, A.subtract), "HS", "AN")
+        op("dve", [ts(T.FO[:, o, :], AN, -0.125 * (o + 1), A.add) for o in range(4)], "AN", "FO")
         op("dve", tt(T.PZ[:, 1:129:2], T.HJ[:, 0, :], KBX, A.add), "HJ KBX", "PZ")
-        op("dve", [ts(T.MO[:, 64 * o:64 * o + 64], AN, 0.125 * (o + 1), A.is_equal) for o in range(4)], "AN", "MO")
-        mm([(P[7][:, 192 * h:192 * h + 192], T.MO[:, 128 * h:128 * h + 128], T.TE[:], True, True) for h in range(2)], "MO TE", "P7")
-        either(T.CK[:], P[7][:, 0:384], "", "P7 CK")
+        op("dve", [tt(T.MO[:, 64 * o:64 * o + 64], T.FO[:, o, :], HS, A.is_equal) for o in range(4)], "FO HS", "MO")
+        mm([(P[4][:, 192 * h:192 * h + 192], T.MO[:, 128 * h:128 * h + 128], T.TE[:], True, True) for h in range(2)], "MO TE", "P4")
+        either(T.CK[:], P[4][:, 0:384], "", "P4 CK")
         op("dve", [tt(T.PR[:, :, :, t, :], P[1][:, 128 * t:128 * t + 128], T.SEL[:], A.mult) for t in range(4)], "S0 S1", "P1 PR")
         for sh in range(2):
             mm([(P[2 + sh][:, 0:128], T.PR[:, w, sh], T.IDF[:], False, w == 1) for w in range(2)], "PR IDF", "P%d" % (2 + sh))
@@ -441,49 +463,58 @@ def rank_program(g, core, T, topo):
         mm([(P[6][:, 64 * o:64 * o + 64], T.BW[:, o & 1], T.CK[:, 192 * (o >> 1):192 * (o >> 1) + 64], True, True) for o in range(4)], "BW CK", "P6")
         mm([(P[5][:, 64 * o:64 * o + 64], T.BW[:, o & 1] if j == 0 else T.BT[:, o & 1, j - 1],
              T.CK[:, 192 * (o >> 1) + 64 * j:192 * (o >> 1) + 64 * j + 64], j == 0, j == 2) for o in range(4) for j in range(3)]
-           + [(P[5][:, 256:320], T.PZ[:, 1 - kh:129 - kh], T.IDF[:, 64 * kh:64 * kh + 64], kh == 0, kh == 1) for kh in range(2)],
-           "BW BT CK PZ IDF", "P5")
+           + [(P[5][:, 256:320], T.PZ[:, 1 - kh:129 - kh], T.IDF[:, 64 * kh:64 * kh + 64], kh == 0, False) for kh in range(2)]
+           + [(P[5][:, 256:320], T.ONE[:], T.IDB[:, 0:64], False, True)], "BW BT CK PZ IDF IDB ONE", "P5")
         op("act", [act(T.SG[:, 64 * j:64 * j + 64], P[6][:, 64 * (j >> 1):64 * (j >> 1) + 64], F.Sign, bias=T.T3[:, 16 + (j & 1):17 + (j & 1)],
                        scale=-1.0, accum_out=T.CNT[:, j:j + 1]) for j in range(8)], "K2", "P6 SG CNT")
-        op("act", [act(T.UT[:, 0:256], P[5][:, 0:256]), act(T.UT[:, 256:320], P[5][:, 256:320], F.Copy, bias=1.0)], "", "P5 UT")
-        mm([(P[7][:, 0:256], IDB, T.TRI[:], True, False)], "IDB K2", "P7")
+        either(T.UT[:], P[5][:, 0:320], "", "P5 UT")
+        mm([(P[7][:, 0:256], IDB, T.TRI[:, 0:256], True, False)], "IDB K2", "P7")
 
     def claim3():
-        op("dve", [ts(T.CL[:, 2 * o:2 * o + 2], T.CNT[:, 2 * o:2 * o + 2], 0.5, A.mult, 31.0 + 64 * o, A.add) for o in range(4)], "CNT", "CL")
-        op("dve", [ts(T.CL[:, 8:16], T.CNT[:], 0.5, A.mult, 31.0, A.add), ts(T.CF[:], T.CNT[:], 0.5, A.mult, 31.0, A.add)], "CNT", "CM CF")
-        op("dve", tt(T.MF[:], T.UT[:, 0:256].indirect(T.CL[:, 0:8]), T.JT[:], A.is_equal), "UT CL K2", "MF")
+        op("dve", ts(T.CL[:], T.CNT[:], 0.5, A.mult, 31.0, A.add), "CNT", "CL")
+        op("x", (ts(T.CF[:], T.CNT[:], 0.5, A.mult, 31.0, A.add), act(T.CF[:], T.CNT[:], F.Copy, scale=0.5, bias=31.0)), "CNT", "CF")
+        op("dve", [tt(T.MF[:, 32 * o:32 * o + 32], T.UT[:, 64 * o:64 * o + 64].indirect(T.CL[:, 2 * o:2 * o + 2]), T.JT[:], A.is_equal)
+                   for o in range(4)], "UT CL K2", "MF")
         mm([(P[6][:, 0:8], T.IDF[:], T.CF[:], True, False)], "IDF CF", "P6")
         mm([(P[6][:, 0:8], T.B2[:, 15 - i:143 - i], T.MF[:, i::16], False, i == 15) for i in range(16)], "B2 MF", "P6")
-        op("dve", tt(T.VN[:], T.UT[:, 256:320].indirect(T.CL[:, 8:16]), T.MF[:], A.mult), "UT MF CM", "VN")
-        mm([(P[5][:, 0:128], T.BO[:], T.VN[:], True, True)], "BO VN", "P5")
+        op("dve", tt(T.VN[:], T.UT[:, 256:320].indirect(T.CL[:, :]), T.MF[:], A.mult), "UT MF CL", "VN")
+        mm([(P[5][:, 0:128], IDB, T.TRI[:, 256:384], True, False)], "IDB K2", "P5")
+        mm([(P[5][:, 0:128], T.BO[:], T.VN[:], False, True)], "BO VN", "P5")
         mm([(P[7][:, 128 * h:128 * h + 128], T.BO[:], T.VN[:], False, h == 1) for h in range(2)], "BO VN", "P7")
 
     def claim4(rd):
         op("dve", cp(T.NL[:], P[6][:, 0:8]), "", "P6 NL")
-        mm([(P[6][:, 0:64], T.IDF[:], T.TP[:], True, False)], "IDF K2", "P6")
+        mm([(P[6][:, 0:32], T.IDF[:], T.TP[:, 1 if rd == 2 else 0], True, False)], "IDF K2", "P6")
         gather(T.YG[:, rd, :], T.Y[:, :], T.NL[:, :], "NL Y0 Y1", "YG%d" % rd)
-        op("dve", tt(T.DG[:, 0:128], P[5][:, 0:128], T.DIAG[:], A.mult), "K2", "P5 DG")
-        op("dve", scan(T.DS[:], T.RM[:], T.DG[:, 0:128], A.mult, A.add), "RM DG", "DS")
-        op("act", [act(T.AB[:, 32 * j:32 * j + 32], P[7][:, 128 * (j & 1) + 32 * (j >> 1):128 * (j & 1) + 32 * (j >> 1) + 32], F.Abs,
-                       bias=T.DS[:, 16 * j + 15:16 * j + 16], scale=-1.0) for j in range(8)], "DS", "P7 AB")
+        op("dve", scan(T.DS[:], T.RM[:], P[5][:, 0:128], A.mult, A.max), "RM", "P5 DS")
+        for h in range(2):
+            z = [(T.AB[:, 32 * j:32 * j + 31], P[7][:, 128 * (j & 1) + 32 * (j >> 1):128 * (j & 1) + 32 * (j >> 1) + 31],
+                  T.DS[:, 16 * j + 15:16 * j + 16]) for j in range(4 * h, 4 * h + 4)]
+            op("x", ([ts(o, i, k, A.not_equal, 16384.0, A.mult) for o, i, k in z], [act(o, i, F.Abs, bias=k, scale=-1.0) for o, i, k in z]),
+               "DS", "P7 AB%d" % h)
         key, M3 = T.DS[:, 15:128:16], T.M3
-        op("dve", [tt(M3[:, 0:8], key, T.T3[:, 0:8], A.subtract), tt(M3[:, 8:16], key, T.T3[:, 8:16], A.subtract),
-                   ts(M3[:, 16:24], key, 1.0, A.min)], "DS K2", "D3")
+        op("x", (ts(M3[:, 16:24], key, 2.0 ** -14, A.mult), act(M3[:, 16:24], key, F.Copy, scale=2.0 ** -14)), "DS", "D2")
+        j = 8 if rd == 2 else 0
+        op("dve", tt(M3[:, 0:8], T.T3[:, j:j + 8], M3[:, 16:24], A.subtract), "D2 K2", "D3")
+        op("dve", tt(T.AB[:, 31::32], M3[:, 0:8], key, A.min), "D3 DS", "AB2")
 
     def lrec(rd):
         mm([(P[5][:, 128 * s:128 * s + 128], T.RB16[:, s, :], T.YG[:, rd, :], True, True) for s in range(4)], "RB16 YG%d" % rd, "P5")
         either(T.LR[:], P[5][:], "", "P5 LR")
 
     def claim5(rd):
-        M3 = T.M3
-        op("dve", scan(T.DG[:], T.RB[:], T.AB[:], A.add, A.min), "RB AB", "DG")
-        op("dve", tt(M3[:, 24:32], T.DG[:, 31::32], M3[:, 16:24], A.min), "DG D3", "M3")
-        op("dve", [tt(M3[:, 32 + 8 * j:40 + 8 * j], M3[:, 24:32], M3[:, 8 * j:8 * j + 8], A.mult) for j in range(2)], "M3 D3", "WR")
-        mm([(P[6][:, 16 * s:16 * s + 16], T.RW[:, s, :], M3[:, 32:48], False, s == 3) for s in range(4)], "RW WR", "P6")
-        op("dve", cp(T.OO[:, rd], P[6][:, 0:64]), "", "P6 OO%d" % rd)
+        op("dve", scan(T.DG[:, 0:256], T.RB[:], T.AB[:], A.add, A.min), "RB AB0 AB1 AB2", "DG")
+        mm([(P[6][:, 8 * s:8 * s + 8], T.RW[:, s, :], T.DG[:, 31:256:32], False, s == 3) for s in range(4)], "RW DG", "P6")
+        if rd == 2:
+            op("dve", cp(T.OO[:, rd, :, 0:8], P[6][:, 0:32]), "", "P6 OO%d" % rd)
+            return
+        op("dve", cp(T.LF[:], P[6][:, 0:32]), "", "P6 LF")
+        op("dve", tt(T.M3[:, 16:48], P[6][:, 0:32], T.TP[:, 2], A.subtract), "K2", "P6 D2 D4")
+        op("dve", tt(T.M3[:, 16:48], T.M3[:, 16:48], T.TP[:, 1], A.min), "K2", "D2 D4")
+        op("dve", cp(T.OO[:, rd, :, 0:8], T.M3[:, 16:48]), "D2 D4", "OO%d" % rd)
 
     def lscatter(rd, src):
-        op("dve", cp(T.L[:, :].indirect(T.OO[:, rd, src, 0:8]), T.LR[:, 128 * src:128 * src + 128]), "OO%d LR L0 L1 L2 L3" % rd, "L")
+        op("dve", cp(T.L[:, :].indirect(T.LF[:, 8 * src:8 * src + 8]), T.LR[:, 128 * src:128 * src + 128]), "LF LR L0 L1 L2 L3", "L")
 
     def post_rec(rd):
         send([(d, T.LB[:, rd, me ^ d, :], T.YG[:, rd, 32 * d:32 * d + 32], "ar%d" % rd) for d in peers], 4, "YG%d" % rd)
@@ -495,23 +526,24 @@ def rank_program(g, core, T, topo):
 
     def own1(rd):
         own = T.YG[:, rd, 32 * me:32 * me + 32]
-        op("act", [act(T.UH[:, 0:32], own, F.Copy, scale=0.0625, bias=128.53125),
-                   act(T.UH[:, 32:128], T.LB[:, rd, 1:4, :], F.Copy, scale=0.0625, bias=128.53125)], "YG%d LB%d" % (rd, rd), "UH")
+        z = ((T.UH[:, 0:32], own), (T.UH[:, 32:128], T.LB[:, rd, 1:4, :]))
+        op("x", ([ts(o, i, 0.0625, A.mult, 128.53125, A.add) for o, i in z], [act(o, i, F.Copy, scale=0.0625, bias=128.53125) for o, i in z]),
+           "YG%d LB%d" % (rd, rd), "UH")
 
         def rec(d):
             return own if d == me else T.LB[:, rd, me ^ d, :]
-        a, b = (4, 4) if rd < 2 else (2, 3)
+        a, b = (6, 6) if rd < 2 else (2, 3)
         for s in range(4):
             mm([(P[a][:, 32 * s:32 * s + 32], W[:, s, 6 - 2 * d:14 - 2 * d], rec(d) if j == 0 else T.UH[:, 32 * (me ^ d):32 * (me ^ d) + 32],
                  d + j == 0, d + j == 4) for j, W in enumerate((T.WA, T.WB)) for d in range(4)], "WA WB UH YG%d LB%d" % (rd, rd), "P%d" % a)
         for h in range(2):
             mm([(P[b][:, 128 + 32 * s:160 + 32 * s], T.WO[:, s, 6 - 2 * d:14 - 2 * d], rec(d), d == 0, d == 3) for s in (2 * h, 2 * h + 1) for d in range(4)],
                "WO YG%d LB%d" % (rd, rd), "P%d" % b)
-        op("act", act(T.VC[:, rd, :], P[a][:, 0:128], bias=col(24)), "FK", "P%d VC%d" % (a, rd))
+        op("x", (ts(T.VC[:, rd, :], P[a][:, 0:128], col(24), A.add), act(T.VC[:, rd, :], P[a][:, 0:128], bias=col(24))), "FK", "P%d VC%d" % (a, rd))
         either(T.VK[:, rd, :], P[b][:, 128:256], "", "P%d VK%d" % (b, rd))
 
     def own2(rd):
-        a = 8 + 2 * me
+        a = 2 * me
         op("dve", [cp(T.OL[32 * d:32 * d + 32, rd, :], T.OO[32 * d:32 * d + 32, rd, :, a:a + 2] if d == me
                       else T.LO[32 * d:32 * d + 32, rd, d, :, a:a + 2]) for d in range(4)], "OO%d LO%d" % (rd, rd), "OL%d" % rd)
 
@@ -522,8 +554,8 @@ def rank_program(g, core, T, topo):
                 sc((T.CW, T.KW)[w], (T.VC, T.VK)[w], s, ("CW", "KW")[w])
         if rd == 2:
             dma("sp", [(T.ycells[:], T.CW[:, 0:2048])], "CW", "yc")
-            dma("act", [(T.ykids[4 * e:4 * e + 4, :], T.KW[16 * e:16 * e + 4, 0:2048]) for e in range(4)], "KW", "yk")
-            dma("sp", [(T.ykids[4 * e:4 * e + 4, :], T.KW[16 * e:16 * e + 4, 0:2048]) for e in range(4, 8)], "KW", "yl")
+            dma("act", [(T.ykids[t::4, :], T.KW[t::16, 0:2048]) for t in range(2)], "KW", "yk")
+            dma("sp", [(T.ykids[t::4, :], T.KW[t::16, 0:2048]) for t in range(2, 4)], "KW", "yl")
 
     def ynodes():
         mm([(P[0][:, 64 * d:64 * d + 64], T.PF[:, 1 - kh:33 - kh],
@@ -556,12 +588,14 @@ def rank_program(g, core, T, topo):
         hash2()
 
     consts2()
-    either(T.RB16[:], T.RW[:], "RW", "RB16")
+    op("x", (ts(T.RB16[:], T.RW[:], -1.0, A.mult), act(T.RB16[:], T.RW[:], F.Copy, scale=-1.0)), "RW", "RB16")
     consts3()
     part_a()
     for rd in range(3):
         lookup()
         dmm()
+        if rd:
+            own1(rd - 1)
         choose()
         newlist(rd, 0)
         newlist(rd, 1)
@@ -580,8 +614,8 @@ def rank_program(g, core, T, topo):
     send([(d, T.YL[:, me, :], T.YN[:, d >> 1, :], "ay") for d in peers], 4, "YN0 YN1")
     arrives("ay", 12, "YL")
     ynodes()
+    own1(2)
     for rd in range(3):
-        own1(rd)
         own2(rd)
 
     for n in ORDER or range(1, len(prog) + 1):

from concourse.bass import DstId, RemoteDMATransfer
from concourse.mybir import AluOpType as A, ActivationFunctionType as F

f32, b16, i32, u16 = "float32", "bfloat16", "int32", "uint16"
SCRATCH = {}


def _decl(dt, **kw):
    for n, sh in kw.items():
        SCRATCH[n] = ("sbuf", [128] + list(sh), dt)


_decl(b16, XS=[4, 512], X=[2048], H=[4, 512], C0=[4, 128], SH=[8, 4, 4], SX=[8, 4, 4], WH=[4, 128], WX=[4, 128],
      G=[8192], TT=[8192], TO=[4096], L=[8320], LS=[4, 512], CW=[2080], KH=[512], KLO=[512],
      WZ=[13, 4, 4], WY=[13, 16], WT=[4], WC=[16], MK=[8], SM=[2], DM=[8, 16], R0=[2, 2, 2, 16], WF=[2], WD=[32], WK=[32], WE=[64], WJ=[64],
      WQ=[2, 136], RP=[256], B2=[144], TE=[192], IDB=[128], ONE=[128], TRI=[384], BW=[2, 128], BT=[2, 2, 128], WP1=[8, 16], WLX=[128],
      WKD=[8, 128], RB16=[4, 128], WA=[4, 14, 16], WB=[4, 14, 16], WO=[4, 14, 16],
      C=[8, 2, 64], Y=[1024], R=[2048], EQ=[512], TQ=[128], SEL=[128], SC=[6, 64], MO=[256], FO=[4, 64], CK=[384], MF=[128], SG=[512],
      YG=[3, 128], LR=[512], VC=[3, 128], LB=[3, 4, 32], UH=[128])
_decl(f32, RT=[8, 4, 4], CT=[8, 4, 4], FF=[40], J16=[20], GB=[16], KB=[4, 4, 2, 16], KT=[4, 4, 32], NF=[256], MI=[128],
      KF=[512], KW=[2080], IDF=[128], PM=[2, 17, 8], PF=[33, 4], RW=[4, 128], BO=[128], WG=[4], JT=[32], RM=[128],
      RB=[256], T3=[18], TP=[3, 32], NM=[128], HP=[128], PR=[2, 2, 4, 32], PZ=[130], UT=[320], CNT=[8], CF=[8], VN=[128],
      DG=[384], DS=[128], AB=[256], M3=[48], VK=[3, 128], YN=[2, 128], YL=[4, 128], YF=[256])
_decl(i32, PI=[1], FI=[20], KA=[4, 2, 64], NS=[4, 64], NI=[256], KN=[512], WI=[4], HI=[2, 2, 16], HJ=[2, 64])
_decl(u16, KL=[512], TL=[512], PL=[256], LL=[128], CL=[8], NL=[8], LF=[32], OO=[3, 4, 8], LO=[3, 4, 4, 8], OL=[3, 8])
SCRATCH["S"] = ("dram", [4, 128, 512], b16)
for _b in range(8):
    SCRATCH["P%d" % _b] = ("psum", [128, 512], f32)
SEMAPHORES = (["pe", "dve", "act", "pool", "ax0", "ax1", "ax2", "ax3", "ak", "an", "al0", "al1", "al2", "al3",
               "ao0", "ao1", "ao2", "ar0", "ar1", "ar2", "ay"] + ["d%d" % i for i in range(52)])

ORDER = [1,2,10,11,21,12,3,7,18,16,8,14,9,4,13,22,15,-19,17,38,28,32,47,29,-50,65,140,30,51,6,24,31,20,-36,141,52,-86,42,46,43,53,149,5,54,151,55,33,23,64,155,48,142,62,49,143,25,83,60,187,82,-44,56,63,153,-61,34,26,58,70,-57,188,93,41,84,138,-59,85,89,139,66,-94,76,91,35,67,81,90,102,27,-39,72,107,-103,78,98,100,-92,74,148,96,156,-108,37,77,40,75,79,101,104,144,-97,99,111,69,-105,109,68,137,-186,113,-110,87,145,115,114,-112,80,121,88,-116,106,146,95,117,174,165,-122,147,158,-161,119,129,178,123,166,179,169,-164,150,159,130,134,170,152,163,154,-118,-167,125,162,184,-168,124,126,171,131,120,-216,215,127,213,-214,223,224,132,218,-217,227,229,221,128,220,-219,222,228,231,172,232,175,185,233,133,176,234,173,-193,230,238,225,177,226,-45,235,236,-194,157,237,-191,71,-192,241,180,239,195,200,250,181,-240,251,-196,245,252,190,246,242,73,-253,182,247,243,201,248,-244,160,135,249,254,259,189,-255,256,260,263,266,267,268,257,-258,269,183,-202,261,197,262,264,270,-198,205,265,203,291,-271,272,-199,274,273,276,206,136,275,282,207,277,283,278,279,208,285,280,209,284,-326,281,286,288,327,-330,210,287,211,290,334,289,331,335,298,212,204,-333,292,293,294,295,344,-329,296,297,328,300,-332,299,301,345,304,336,-303,305,302,-307,337,310,308,-306,346,309,312,314,347,-313,348,338,315,351,339,316,349,322,350,311,-383,340,317,352,323,341,-353,342,358,343,318,359,363,324,364,365,360,354,-366,325,355,356,319,-362,361,-357,372,320,384,367,385,371,-369,373,376,386,387,368,-370,379,380,388,413,321,575,374,375,377,392,378,389,394,393,381,396,-390,395,382,-391,398,397,404,399,405,400,401,407,402,406,448,-450,403,-451,449,409,410,411,408,458,412,456,452,-453,457,460,420,459,414,-455,461,415,416,466,467,419,417,-454,418,470,421,423,422,426,425,-429,424,427,468,432,430,469,-428,431,434,576,577,471,-435,436,472,473,437,578,474,438,462,444,-475,433,463,-505,476,480,439,477,481,478,445,464,-479,465,482,485,446,-484,486,-494,487,440,447,483,-488,535,495,506,489,441,507,-492,493,442,508,509,510,490,-491,501,511,503,579,-512,496,513,580,581,443,497,498,514,499,504,-515,516,500,517,502,518,519,520,521,522,523,526,524,-525,582,583,584,531,532,533,585,586,587,527,534,528,536,-537,-529,538,542,539,530,540,541,561,588,589,543,545,590,544,-547,548,551,554,546,-549,552,553,591,592,-550,556,562,557,563,558,555,-566,559,571,564,572,567,565,574,568,569,570,560,-573,593,595,594,597,596,598,600,599,602,601,603,604]


def rank_program(g, core, T, topo):
    me = T.rank_of(core)
    if me is None:
        return
    Q = {"pe": g.tensor, "dve": g.vector, "act": g.scalar, "pool": g, "sp": g.sync}
    V, P = g.vector, [T["P%d" % b] for b in range(8)]
    cnt = {"pe": 0, "dve": 0, "act": 0, "pool": 0}
    seen = {q: {} for q in Q}
    wrote, read, total, nsem = {}, {}, {}, [0]
    peers = [me ^ 1, me ^ 2, me ^ 3]

    def need(q, r, w):
        m = {}
        for k in list(r) + list(w):
            for s, v in wrote.get(k, []) + (read.get(k, []) if k in w else []):
                m[s] = max(m.get(s, 0), v)
        for s, v in m.items():
            if seen[q].get(s, 0) < v and not (q == "pe" and s == "pe"):
                Q[q].wait_ge(T.sem[s], v)
                seen[q][s] = v

    def done(s, v, r, w):
        total[s] = v
        for k in r:
            read.setdefault(k, []).append((s, v))
        for k in w:
            wrote[k] = [(s, v)]
            read[k] = []

    prog = []

    def op(q, fns, r, w):
        prog.append(("op", q, fns, r.split(), w.split()))

    def dma(q, pairs, r, w):
        prog.append(("dma", q, pairs, r.split(), w.split()))

    def send(items, n, r):
        prog.append(("send", "pool", (items, n), r.split(), []))

    def arrives(s, v, w):
        prog.append(("arr", "ext", (s, v), [], w.split()))

    def either(o, i, r, w):
        op("x", (cp(o, i), act(o, i)), r, w)

    def do_op(q, fns, r, w):
        need(q, r, w)
        for f in (fns if isinstance(fns, list) else [fns]):
            f().then_inc(T.sem[q], 1)
            cnt[q] += 1
        done(q, cnt[q], r, w)

    def newsem():
        nsem[0] += 1
        return "d%d" % (nsem[0] - 1)

    def do_dma(q, pairs, r, w):
        need(q, r, w)
        s = newsem()
        for o, i in pairs:
            Q[q].dma_start(o, i).then_inc(T.sem[s], 16)
        done(s, 16 * len(pairs), r, w)

    def emask(d, lo, n):
        m = 0
        for e in topo.engines(core, T.cores[d])[lo:lo + n]:
            m |= 1 << e
        return m

    def do_send(items, n, r):
        need("pool", r, [])
        s = newsem()
        if len(items) == 1:
            d, o, i, rs = items[0]
            rid, pid = topo.addr(T.cores[d])[:2]
            g.remote_dma(o, i, T.sem[rs], T.sem[s], pid, rid, emask(d, 0, n))
        else:
            tr = []
            for j, (d, o, i, rs) in enumerate(items):
                rid, pid = topo.addr(T.cores[d])[:2]
                tr.append(RemoteDMATransfer(dst_ids=[DstId(rid=rid, pnc=pid)], dma_engine_mask=emask(d, j * n, n),
                                            remote_sem=T.sem[rs], srcs=[i], dsts=[o]))
            g.remote_dma_fused(tr, local_sem=T.sem[s])
        done(s, n * len(items), r, [])

    def mm(ms, r, w):
        op("pe", [(lambda m=m: g.tensor.matmul(*m)) for m in ms], r, w)

    def ts(o, i, s1, o0, s2=None, o1=None):
        if o1 is None:
            return lambda: V.tensor_scalar(o, i, s1, None, o0)
        return lambda: V.tensor_scalar(o, i, s1, s2, o0, o1)

    def tt(o, a, b, p):
        return lambda: V.tensor_tensor(o, a, b, p)

    def cp(o, i):
        return lambda: V.tensor_copy(o, i)

    def ms(o, c):
        return lambda: V.memset(o, c)

    def scan(o, a, b, p0, p1):
        return lambda: V.tensor_tensor_scan(o, a, b, 0.0, p0, p1)

    def act(o, i, f=F.Identity, **k):
        return lambda: g.scalar.activation(o, i, f, **k)

    def io(o, pat, base, cm=0):
        return lambda: g.iota(o, pat, base, cm, allow_small_or_imprecise_dtypes=True)

    def puts(key, items):
        op("pool", [(lambda o=o, pat=pat, base=base, val=val: g.affine_select(o, o, pat, A.not_equal, float(val), base, 1))
                    for o, pat, base, val in items], "", key)

    def put(key, o, pat, base, val, cm=1):
        op("pool", lambda: g.affine_select(o, o, pat, A.not_equal, float(val), base, cm), "", key)

    def keep(key, o, pat, base, cm):
        op("pool", lambda: g.affine_select(o, o, pat, A.is_ge, 0.0, base, cm), "", key)

    SHR, AND = A.arith_shift_right, A.bitwise_and
    FF, IDB = T.FF, T.IDB[:]

    def col(j):
        return FF[:, j:j + 1]

    def xload(dst, d):
        return [(dst(h), T.cells[32 * d:32 * d + 32, 1024 * h:1024 * h + 1024]) for h in range(2)]
    for d in peers:
        for h, q in enumerate(("sp", "act")):
            dma(q, xload(lambda h: T.XS[64 * h:64 * h + 64, d, :], d)[h:h + 1], "", "XS%d%s" % (d, "ab"[h]))
    dma("act", xload(lambda h: T.X[64 * h:64 * h + 64, 512 * me:512 * me + 512], me), "", "X%d" % me)
    dma("sp", [(T.KA[:, e // 2, e % 2, :], T.kids[4 * e:4 * e + 4, :]) for e in range(8)], "", "KA")
    dma("act", [(T.KN[:], T.kids[:])], "", "KN")

    op("pool", lambda: g.iota(T.PI[:], [[0, 1]], 0, 1), "", "PI")
    op("dve", [ms(T.BO[:], 1.0), ms(T.SH[:], 0.0)], "", "SH BO")
    op("dve", scan(T.MI[:], T.BO[:], T.BO[:], A.mult, A.add), "BO", "MI")
    fields = [(3, 3), (1, 16), (1, 3), (0, 65), (0, 15), (0, 12), (2, 9), (4, 1), (6, 1), (0, 1), (0, 29), (0, 32), (1, 1), (0, 3), (5, 3),
              (0, 63), (2, 1), (3, 15)]
    op("dve", [ts(T.FI[:, j:j + 1], T.PI[:], s, SHR, m, AND) for j, (s, m) in enumerate(fields[:6])], "PI", "FI")
    op("dve", [ts(T.FI[:, j + 6:j + 7], T.PI[:], s, SHR, m, AND) for j, (s, m) in enumerate(fields[6:])], "PI", "FJ")
    op("dve", [cp(FF[:, 6:17], T.FI[:, 6:17]), cp(col(36), T.FI[:, 17:18])], "FJ", "FE")
    op("x", ([ts(T.C0[:, a, :], T.MI[:], -1.0, A.add) for a in range(4)], [act(T.C0[:, a, :], T.MI[:], F.Copy, bias=-1.0) for a in range(4)]), "MI", "C0")
    op("dve", cp(FF[:, 0:6], T.FI[:, 0:6]), "FI", "FF")
    op("x", ([ts(T.RP[:, 0:128], T.MI[:], -41.0, A.add), ts(T.RP[:, 128:256], T.MI[:], 87.0, A.add)],
             [act(T.RP[:, 0:128], T.MI[:], F.Copy, bias=-41.0), act(T.RP[:, 128:256], T.MI[:], F.Copy, bias=87.0)]), "MI", "RP")
    for p in (32, 96):
        op("x", ([ms(T.C0[p:p + 32, a, :], float(a)) for a in range(4)],
                 [act(T.C0[p:p + 32, a, :], T.MI[p:p + 32, :], F.Copy, scale=0.0, bias=float(a)) for a in range(4)]), "MI", "C0")

    def hconst(slot):
        op("act", [act(T.H[64:128, slot, :], T.C0[64:128]), act(T.H[0:64, 2 + slot, :], T.C0[0:64])], "C0", "HC%d" % slot)
    op("pool", [io(T.RT[:, 2 * t:2 * t + 2], [[16, 2], [1, 4], [0, 4]], 3 * (t >> 1) - 1) for t in range(4)]
       + [io(T.CT[:, 4 * h:4 * h + 4], [[3, 2], [0, 8], [1, 4]], -1) for h in range(2)]
       + [io(T.J16[:, 16:20], [[64, 2], [1, 2]], 0), io(T.J16[:, 0:16], [[1, 16]], 0)], "", "RT CT J16")
    for d in peers:
        send([(d, T.X[:, 512 * me:512 * me + 512], T.XS[:, d, :], "ax%d" % me)], 16, "XS%da XS%db" % (d, d))
        arrives("ax%d" % d, 16, "X%d" % d)
    op("dve", [tt(col(20), col(0), col(1), A.add), ts(col(21), col(4), 3.0, A.is_equal, 4.0, A.mult),
               ts(col(22), col(5), 12.0, A.is_equal, -1.0, A.mult)], "FF", "FG")
    op("dve", [ts(col(17), col(7), 60.0, A.mult, col(2), A.add), ts(col(18), col(16), 30.0, A.mult, col(0), A.add)], "FF FE", "FA")
    op("dve", ts(col(19), col(17), col(18), A.add, col(20), A.add), "FA FG", "FB")
    op("dve", ts(T.SX[:], T.RP[:, 28:156], col(19), A.is_equal), "RP FB", "SX")
    op("dve", [ts(col(23), col(6), 8.0, A.is_equal, -129.0, A.mult),
               ts(col(26), col(11), 2.0, A.mult, col(10), A.add), ts(col(27), col(12), 15.0, A.mult, 1.0, A.add),
               ts(col(28), col(5), 2.0, A.mult, col(13), A.add), cp(col(29), T.PI[:])], "FF FE PI", "FD")
    dma("sp", [(T.NS[:, d, :], T.nodes[32 * d:32 * d + 32, :]) for d in peers], "", "NS")
    dma("sp", [(T.NI[:, 64 * me:64 * me + 64], T.nodes[32 * me:32 * me + 32, :]), (T.WI[0:32, 0:1], T.wt[32 * me:32 * me + 32, :])], "", "NIo WI")
    for n, k in (("PM", 136), ("DM", 128), ("R0", 128), ("WZ", 208), ("WY", 208), ("WP1", 128), ("WD", 32), ("WE", 64), ("WK", 32), ("WJ", 64), ("WQ", 136)):
        parts = [T[n][:, 0], T[n][:, 1]] if k == 136 else [T[n][:]]
        op("x", (ms(T[n][:], 0.0), [act(o, T.RP[:, 0:k], F.Copy, scale=0.0) for o in parts]), "RP", n)
    hconst(0)
    op("act", [act(T.RT[:], T.RT[:], F.Abs, bias=col(20), scale=-1.0), act(T.CT[:], T.CT[:], F.Abs, bias=col(2), scale=-1.0)],
       "FF FG", "RT CT")
    hconst(1)

    def hot(src, slot):
        c = slice(512 * src, 512 * src + 512)
        for h in range(2):
            o, i = T.H[64 * h:64 * h + 64, 2 * h + slot, :], T.X[64 * h:64 * h + 64, c]
            op("x", (ts(o, i, 15.0, A.is_equal), act(o, i, F.Relu, bias=-14.0)), "X%d" % src, "H%d%d" % (slot, h))

    hot(me, 0)
    op("dve", [ts(T.GB[:], T.J16[:, 0:16], col(21), A.mult, col(22), A.add), ts(T.J16[:, 16:20], T.J16[:, 16:20], col(3), A.is_equal),
               tt(T.RT[:], T.RT[:], T.CT[:], A.max)], "FF FG CT", "J16 GB RT")
    op("dve", [ts(T.SH[:, :, 0:3, 0:3], T.RT[:, :, 0:3, 0:3], 1.0, A.is_equal),
               ts(T.SX[:, :, 0:3, 0:3], T.RT[:, :, 0:3, 0:3], 0.0, A.is_equal, 16.0, A.mult)], "RT", "SH SX")
    op("dve", [ts(T.WH[:, j, :], T.SH[:], T.J16[:, 16 + j:17 + j], A.mult) for j in range(4)], "SH J16", "WH")
    op("dve", [ts(T.WX[:, j, :], T.SX[:], T.J16[:, 16 + j:17 + j], A.mult) for j in range(4)], "SX J16", "WX")
    op("dve", [ms(T.WH[64 * (1 - h) + 32 * b:64 * (1 - h) + 32 * b + 1, 2 * h:2 * h + 2, 7 - 4 * b::16], 1.0) for h in range(2) for b in range(2)],
       "", "WH")

    def gbuild(i, src, j):
        ch, c, b = 4 * src + j, slice(512 * src, 512 * src + 512), (4 * i + j) % 8
        mm([(P[b][:], T.WX[:, j, :], T.X[:, c], True, False), (P[b][:], T.WH[:, j, :], T.H[:, (j & 2) + (i & 1), :], False, True)],
           "WH WX HC%d X%d H%d%d" % (i & 1, src, i & 1, j >> 1), "P%d" % b)
        o, bias = T.G[:, 512 * ch:512 * ch + 512], T.GB[:, ch:ch + 1]
        op("x", (ts(o, P[b][:], bias, A.add, 0.0, A.max), act(o, P[b][:], F.Relu, bias=bias)), "GB", "P%d G%d" % (b, ch))
    for j in range(4):
        gbuild(0, me, j)
    op("dve", cp(T.KF[:], T.KN[:]), "KN", "KF")
    op("dve", [ts(col(30), col(8), 2.0, A.mult, col(26), A.add), ts(col(31), col(7), 64.0, A.mult, col(28), A.add)]
       + [ts(col(32 + d), col(14), float(d), A.is_equal) for d in range(4)], "FE FD", "FH")
    op("dve", ts(T.KN[:], T.KN[:], 127, AND), "", "KN")
    op("act", act(T.KH[:], T.KF[:], F.Copy, scale=1.0 / 128, bias=128.50390625), "KF", "KH")
    op("dve", [ts(T.WLX[:], T.RP[:, 40:168], col(30), A.is_equal, col(27), A.mult)]
       + [ts(T.WKD[:, 2 * d + e], T.RP[:, 8 - 4 * e:136 - 4 * e], col(31), A.is_equal, col(32 + d), A.mult) for d in range(4) for e in range(2)],
       "RP FD FH", "WLX WKD")
    op("dve", cp(T.KLO[:], T.KN[:]), "KN", "KLO")
    op("dve", [cp(T.KB[:, :, :, s, :], T.KA[:, :, s, :]) for s in range(2)], "KA", "KB")
    op("dve", [ts(T.IDF[:], T.RP[:, 40:168], col(29), A.is_equal), ts(IDB, T.RP[:, 40:168], col(29), A.is_equal)], "RP FD", "IDF IDB")
    op("dve", lambda: V.transpose(T.KT[:], T.KB[:]), "KB", "KT")
    op("dve", [ts(T.TE[:, 64:192], T.RP[:, 40:168], col(29), A.is_equal), ts(T.TE[:, 0:64], T.RP[:, 40:104], col(15), A.is_gt)], "RP FE FD", "TE")
    op("dve", [cp(T.KL[:, b::4], T.KT[:, :, b, :]) for b in range(4)], "KT", "KL")
    op("dve", cp(T.TL[:, 128 * me:128 * me + 128], T.KL[:, 128 * me:128 * me + 128]), "KL", "TLo")
    send([(d, T.NI[:, 64 * me:64 * me + 64], T.NS[:, d, :], "an") for d in peers], 4, "NS")
    arrives("an", 12, "NI")
    puts("PM", [(T.PM[:, kh, 1::2, :], [[1, 4], [-64, 2], [-8, 8]], -3 - 4 * kh, 1) for kh in range(2)])
    send([(d, T.TL[:, 128 * me:128 * me + 128], T.KL[:, 128 * d:128 * d + 128], "ak") for d in peers], 4, "KL")
    arrives("ak", 12, "TL")
    quad = [(t, 1 - (t >> 1), 1 - (t & 1)) for t in range(4)]
    puts("DM", [(T.DM[:, 2 * t:2 * t + 2, 12:16], [[-16, 2], [-4, 2], [-1, 2]], -8 * tr - 2 * tc, 1) for t, tr, tc in quad])

    def lpack(d):
        b = d ^ me
        xs, k = (T.X[:, 512 * me:512 * me + 512], "X%d" % me) if d == me else (T.XS[:, d, :], "XS%da XS%db" % (d, d))
        mm([(P[b][:], T.WLX[:], xs, True, False), (P[b][:], T.WKD[:, 2 * d], T.KH[:], False, False),
            (P[b][:], T.WKD[:, 2 * d + 1], T.KLO[:], False, True)], "WLX WKD KH KLO " + k, "P%d" % b)
        op("x", (ts(T.LS[:, d, :], P[b][:], col(23), A.add), act(T.LS[:, d, :], P[b][:], bias=col(23))), "FD", "P%d LS%d" % (b, d))
    hot(peers[0], 1)
    hot(peers[1], 0)
    for n, parts in (("MK", [T.MK[:]]), ("BT", [T.BT[:, 0], T.BT[:, 1]])):
        op("x", (ms(T[n][:], 1.0), [act(o, T.RP[:, 0:8 if n == "MK" else 256], F.Copy, scale=0.0, bias=1.0) for o in parts]), "RP", n)
    op("dve", [ts(T.WI[0:32, 1:2], T.WI[0:32, 0:1], 6, SHR), ts(T.WI[0:32, 2:3], T.WI[0:32, 0:1], 63, AND),
               cp(T.SM[:, 1:2], col(7)), ts(T.SM[:, 0:1], col(7), 0.0, A.is_equal)], "WI FE", "WI2 SM")
    for i in range(1, 4):
        for j in range(4):
            if (i, j) == (1, 3):
                op("dve", [ts(T.WF[0:32, 0:1], T.WI[0:32, 1:2], 64.0, A.mult), cp(T.WF[0:32, 1:2], T.WI[0:32, 2:3])], "WI2", "WF")
            if (i, j) == (2, 0):
                hot(peers[2], 1)
            if (i, j) == (2, 3):
                op("dve", cp(T.NF[:], T.NI[:]), "NI NIo", "NF")
            gbuild(i, peers[i - 1], j)
    for d in peers + [me]:
        lpack(d)
    for d in peers:
        send([(d, T.S[me], T.LS[:, d, :], "al%d" % me)], 16, "LS%d" % d)
        arrives("al%d" % d, 16, "S%d" % d)
    for d in [me] + peers:
        dma("sp", [(T.L[32 * r:32 * r + 32, 2048 * d:2048 * d + 2048], T.LS[:, d, :] if d == me else T.S[d]) for r in range(4)],
            "LS%d" % d if d == me else "S%d" % d, "L%d" % d + (" KL" if d == me else ""))
    dma("sp", [(T.KW[16 * e:16 * e + 4, 0:2048], T.KF[16 * e:16 * e + 16, :]) for e in range(8)], "KF L0 L1 L2 L3", "KW")
    dma("sp", [(T.CW[:, 0:2048], T.cells[:])], "L0 L1 L2 L3", "CW")
    GALL = " ".join("G%d" % c for c in range(16))
    LALL = "L0 L1 L2 L3 L"

    puts("R0", [(T.R0[:, sh], [[-16, 2], [0, 2], [-1, 16]], 0, 1) for sh in range(2)])
    keep("MK", T.MK[:], [[-32, 2], [-64, 2], [-16, 2]], 0, 1)
    keep("MK", T.MK[:], [[32, 2], [64, 2], [16, 2]], 15, -1)
    for t, tr, tc in quad:
        put("WZ", T.WZ[:, 5:8:2, tr:tr + 3, tc:tc + 3], [[-16, 2], [-4, 3], [-1, 3]], -32 * t, 1)
    for mc in range(2):
        puts("WY", [(T.WY[:, 5:8:2, 4 * tr + tc:4 * tr + tc + 3:2], [[-16, 2], [-2, 2]], -32 * t - 12 - mc, 16 ** mc) for t, tr, tc in quad]
             + [(T.WY[:, 5:8:2, 8 + mc::2], [[-16, 2], [32, 4]], -99 - 4 * mc, 1)])
    put("WP1", T.WP1[:, :, 0:8], [[-16, 8], [-2, 8]], 0, 1)
    put("WP1", T.WP1[:, :, 0:8], [[-16, 8], [-2, 8]], -1, 16)
    for e in range(3):
        n = 3 if e < 2 else 2
        put("WD", T.WD[:, 0:8 * n], [[-3, n], [-16, 8]], -e, 256 ** e)
        put("WE", T.WE[:, 0:16 * n], [[-3, n], [0, 2], [-16, 8]], -e, -256 ** e)
    put("WD", T.WD[:, 24:32], [[-16, 8]], 0, 1)
    for e in range(2):
        v = 128 if e == 0 else 1
        put("WK", T.WK[:], [[2, 4], [-16, 8]], -14 - e, v)
        put("WJ", T.WJ[:], [[2, 4], [0, 2], [-16, 8]], -14 - e, -v)
        puts("WQ", [(T.WQ[:, sh, 7:135:8], [[2, 4], [-32, 2], [-16, 2]], -64 * sh - 14 - e, v) for sh in range(2)])

    def gather(o, win, off, r, w):
        either(o, win.indirect(off), r, w)

    for a in range(0, 512, 64):
        gather(T.TT[:, 16 * a:16 * a + 1024], T.G[:, :], T.TL[:, a:a + 64], GALL + " TL TLo", "TT%d" % a)
    mm([(P[5][:, 64 * (2 * sh + kh):64 * (2 * sh + kh) + 64], T.PM[:, kh, 1 - sl:17 - sl], T.NF[:, 64 * (2 * sh + sl):64 * (2 * sh + sl) + 64],
         sl == 0, sl == 1) for sh in range(2) for kh in range(2) for sl in range(2)], "PM NF", "P5")
    mm([(P[4][:, 0:2], T.R0[0:32], T.WF[0:32, :], True, True), (P[4][:, 2:4], T.DM[0:32], T.WF[0:32, :], True, True)], "R0 DM WF", "P4")
    op("dve", cp(T.PL[:], P[5][:, 0:256]), "", "P5 PL0 PL1")
    op("dve", cp(T.WG[:], P[4][:, 0:4]), "", "P4 WG")
    op("dve", [ts(T.WC[:, 8 * f:8 * f + 8], T.MK[:], T.WG[:, f:f + 1], A.mult) for f in range(2)]
       + [ts(T.WT[:, 2 * f:2 * f + 2], T.SM[:], T.WG[:, 2 + f:3 + f], A.mult) for f in range(2)], "WG MK SM", "WC WT")
    TALL = " ".join("TT%d" % a for a in range(0, 512, 64))

    op("dve", ts(col(37), col(36), -1.0, A.mult, -129.0, A.add), "FE", "FL")
    op("act", act(T.BW[:], T.RP[:], F.Copy, scale=0.0625, bias=131.03125), "RP", "BW")
    op("act", act(T.BW[:], T.BW[:], F.Abs, bias=col(37)), "FL", "BW")
    op("act", act(T.BW[:], T.BW[:], F.Relu, scale=-1.0, bias=1.0), "", "BW")
    for kh in range(2):
        keep("BT", T.BT[:, :, kh, :], [[128, 2], [16, 8], [1, 16]], -kh, -2)
        put("BT", T.BT[:, :, kh, :], [[128, 2], [16, 8], [1, 16]], -kh, -127, -2)
        op("dve", tt(T.BT[:, :, kh, :], T.BT[:, :, kh, :], T.BW[:], A.mult), "BW", "BT")
    op("pool", [io(T.T3[:, 16:18], [[16, 2]], 0), io(T.JT[:], [[1, 32]], -127), io(T.DG[:, 256:384], [[0, 8], [1, 16]], 0),
                io(T.DG[:, 0:256], [[-16, 2], [0, 4], [1, 32]], 0), io(T.T3[:, 0:8], [[16, 8]], 8193), io(T.T3[:, 8:16], [[2048, 4], [16, 2]], 2049),
                io(T.TP[:, 0], [[0, 4], [16, 8]], 8192), io(T.TP[:, 1], [[0, 16], [16, 2]], 2048), io(T.TP[:, 2], [[0, 4], [2048, 4], [0, 2]], 0)],
       "", "K2 DG")
    op("x", (ms(T.RW[:], 0.0), act(T.RW[:], T.C0[:], F.Copy, scale=0.0)), "C0", "RW")
    op("x", (ms(T.B2[:], 0.0), act(T.B2[:], T.RP[:, 0:144], F.Copy, scale=0.0)), "RP", "B2")
    keep("BO", T.BO[:], [[-16, 8], [0, 16]], 0, 1)
    keep("BO", T.BO[:], [[16, 8], [0, 16]], 15, -1)
    puts("RW", [(T.RW[:, src, :], [[0, 4], [-32, 2], [-1, 16]], -64 * (src >> 1) - 16 * (src & 1), -1) for src in range(4)])

    def consts2():
        c4 = col(4)
        op("dve", [ts(col(24), col(9), -2193.0, A.mult, 2064.0, A.add), ts(col(25), c4, 64.0, A.mult)], "FF FE", "FK")
        for n, k, v in (("RM", 128, 1.0), ("ONE", 128, 1.0), ("RB", 256, 0.0), ("PZ", 130, 0.0)):
            op("x", (ms(T[n][:], v), act(T[n][:], T.RP[:, 0:k], F.Copy, scale=0.0, bias=v)), "RP", n)
        op("dve", ts(T.T3[:, 16:18], T.T3[:, 16:18], c4, A.add, 0.5, A.add), "FF", "K2")
        op("x", ([ts(T.T3[:, 0:16], T.T3[:, 0:16], c4, A.add), ts(T.TP[:, 0:2], T.TP[:, 0:2], c4, A.add)],
                 [act(T.T3[:, 0:16], T.T3[:, 0:16], bias=c4), act(T.TP[:, 0:2], T.TP[:, 0:2], bias=c4)]), "FF", "K2")
        op("dve", [ms(T.RM[:, 0::16], 0.0), ms(T.RB[:, 0::32], 2.0 ** 29), ts(T.TRI[:, 256:384], T.DG[:, 256:384], c4, A.not_equal, -2.0 ** 28, A.mult),
                   ts(T.TRI[:, 0:256], T.DG[:, 0:256], c4, A.is_ge, 2.0 ** 28, A.mult), ts(T.B2[:, 15:143:16], T.BO[:, 0::16], col(25), A.mult)],
           "FF FK DG BO", "RM RB K2 B2")
        op("x", (ts(T.BO[:], T.BO[:], 16384.0, A.mult), act(T.BO[:], T.BO[:], F.Copy, scale=16384.0)), "", "BO")

    def consts3():
        for n in ("WA", "WB", "WO"):
            op("x", (ms(T[n][:], 0.0), act(T[n][:], T.G[:, 0:896], F.Copy, scale=0.0)), GALL, n)
        op("x", (ms(T.PF[:], 0.0), act(T.PF[:], T.RP[:, 0:132], F.Copy, scale=0.0)), "RP", "PF")
        put("PF", T.PF[:, 1::2, :], [[-16, 2], [-1, 8], [32, 4]], -96 - 8 * (me & 1), 1)
        for src in range(4):
            b = -64 * (src >> 1) - 16 * (src & 1)
            puts("WA WB WO", [(T.WA[:, src, 6:8, 0::2], [[-32, 2], [-1, 8]], b, 1), (T.WB[:, src, 6:8, 0::2], [[-32, 2], [-1, 8]], b, -16),
                              (T.WB[:, src, 6:8, 1::2], [[-32, 2], [-1, 8]], b, 1), (T.WO[:, src, 6:8, 0:4], [[-32, 2], [-2, 4]], b - 8, 128)])
            put("WO", T.WO[:, src, 6:8, 0:4], [[-32, 2], [-2, 4]], b - 9, 1)

    TO = T.TO
    OW, AN, KBX, A1, HS = (T.SC[:, j, :] for j in range(5))

    def tgather(sh, kh, a):
        c = 128 * sh + 64 * kh + 32 * a
        gather(TO[:, 16 * c:16 * c + 512], T.TT[:, :], T.PL[:, c:c + 32], TALL + " PL%d" % sh, "TO%d%d%d" % (sh, kh, a))

    def tok(sh, kh):
        return " TO%d%d0 TO%d%d1" % (sh, kh, sh, kh)

    def win(W, sh, sl):
        return W[:, 5 - 4 * sh - sl:13 - 4 * sh - sl]

    def zmm(sh, kh):
        c = 2048 * sh + 1024 * kh
        for sl in range(2):
            mm([(P[kh][:, 64 * kl:64 * kl + 64], win(T.WZ, sh, sl), TO[:, c + 8 * sl + kl:c + 1024:16], sh + sl + kl == 0, sh + sl + kl == 9)
                for kl in range(8)], "WZ" + tok(sh, kh), "P%d" % kh)

    def cond(kh):
        op("dve", ts(T.C[:, :, kh, :], P[kh][:], 2.0, A.is_equal, 15.0, A.mult), "", "P%d C%d" % (kh, kh))

    def tpart(sh):
        for a in (0, 8):
            mm([(P[4][:, 16 * sh + i:128:32], TO[:, 2048 * sh + i:2048 * sh + 2048:16], T.WT[:], sh + i == 0, False) for i in range(a, a + 8)],
               "WT" + tok(sh, 0) + tok(sh, 1), "P4")

    def cmm():
        mm([(P[4][:, kl:128:8], T.C[:, kl], T.WC[:], False, kl == 7) for kl in range(8)], "WC C0 C1", "P4")
        either(T.NM[:], P[4][:, 0:128], "", "P4 NM")

    def ymm(sh, b):
        for sl in range(2):
            mm([(P[2 + b][:, 128 * u:128 * u + 128], win(T.WY, sh, sl), TO[:, 2048 * sh + 8 * sl + 4 * b + u:2048 * sh + 2048:16],
                 sh + sl + u == 0, False) for u in range(4)], "WY" + tok(sh, 0) + tok(sh, 1), "P%d" % (2 + b))

    def ycm(b):
        mm([(P[2 + b][:], T.WP1[:], T.C[:, 4 * b:4 * b + 4], False, True)], "WP1 C0 C1", "P%d" % (2 + b))
        either(T.Y[:, 512 * b:512 * b + 512], P[2 + b][:], "", "P%d Y%d" % (2 + b, b))

    def hash1():
        op("dve", [tt(T.HI[:, :, s, :], T.NM[:, 32 * s:32 * s + 32], T.NM[:, 64 + 32 * s:96 + 32 * s], A.add) for s in range(2)], "NM", "HI")
        op("dve", [ts(T.HJ[:, 0, :], T.HI[:], 8190, AND), ts(T.HJ[:, 1, :], T.HI[:], 1, AND)], "HI", "HJ")
        op("dve", [tt(T.HP[:, 0:64], T.HJ[:, 0, :], T.HJ[:, 1, :], A.add), tt(T.HP[:, 64:128], T.HJ[:, 0, :], T.HJ[:, 1, :], A.subtract)], "HJ", "HP")
        mm([(P[4][:, 128:256], T.HP[:], T.IDF[:], True, True)], "HP IDF", "P4")
        op("x", (ts(OW, T.HP[:, 0:64], 2.0 ** -11, A.mult, 128.500244140625, A.add),
                 act(OW, T.HP[:, 0:64], F.Copy, scale=2.0 ** -11, bias=128.500244140625)), "HP", "OW")

    def hash2():
        op("dve", ts(T.LL[:], P[4][:, 128:256], col(8), A.add), "FE", "P4 LL")

    def lookup():
        for j in range(4):
            gather(T.R[:, 512 * j:512 * j + 512], T.L[:, 0:8192], T.LL[:, 32 * j:32 * j + 32], LALL + " LL", "R%d" % j)
        op("x", (ts(OW, OW, 0.125, A.mult, -16.0, A.add), act(OW, OW, F.Copy, scale=0.125, bias=-16.0)), "", "OW")

    def dmm():
        for b, Wy, Wr, k in ((0, T.WE, T.WD, "WE WD"), (1, T.WJ, T.WK, "WJ WK")):
            mm([(P[b][:, kl::8], T.Y[:, 128 * kl:128 * kl + 128], Wy[:], kl == 0, False) for kl in range(4)], k + " Y0", "P%d" % b)
            mm([(P[b][:, i::16], T.R[:, i::16], Wr[:], False, False) for i in range(16)], k + " R0 R1 R2 R3", "P%d" % b)
            mm([(P[b][:, kl::8], T.Y[:, 128 * kl:128 * kl + 128], Wy[:], False, kl == 7) for kl in range(4, 8)], k + " Y1", "P%d" % b)
        for sh in range(2):
            for b in range(2):
                mm([(P[2 + sh][:, 0:128], T.WQ[:, sh, 7 - kl:135 - kl], T.Y[:, 128 * kl:128 * kl + 128], kl == 0, False) for kl in range(4 * b, 4 * b + 4)],
                   "WQ Y%d" % b, "P%d" % (2 + sh))

    def choose():
        EQ, S0, E0 = T.EQ, T.SEL[:, 0:64], T.EQ[:, 384:448]
        op("dve", ts(EQ[:, 0:384], P[0][:, 0:384], 0.0, A.is_equal), "", "P0 EQ")
        op("x", (ts(EQ[:, 384:512], P[0][:, 384:512], 0.0, A.is_lt), act(EQ[:, 384:512], P[0][:, 384:512], F.Relu, scale=-1.0 / 17)), "", "P0 EM")
        op("dve", tt(T.TQ[:], EQ[:, 0:128], EQ[:, 128:256], A.mult), "EQ", "TQ")
        op("dve", [tt(AN, E0, EQ[:, 448:512], A.max), tt(KBX, T.HJ[:, 1, :], E0, A.is_equal)], "EM HJ", "AN KBX")
        op("dve", [tt(S0, T.TQ[:, 0:64], EQ[:, 256:320], A.mult), tt(A1, T.TQ[:, 64:128], EQ[:, 320:384], A.mult)], "TQ EQ", "S0 A1")
        op("dve", tt(AN, AN, OW, A.mult), "OW", "AN")
        op("dve", [tt(T.SEL[:, 64:128], A1, S0, A.is_gt), tt(HS, A1, S0, A.max)], "S0 A1", "S1 HS")
        op("dve", [ts(T.FO[:, o, :], AN, -0.125 * (o + 1), A.add) for o in range(4)], "AN", "FO")
        op("dve", tt(T.PZ[:, 1:129:2], T.HJ[:, 0, :], KBX, A.add), "HJ KBX", "PZ")
        op("dve", [tt(T.MO[:, 64 * o:64 * o + 64], T.FO[:, o, :], HS, A.is_equal) for o in range(4)], "FO HS", "MO")
        mm([(P[4][:, 192 * h:192 * h + 192], T.MO[:, 128 * h:128 * h + 128], T.TE[:], True, True) for h in range(2)], "MO TE", "P4")
        either(T.CK[:], P[4][:, 0:384], "", "P4 CK")
        op("dve", [tt(T.PR[:, :, :, t, :], P[1][:, 128 * t:128 * t + 128], T.SEL[:], A.mult) for t in range(4)], "S0 S1", "P1 PR")
        for sh in range(2):
            mm([(P[2 + sh][:, 0:128], T.PR[:, w, sh], T.IDF[:], False, w == 1) for w in range(2)], "PR IDF", "P%d" % (2 + sh))

    def newlist(rd, sh):
        if rd == 2:
            either(T.YN[:, sh, :], P[2 + sh][:, 0:128], "", "P%d YN%d" % (2 + sh, sh))
        else:
            op("dve", cp(T.PL[:, 128 * sh:128 * sh + 128], P[2 + sh][:, 0:128]), "", "P%d PL%d" % (2 + sh, sh))

    def claim2():
        mm([(P[6][:, 64 * o:64 * o + 64], T.BW[:, o & 1], T.CK[:, 192 * (o >> 1):192 * (o >> 1) + 64], True, True) for o in range(4)], "BW CK", "P6")
        mm([(P[5][:, 64 * o:64 * o + 64], T.BW[:, o & 1] if j == 0 else T.BT[:, o & 1, j - 1],
             T.CK[:, 192 * (o >> 1) + 64 * j:192 * (o >> 1) + 64 * j + 64], j == 0, j == 2) for o in range(4) for j in range(3)]
           + [(P[5][:, 256:320], T.PZ[:, 1 - kh:129 - kh], T.IDF[:, 64 * kh:64 * kh + 64], kh == 0, False) for kh in range(2)]
           + [(P[5][:, 256:320], T.ONE[:], T.IDB[:, 0:64], False, True)], "BW BT CK PZ IDF IDB ONE", "P5")
        op("act", [act(T.SG[:, 64 * j:64 * j + 64], P[6][:, 64 * (j >> 1):64 * (j >> 1) + 64], F.Sign, bias=T.T3[:, 16 + (j & 1):17 + (j & 1)],
                       scale=-1.0, accum_out=T.CNT[:, j:j + 1]) for j in range(8)], "K2", "P6 SG CNT")
        either(T.UT[:], P[5][:, 0:320], "", "P5 UT")
        mm([(P[7][:, 0:256], IDB, T.TRI[:, 0:256], True, False)], "IDB K2", "P7")

    def claim3():
        op("dve", ts(T.CL[:], T.CNT[:], 0.5, A.mult, 31.0, A.add), "CNT", "CL")
        op("x", (ts(T.CF[:], T.CNT[:], 0.5, A.mult, 31.0, A.add), act(T.CF[:], T.CNT[:], F.Copy, scale=0.5, bias=31.0)), "CNT", "CF")
        op("dve", [tt(T.MF[:, 32 * o:32 * o + 32], T.UT[:, 64 * o:64 * o + 64].indirect(T.CL[:, 2 * o:2 * o + 2]), T.JT[:], A.is_equal)
                   for o in range(4)], "UT CL K2", "MF")
        mm([(P[6][:, 0:8], T.IDF[:], T.CF[:], True, False)], "IDF CF", "P6")
        mm([(P[6][:, 0:8], T.B2[:, 15 - i:143 - i], T.MF[:, i::16], False, i == 15) for i in range(16)], "B2 MF", "P6")
        op("dve", tt(T.VN[:], T.UT[:, 256:320].indirect(T.CL[:, :]), T.MF[:], A.mult), "UT MF CL", "VN")
        mm([(P[5][:, 0:128], IDB, T.TRI[:, 256:384], True, False)], "IDB K2", "P5")
        mm([(P[5][:, 0:128], T.BO[:], T.VN[:], False, True)], "BO VN", "P5")
        mm([(P[7][:, 128 * h:128 * h + 128], T.BO[:], T.VN[:], False, h == 1) for h in range(2)], "BO VN", "P7")

    def claim4(rd):
        op("dve", cp(T.NL[:], P[6][:, 0:8]), "", "P6 NL")
        mm([(P[6][:, 0:32], T.IDF[:], T.TP[:, 1 if rd == 2 else 0], True, False)], "IDF K2", "P6")
        gather(T.YG[:, rd, :], T.Y[:, :], T.NL[:, :], "NL Y0 Y1", "YG%d" % rd)
        op("dve", scan(T.DS[:], T.RM[:], P[5][:, 0:128], A.mult, A.max), "RM", "P5 DS")
        for h in range(2):
            z = [(T.AB[:, 32 * j:32 * j + 31], P[7][:, 128 * (j & 1) + 32 * (j >> 1):128 * (j & 1) + 32 * (j >> 1) + 31],
                  T.DS[:, 16 * j + 15:16 * j + 16]) for j in range(4 * h, 4 * h + 4)]
            op("x", ([ts(o, i, k, A.not_equal, 16384.0, A.mult) for o, i, k in z], [act(o, i, F.Abs, bias=k, scale=-1.0) for o, i, k in z]),
               "DS", "P7 AB%d" % h)
        key, M3 = T.DS[:, 15:128:16], T.M3
        op("x", (ts(M3[:, 16:24], key, 2.0 ** -14, A.mult), act(M3[:, 16:24], key, F.Copy, scale=2.0 ** -14)), "DS", "D2")
        j = 8 if rd == 2 else 0
        op("dve", tt(M3[:, 0:8], T.T3[:, j:j + 8], M3[:, 16:24], A.subtract), "D2 K2", "D3")
        op("dve", tt(T.AB[:, 31::32], M3[:, 0:8], key, A.min), "D3 DS", "AB2")

    def lrec(rd):
        mm([(P[5][:, 128 * s:128 * s + 128], T.RB16[:, s, :], T.YG[:, rd, :], True, True) for s in range(4)], "RB16 YG%d" % rd, "P5")
        either(T.LR[:], P[5][:], "", "P5 LR")

    def claim5(rd):
        op("dve", scan(T.DG[:, 0:256], T.RB[:], T.AB[:], A.add, A.min), "RB AB0 AB1 AB2", "DG")
        mm([(P[6][:, 8 * s:8 * s + 8], T.RW[:, s, :], T.DG[:, 31:256:32], False, s == 3) for s in range(4)], "RW DG", "P6")
        if rd == 2:
            op("dve", cp(T.OO[:, rd, :, 0:8], P[6][:, 0:32]), "", "P6 OO%d" % rd)
            return
        op("dve", cp(T.LF[:], P[6][:, 0:32]), "", "P6 LF")
        op("dve", tt(T.M3[:, 16:48], P[6][:, 0:32], T.TP[:, 2], A.subtract), "K2", "P6 D2 D4")
        op("dve", tt(T.M3[:, 16:48], T.M3[:, 16:48], T.TP[:, 1], A.min), "K2", "D2 D4")
        op("dve", cp(T.OO[:, rd, :, 0:8], T.M3[:, 16:48]), "D2 D4", "OO%d" % rd)

    def lscatter(rd, src):
        op("dve", cp(T.L[:, :].indirect(T.LF[:, 8 * src:8 * src + 8]), T.LR[:, 128 * src:128 * src + 128]), "LF LR L0 L1 L2 L3", "L")

    def post_rec(rd):
        send([(d, T.LB[:, rd, me ^ d, :], T.YG[:, rd, 32 * d:32 * d + 32], "ar%d" % rd) for d in peers], 4, "YG%d" % rd)
        arrives("ar%d" % rd, 12, "LB%d" % rd)

    def post_off(rd):
        send([(d, T.LO[:, rd, me], T.OO[:, rd], "ao%d" % rd) for d in peers], 4, "OO%d" % rd)
        arrives("ao%d" % rd, 12, "LO%d" % rd)

    def own1(rd):
        own = T.YG[:, rd, 32 * me:32 * me + 32]
        z = ((T.UH[:, 0:32], own), (T.UH[:, 32:128], T.LB[:, rd, 1:4, :]))
        op("x", ([ts(o, i, 0.0625, A.mult, 128.53125, A.add) for o, i in z], [act(o, i, F.Copy, scale=0.0625, bias=128.53125) for o, i in z]),
           "YG%d LB%d" % (rd, rd), "UH")

        def rec(d):
            return own if d == me else T.LB[:, rd, me ^ d, :]
        a, b = (6, 6) if rd < 2 else (2, 3)
        for s in range(4):
            mm([(P[a][:, 32 * s:32 * s + 32], W[:, s, 6 - 2 * d:14 - 2 * d], rec(d) if j == 0 else T.UH[:, 32 * (me ^ d):32 * (me ^ d) + 32],
                 d + j == 0, d + j == 4) for j, W in enumerate((T.WA, T.WB)) for d in range(4)], "WA WB UH YG%d LB%d" % (rd, rd), "P%d" % a)
        for h in range(2):
            mm([(P[b][:, 128 + 32 * s:160 + 32 * s], T.WO[:, s, 6 - 2 * d:14 - 2 * d], rec(d), d == 0, d == 3) for s in (2 * h, 2 * h + 1) for d in range(4)],
               "WO YG%d LB%d" % (rd, rd), "P%d" % b)
        op("x", (ts(T.VC[:, rd, :], P[a][:, 0:128], col(24), A.add), act(T.VC[:, rd, :], P[a][:, 0:128], bias=col(24))), "FK", "P%d VC%d" % (a, rd))
        either(T.VK[:, rd, :], P[b][:, 128:256], "", "P%d VK%d" % (b, rd))

    def own2(rd):
        a = 2 * me
        op("dve", [cp(T.OL[32 * d:32 * d + 32, rd, :], T.OO[32 * d:32 * d + 32, rd, :, a:a + 2] if d == me
                      else T.LO[32 * d:32 * d + 32, rd, d, :, a:a + 2]) for d in range(4)], "OO%d LO%d" % (rd, rd), "OL%d" % rd)

        def sc(W, Vv, s, k):
            op("dve", cp(W[:, :].indirect(T.OL[:, rd, 2 * s:2 * s + 2]), Vv[:, rd, 32 * s:32 * s + 32]), "OL%d V%s%d" % (rd, k[0], rd), k)
        for s in (3, 2, 1, 0):
            for w in range(2):
                sc((T.CW, T.KW)[w], (T.VC, T.VK)[w], s, ("CW", "KW")[w])
        if rd == 2:
            dma("sp", [(T.ycells[:], T.CW[:, 0:2048])], "CW", "yc")
            dma("act", [(T.ykids[t::4, :], T.KW[t::16, 0:2048]) for t in range(2)], "KW", "yk")
            dma("sp", [(T.ykids[t::4, :], T.KW[t::16, 0:2048]) for t in range(2, 4)], "KW", "yl")

    def ynodes():
        mm([(P[0][:, 64 * d:64 * d + 64], T.PF[:, 1 - kh:33 - kh],
             T.YN[:, me >> 1, 64 * kh:64 * kh + 64] if d == me else T.YL[:, d, 64 * kh:64 * kh + 64], kh == 0, kh == 1)
            for d in range(4) for kh in range(2)], "PF YN0 YN1 YL", "P0")
        either(T.YF[:], P[0][:, 0:256], "", "P0 YF")
        dma("sp", [(T.ynodes[32 * d:32 * d + 32, :], T.YF[:, 64 * d:64 * d + 64]) for d in range(4)], "YF", "yn")

    def part_a():
        for sh in range(2):
            for kh in range(2):
                tgather(sh, kh, 0)
                tgather(sh, kh, 1)
        zmm(0, 0)
        zmm(0, 1)
        tpart(0)
        ymm(0, 0)
        ymm(0, 1)
        zmm(1, 0)
        zmm(1, 1)
        cond(0)
        tpart(1)
        cond(1)
        cmm()
        ymm(1, 0)
        ycm(0)
        hash1()
        ymm(1, 1)
        ycm(1)
        hash2()

    consts2()
    op("x", (ts(T.RB16[:], T.RW[:], -1.0, A.mult), act(T.RB16[:], T.RW[:], F.Copy, scale=-1.0)), "RW", "RB16")
    consts3()
    part_a()
    for rd in range(3):
        lookup()
        dmm()
        if rd:
            own1(rd - 1)
        choose()
        newlist(rd, 0)
        newlist(rd, 1)
        claim2()
        claim3()
        claim4(rd)
        post_rec(rd)
        if rd < 2:
            lrec(rd)
        claim5(rd)
        post_off(rd)
        if rd < 2:
            for src in (3, 2, 1, 0):
                lscatter(rd, src)
            part_a()
    send([(d, T.YL[:, me, :], T.YN[:, d >> 1, :], "ay") for d in peers], 4, "YN0 YN1")
    arrives("ay", 12, "YL")
    ynodes()
    own1(2)
    for rd in range(3):
        own2(rd)

    for n in ORDER or range(1, len(prog) + 1):
        rec = prog[abs(n) - 1]
        kind, q, pay, r, w = rec
        if kind == "op":
            if q == "x":
                q, pay = ("act", pay[1]) if n < 0 else ("dve", pay[0])
            do_op(q, pay, r, w)
        elif kind == "dma":
            do_dma(q, pay, r, w)
        elif kind == "send":
            do_send(pay[0], pay[1], r)
        else:
            done(pay[0], pay[1], [], w)
    for s, v in total.items():
        if seen["pool"].get(s, 0) < v:
            g.wait_ge(T.sem[s], v)
